import numpy as np, ml_dtypes
CORES = [23,119,17,113]
N = 4
BF = ml_dtypes.bfloat16
def gentries(a):
    return np.ascontiguousarray(a.reshape(8, 16, -1).transpose(0, 2, 1)).reshape(8, -1)
def gtable(e):
    e = np.asarray(e); return np.ascontiguousarray(e.reshape(8, -1, 16).transpose(0, 2, 1)).reshape(128, -1).astype(np.int32)
V, G, CAP, TH, Q, RO = 3584, 384, 96, 6, 9, 5
H = (N - 1) * G
W = V + H
def near(rng, b, m, C, L):
    k = (rng.random((N, 8, m)) * C).astype(np.int64)
    f = np.take_along_axis(np.broadcast_to(b, (N, 8, 15, 4)), k[:, :, None, :], 3) + rng.integers(-4, 5, (N, 8, 15, m))
    lev = (rng.random((N, 8, m)) * (L + 1)).astype(np.int64)
    return np.concatenate([f & 63, lev[:, :, None]], axis=2)
def parts(rng):
    b = rng.integers(0, 64, (8, 15, 4)); C = rng.integers(1, 4, (N, 8, 1)); L = rng.choice(np.array([2, 3, 5]), (N, 8, 1))
    x = near(rng, b, V, C, L); gx = near(rng, b, H, C, L); c0 = rng.integers(0, 16, (N, 8, V))
    pl = rng.integers(0, W, (N, 8, 16, V)); dr = rng.integers(0, 4, (N, 8, 16, V))
    snd = np.ascontiguousarray(np.argsort(rng.random((N, 8, N - 1, V)), axis=-1)[..., :G])
    return x, gx, c0, pl, dr, snd
def pack(x, gx, c0, pl, dr, snd):
    return {"x": np.ascontiguousarray(x.reshape(N, 128, V)).astype(np.float32).astype(BF), "nb": np.ascontiguousarray((4 * pl + dr).reshape(N, 128, V)).astype(np.int32),
            "gx": np.ascontiguousarray(gx.reshape(N, 128, H)).astype(np.float32).astype(BF), "c0": c0.astype(np.float32).astype(BF),
            "snd": np.stack([gtable(a.reshape(8, -1)) for a in snd])}
def setup_inputs(rng):
    return pack(*parts(rng))
def setup_inputs_room(rng):
    x, gx, c0, pl, dr, snd = parts(rng); u = V // 4; P = rng.integers(16, 48, (8, 15, 1)); C = np.array([0, 1, CAP - 1, CAP, CAP + 1, G])
    first = ((CAP, CAP + 1, G, CAP - 1, 1, 0, CAP, CAP + 1), (CAP, CAP + 1, G, CAP - 1, 2, 1, G, CAP + 1))
    later = (first[0], (0, 0, 1, 0, 1, 0, CAP, CAP))
    watch, slots = {}, {}
    def close(m, g):
        return P[g] + rng.integers(-1, 2, (15, m))
    for q in range(N):
        for g in range(8):
            o = rng.permutation(V); a, b, t, w = o[:u], o[u:2 * u], o[2 * u:3 * u], o[3 * u:]
            watch[q, g] = w; gx[q, g, :15] = close(H, g); gx[q, g, 15] = 1
            x[q, g, 15, a] = rng.integers(20, 64, u); x[q, g, 15, b] = 0; x[q, g, 15, t] = 1; x[q, g, 15, w] = 2
            for part in (b, t, w): x[q, g, :15][:, part] = close(len(part), g)
            pl[q, g][:, a] = b[rng.integers(0, u, (16, u))]; pl[q, g][:, t] = b[rng.integers(0, u, (16, u))]
            c0[q, g, t] = rng.integers(0, 9, u)
            for i in range(int(rng.integers(1, 3))): pl[q, g][c0[q, g, t] + i, t] = a[rng.integers(0, u, u)]
            dr[q, g][:, t] = dr[q, g][:, t] & 1; dr[q, g][:, a[:u // 2]] = 0
            for d in range(N - 1):
                n = int(rng.choice(C)); k = n if rng.random() < 0.5 else min(n, int(rng.choice(C)))
                if q < 2 and d == 0: n, k = first[q][g], later[q][g]
                kind = np.repeat(np.array([2, 1, 0]), np.array([k, n - k, G - n]))
                v = np.concatenate([rng.permutation(a)[:k], rng.permutation(t)[:n - k], rng.permutation(b)[:G - n]])
                s = rng.permutation(G); kind = kind[s]; v = v[s]
                if (q + d + g) % 2 == 0 and 0 < n <= CAP:
                    i = int(np.flatnonzero(kind)[-1]); e = np.array([i, G - 1]); kind[e] = kind[e[::-1]]; v[e] = v[e[::-1]]
                snd[q, g, d] = v; m = np.flatnonzero(kind); z = np.flatnonzero(kind == 2)
                slots[q, g, d] = np.concatenate([np.array([0, G - 1]), m[:1], m[:CAP][-1:], m[CAP:CAP + 1], z[:1], z[-1:], rng.permutation(m)[:8], rng.integers(0, G, 4)]).astype(np.int64)
    for q in range(N):
        for g in range(8):
            w = watch[q, g]; see = np.concatenate([V + d * G + slots[(q - d - 1) % N, g, d] for d in range(N - 1)])
            pl[q, g][c0[q, g, w], w] = see[np.arange(len(w)) % len(see)]
    return pack(x, gx, c0, pl, dr, snd)
def setup_inputs_ties(rng):
    x, gx, c0, pl, dr, snd = parts(rng); b = rng.integers(TH + 1, 63 - TH, (8, 15, 1))
    def edge(m):
        n = Q - 1 + rng.integers(0, 2, (N, 8, 1, m)); k = np.argsort(rng.random((N, 8, 15, m)), axis=2) < n
        root = rng.random((N, 8, 1, m)) < 0.5
        f = b + np.where(root, 0, np.where(k, TH, TH + 1) * (2 * rng.integers(0, 2, (N, 8, 15, m)) - 1))
        return np.concatenate([f, np.where(root, 0, rng.choice(np.array([1, 1, 1, 2]), (N, 8, 1, m)))], axis=2)
    return pack(edge(V), edge(H), c0, pl, dr, snd)
def setup_inputs_ends(rng):
    x, gx, c0, pl, dr, snd = parts(rng)
    c0[:, ::2] = rng.integers(14, 16, (N, 4, V)); c0[:, 1] = 0
    x[:, 2:4, 15] = rng.choice(np.array([0, 62, 62, 63]), (N, 2, V)); gx[:, 2:4, 15] = rng.choice(np.array([61, 62, 63]), (N, 2, H))
    x[:, 4, :15] = 63 * rng.integers(0, 2, (N, 15, V)); dr[:, 5] = 3
    pl[:, 1] = rng.choice(np.array([0, V - 1, V, W - 1]), (N, 16, V)); pl[:, 5] = rng.choice(np.array([0, V - 1, V, W - 1]), (N, 16, V))
    pl[:, 3] = np.arange(V); pl[:, 6] = rng.integers(V, W, (N, 16, V)); pl[:, 7] = pl[:, 7, :1]
    snd[:, ::2] = rng.choice(np.array([0, V - 1, V // 2, 3]), (N, 4, N - 1, G))
    return pack(x, gx, c0, pl, dr, snd)
def setup_inputs_still(rng):
    x, gx, c0, pl, dr, snd = parts(rng); q = rng.permutation(N); a, b = int(q[0]), int(q[1])
    few = rng.permutation(V)[None, :] < CAP // 2
    x[a, :, 15] = np.where(few, np.maximum(x[a, :, 15], 1), 0); x[b, :, 15] = rng.integers(40, 64, (8, V))
    x[:, int(rng.integers(0, 8)), 15] = 0
    return pack(x, gx, c0, pl, dr, snd)
def setup_inputs_spread(rng):
    x, gx, c0, pl, dr, snd = parts(rng)
    def cols(m):
        f = (np.exp2(6 * rng.random((N, 8, 1, m))) * rng.random((N, 8, 15, m))).astype(np.int64)
        return np.minimum(np.concatenate([f, (64 * rng.random((N, 8, 1, m)) ** 3).astype(np.int64)], axis=2), 63)
    pl = np.minimum((W * rng.random(pl.shape) ** 2).astype(np.int64), W - 1); c0 = np.minimum((16 * rng.random(c0.shape) ** 2).astype(np.int64), 15)
    return pack(cols(V), cols(H), c0, pl, dr, snd)
def check_inputs(d):
    bad = []
    for k, hi in (("x", 63), ("gx", 63), ("c0", 15)):
        a = np.asarray(d[k]).astype(np.float32)
        if not np.all((a >= 0) & (a <= hi) & (a == np.floor(a))): bad.append("numbers of " + k)
    for k, hi in (("nb", 4 * W - 1), ("snd", V - 1)):
        if np.min(d[k]) < 0 or np.max(d[k]) > hi: bad.append("range of " + k)
    return bad
def reference(x, nb, gx, c0, snd):
    own = x.astype(np.float32).astype(np.int64).reshape(N, 8, 16, V); gh = gx.astype(np.float32).astype(np.int64).reshape(N, 8, 16, H)
    cur = c0.astype(np.float32).astype(np.int64)
    e = nb.astype(np.int64).reshape(N, 8, 16, V); pl = e >> 2; dr = e & 3
    sl = np.stack([gentries(a) for a in snd]).astype(np.int64).reshape(N, 8, N - 1, G)
    root = own[:, :, 15] == 0
    for s in range(RO):
        p = np.take_along_axis(pl, cur[:, :, None], 2)
        diff = np.take_along_axis(np.concatenate([own, gh], axis=3), p, 3) - own
        votes = np.add.reduce((np.abs(diff[:, :, :15]) <= TH).astype(np.int64), axis=2)
        ok = (votes >= Q) & (diff[:, :, 15] == -1)
        moved = ~ok & ~root
        f, lev = own[:, :, :15], own[:, :, 15]
        f = np.where(ok[:, :, None], f + np.clip(diff[:, :, :15], -1, 1), np.where(moved[:, :, None], (f + dr[:, :, :15]) & 63, f))
        lev = np.where(moved & (cur == 15), np.minimum(lev + 1, 63), lev)
        cur = np.where(moved, (cur + 1) & 15, cur)
        own = np.concatenate([f, lev[:, :, None]], axis=2)
        if s == RO - 1: break
        for a in range(N):
            for t in range(1, N):
                q = (a - t) % N; ix = sl[q, :, t - 1]
                m = np.take_along_axis(moved[q], ix, 1).astype(np.int64); before = np.add.accumulate(m, axis=1) - m
                come = ((m == 1) & (before < CAP))[:, None, :]
                v = np.take_along_axis(own[q], ix[:, None, :], 2)
                gh[a, :, :, (t - 1) * G:t * G] = np.where(come, v, gh[a, :, :, (t - 1) * G:t * G])
    return {"yx": own.reshape(N, 128, V).astype(np.float32).astype(BF), "yc": cur.astype(np.float32)}

@@ -1,0 +1,644 @@
+from concourse.bass import DstId, RemoteDMATransfer
+from concourse.mybir import AluOpType as ALU, ActivationFunctionType as ACT
+
+N, V, G, RO = 4, 3584, 384, 5
+H = (N - 1) * G
+LC, SC = V // 16, H // 16
+OWN, GH = H, H + V
+CH = [56, 56, 56, 56]
+BIG = 2.0 ** 17
+
+
+def _sb(cols, dtype):
+    return ("sbuf", [128, cols], dtype)
+
+
+SCRATCH = {"xb0": _sb(V + 2 * H, "bfloat16"), "xb1": _sb(V + 2 * H, "bfloat16"), "nbt": _sb(V, "int32"),
+           "tw": _sb(3 * V + 64, "bfloat16"), "mb": _sb(H, "bfloat16"), "inc": _sb(H, "bfloat16"), "ycs": _sb(1024, "float32"),
+           "pi": _sb(8, "int32"), "col": _sb(32, "float32"), "colb": _sb(16, "bfloat16"), "one": _sb(512, "bfloat16"),
+           "bt": _sb(32, "bfloat16"), "cu": _sb(512, "bfloat16"), "wi": _sb(16, "int32"), "wa": _sb(80, "float32"),
+           "wtab": _sb(16, "bfloat16"), "k72": _sb(SC, "bfloat16"), "ee": _sb(2 * LC, "float32"), "li": _sb(4 * LC, "int32"),
+           "qlo": _sb(5 * LC, "int32"), "qhi": _sb(5 * LC, "int32"), "qq": _sb(5 * LC, "float32"),
+           "sndi": _sb(SC, "int32"), "sndu": _sb(SC, "uint16"), "soff": _sb(SC, "uint16"),
+           "ps": ("psum", [128, 4096], "float32")}
+SCRATCH.update({n: _sb(V, "bfloat16") for n in ("zz", "wsb", "lr", "pb", "ph", "pl", "dd", "aa", "tt", "sg", "yy", "x2")})
+SCRATCH.update({n: _sb(144, "bfloat16") for n in ("b0", "bv", "be", "bo", "bz", "bi", "bm")})
+SCRATCH.update({n: _sb(128, "bfloat16") for n in ("idn", "idm", "idb", "ids", "idv")})
+SCRATCH.update({n: _sb(LC, "float32") for n in ("nr", "z", "t1", "t2", "t3", "t4", "t5", "pos", "posc", "pf0", "pf", "ff")})
+SCRATCH.update({n: _sb(LC, "int32") for n in ("zi", "ci")})
+SCRATCH.update({n: _sb(LC, "uint16") for n in ("cu16", "off", "sel")})
+SCRATCH.update({n: _sb(LC, "bfloat16") for n in ("bias", "curb")})
+SCRATCH.update({n: _sb(SC, "float32") for n in ("sndp", "mpos", "s1", "s2")})
+SEMAPHORES = (["qv", "qs", "qp", "qg"] + ["d%d" % k for k in range(40)]
+              + ["arr%d" % k for k in range(RO)] + ["loc%d" % k for k in range(RO)])
+
+PLAN = {"T": ["ssvs", "sshs", "sshs", "sshs", "shvs"], "W": ["ssss", "sshh", "sshh", "sshh", "sshh"],
+        "X": ["hsss", "shsv", "shsv", "shsv", "sssh"], "C": ["ssvv", "svvv", "svvv", "svvv", "svss"], "D": ["vsvv"] * 5,
+        "R1": "ssss", "XS": "sss", "X2": "ssss", "FB": "svs", "GS": 36, "TOL": 0.1, "SP": 1, "LT": 1, "TRY": 2500}
+CY, PCY, FIX, LAT, GA, TTB, REMOTE_US = 1.0e-3, 0.5e-3, 0.06, 0.10, 1.5, 1.5, 4.5
+ORDER = []
+
+
+def build(g, core, T, topo, ops):
+    rank = T.rank_of(core)
+    late = [1]
+
+    def reg(name, lo, hi):
+        if name == "ps":
+            return [("ps%d" % b, 0, 1) for b in range(lo // 512, (hi - 1) // 512 + 1)]
+        return [(name, lo, hi)]
+
+    def A(name, lo=0, hi=None, step=1, p0=0, p1=128):
+        hi = SCRATCH[name][1][1] if hi is None else hi
+        ap = T[name][p0:p1, lo:hi:step] if step > 1 else T[name][p0:p1, lo:hi]
+        return (ap, reg(name, lo, hi), (hi - lo + step - 1) // step, SCRATCH[name][2], name)
+
+    def PS(bank, lo, hi):
+        return A("ps", 512 * bank + lo, 512 * bank + hi)
+
+    def IND(win, offs):
+        return (win[0].indirect(offs[0]), win[1] + offs[1], 16 * offs[2], win[3], "ind")
+
+    def add(q, fn, reads, writes, dur, kind="c", extra=None):
+        ops.append({"q": q, "fn": fn, "r": reads, "w": writes, "dur": dur, "kind": kind, "x": extra, "late": late[0]})
+        return len(ops) - 1
+
+    def two(*aps):
+        return all(a[3] in ("bfloat16", "uint16") for a in aps)
+
+    def sc(s):
+        return (s[0], s[1]) if isinstance(s, tuple) else (s, [])
+
+    def vcost(n, f):
+        return FIX + CY * max(64, n * f)
+
+    def ts(out, in0, s1, op0, s2=None, op1=None):
+        a1, r1 = sc(s1); a2, r2 = sc(s2)
+        f = GA if in0[4] == "ind" else (0.5 if two(out, in0) else 1.0)
+        if op1 is None:
+            fn = lambda: g.vector.tensor_scalar(out[0], in0[0], a1, None, op0)
+        else:
+            fn = lambda: g.vector.tensor_scalar(out[0], in0[0], a1, a2, op0, op1)
+        return add("v", fn, in0[1] + r1 + r2, out[1], vcost(out[2], f))
+
+    def tt(out, in0, in1, op):
+        f = GA if in0[4] == "ind" else (1.0 if "ps" in (in0[4], in1[4]) else (TTB if two(out, in0, in1) else 2.0))
+        return add("v", lambda: g.vector.tensor_tensor(out[0], in0[0], in1[0], op), in0[1] + in1[1], out[1], vcost(out[2], f))
+
+    def cp(out, in0):
+        f = GA if in0[4] == "ind" else (0.5 if two(out, in0) else 1.0)
+        return add("v", lambda: g.vector.tensor_copy(out[0], in0[0]), in0[1], out[1], vcost(out[2], f))
+
+    def ms(out, val):
+        return add("v", lambda: g.vector.memset(out[0], val), [], out[1], vcost(out[2], 0.5 if two(out) else 1.0))
+
+    def scan(out, in0):
+        return add("v", lambda: g.vector.tensor_tensor_scan(out[0], in0[0], in0[0], 0.0, ALU.add, ALU.max), in0[1], out[1], vcost(out[2], 0.5))
+
+    def act(out, in0, func, bias=0.0, scale=1.0):
+        ab, rb = sc(bias); as_, rs = sc(scale)
+        f = GA if in0[4] == "ind" else 1.0
+        return add("s", lambda: g.scalar.activation(out[0], in0[0], func, bias=ab, scale=as_), in0[1] + rb + rs, out[1], vcost(out[2], f))
+
+    def mm(items):
+        def fn():
+            ins = None
+            for o, l, r, st, sp in items:
+                ins = g.tensor.matmul(o[0], l[0], r[0], st, sp)
+            return ins
+        rd, wr, dur = [], [], FIX
+        for o, l, r, st, sp in items:
+            rd += l[1] + r[1]; wr += o[1]; dur += PCY * max(min(64, l[2]), r[2])
+        return add("p", fn, sorted(set(rd)), sorted(set(wr)), dur)
+
+    def iota(out, pattern, base, cm):
+        if out[3] == "int32":
+            fn = lambda: g.iota(out[0], pattern, base, cm)
+        else:
+            fn = lambda: g.iota(out[0], pattern, base, cm, allow_small_or_imprecise_dtypes=True)
+        return add("g", fn, [], out[1], 0.13 + 2 * CY * out[2])
+
+    def asel(out, in0, pattern, cmp_, base, cm):
+        return add("g", lambda: g.affine_select(out[0], in0[0], pattern, cmp_, 0.0, base, cm), in0[1], out[1], 0.17 + 2 * CY * out[2])
+
+    def dma(q, out, in_, reads, writes, nbytes):
+        eng = g.sync if q == "y" else g.scalar
+        return add(q, lambda: eng.dma_start(out, in_), reads, writes, 2.0 + nbytes / 200e3, "dma")
+
+    def listmm(out, band, src, lo, hi, k=128, start=True, stop=True):
+        return [(out, A(band, 15 - i, 143 - i, p1=k), A(src, lo + i, hi, 16, p1=k), start and i == 0, stop and i == 15)
+                for i in range(16)]
+
+    cols = {}
+
+    def C(name):
+        return A("col", cols[name], cols[name] + 1)
+
+    def CB(k):
+        return A("colb", k, k + 1)
+
+    def DL(t):
+        return PS(6, 96, 96 + LC) if t % 2 else PS(7, 160, 160 + LC)
+
+    def Q(name, t):
+        return A(name, t * LC, (t + 1) * LC)
+
+    nch = len(CH)
+    c0s = [sum(CH[:k]) for k in range(nch + 1)]
+    tw0 = [3 * 16 * c0s[k] + 16 * k for k in range(nch)]
+    xb = ["xb0", "xb1"]
+
+    late[0] = 0
+    dma("s", T.zz[0:8, :], T.c0[:, :], [], reg("zz", 0, V), 60e3)
+    dma("s", T.zz[8:16, :], T.x[15::16, :], [], [("zz2", 0, 1)], 60e3)
+    cuts = [0, 8 * CH[0]] + [16 * c for c in c0s[1:]]
+    for a, b in zip(cuts, cuts[1:]):
+        dma("y", T.nbt[:, a:b], T.nb[:, a:b], [], reg("nbt", a, b), 512 * b)
+    dma("y", T.xb0[:, GH:GH + H], T.gx[:, :], [], reg("xb0", GH, GH + H), 2.2e6)
+    dma("y", T.sndi[:, :], T.snd[:, :], [], reg("sndi", 0, SC), 2.2e6)
+    dma("y", T.xb0[:, OWN:GH], T.x[:, :], [], reg("xb0", OWN, GH), 3.1e6)
+    late[0] = 1
+
+    iota(A("pi", 0, 1), [[0, 1]], 0, 1)
+    ts(A("pi", 1, 2), A("pi", 0, 1), 15, ALU.bitwise_and)
+    ts(A("pi", 2, 3), A("pi", 0, 1), 1, ALU.bitwise_and)
+    cols.update({"pm": 0, "lev": 1, "zw": 2, "zx": 3, "ys": 23, "we": 24, "wo": 25})
+    cp(C("pm"), A("pi", 1, 2))
+    ts(C("lev"), A("pi", 1, 2), 15.0, ALU.is_equal)
+    ts(C("zx"), A("pi", 0, 1), 8.0, ALU.is_ge, 16.0, ALU.mult)
+    ts(C("zw"), C("zx"), 1.0, ALU.max)
+    percol = {"xs": (1.25, 1.0), "xb": (-40.0, 128.0), "f1": (1.0, 0.0), "rb": (704.0, 64.0), "xn": (-40.0, -32.0),
+              "yb": (0.0, -160.0), "wv": (-BIG, -16 * BIG), "wi": (0.0, -2 * BIG), "wm": (0.0, 400 * BIG),
+              "w80": (-80.0, -64.0), "wn": (-39.5, -191.5), "wt": (40.0, 192.0)}
+    for k, nm in enumerate(percol):
+        cols[nm] = 4 + k
+        ts(C(nm), C("lev"), percol[nm][1] - percol[nm][0], ALU.mult, percol[nm][0], ALU.add)
+    ts(C("ys"), C("lev"), 0.8, ALU.max)
+    ts(C("we"), A("pi", 2, 3), -0.25, ALU.mult, 0.25, ALU.add)
+    ts(C("wo"), A("pi", 2, 3), 0.25, ALU.mult)
+    MAG = 1.5 * 2 ** 27
+    for k, (f, l) in enumerate([(MAG, 0.0), (0.0, 0.0), (-1.0, 0.0), (1.0, 0.0), (0.0, 1.0), (1.25, 1.0), (-40.0, 128.0)]):
+        if k == 1:
+            ts(CB(1), CB(0), C("lev"), ALU.subtract)
+        else:
+            ts(CB(k), C("lev"), l - f, ALU.mult, f, ALU.add)
+
+    ms(A("one"), 1.0)
+    ms(A("b0"), 0.0)
+    ms(A("bz"), 0.0)
+    asel(A("bt", 0, 16), A("one", 0, 16), [[-8, 2], [-1, 8]], ALU.is_equal, 0, 1)
+    tt(A("bt", 24, 32), A("bt", 0, 8), A("bt", 8, 16), ALU.add)
+    ts(A("bz", 15, 143, 16), A("bt", 24, 32), C("zw"), ALU.mult)
+    asel(A("bt", 16, 24), A("one", 0, 8), [[-16, 8]], ALU.is_ge, 0, 1)
+    asel(A("b0", 15, 143, 16), A("bt", 16, 24), [[16, 8]], ALU.is_ge, 15, -1)
+    asel(A("idn"), A("one", 0, 128), [[-1, 128]], ALU.is_equal, 0, 1)
+    for nm, c in (("be", "we"), ("bo", "wo"), ("bv", "wv"), ("bi", "wi"), ("bm", "wm")):
+        act(A(nm), A("b0"), ACT.Identity, scale=C(c))
+    act(A("idm"), A("idn"), ACT.Identity, scale=-1.0)
+    act(A("idb"), A("idn"), ACT.Identity, scale=BIG)
+    act(A("ids"), A("idn"), ACT.Identity, scale=C("xn"))
+    act(A("idv"), A("idn"), ACT.Identity, scale=C("w80"))
+    iota(A("wi"), [[-1, 16]], 128, 1)
+    ts(A("wi"), A("wi"), 15, ALU.bitwise_and)
+    ts(A("wa", 0, 16), A("wi"), 1.5, ALU.is_le)
+    ts(A("wa", 16, 32), A("wi"), 3.5, ALU.is_le, 256.0, ALU.mult)
+    ts(A("wa", 32, 48), A("wi"), 1.5, ALU.is_ge)
+    ts(A("wa", 48, 64), A("wi"), 4.0, ALU.is_equal, 65536.0, ALU.mult)
+    tt(A("wa", 16, 32), A("wa", 16, 32), A("wa", 32, 48), ALU.mult)
+    tt(A("wa", 0, 16), A("wa", 0, 16), A("wa", 48, 64), ALU.add)
+    tt(A("wtab"), A("wa", 0, 16), A("wa", 16, 32), ALU.add)
+    for k in range(nch):
+        iota(A("pos", c0s[k], c0s[k + 1]), [[16, CH[k]]], 16, 0)
+        ms(A("tw", tw0[k], tw0[k] + 16), 0.0)
+    iota(A("mpos"), [[16, SC]], 0, 0)
+    asel(A("cu"), A("one"), [[-1, 16], [-16, 32]], ALU.is_equal, 0, 1)
+    ms(A("k72"), -207.0)
+
+    ZL = PS(7, 0, LC)
+    o = mm(listmm(ZL, "bz", "zz", 0, V, k=16))
+    ops[o]["r"] = ops[o]["r"] + [("zz2", 0, 1)]
+    cp(A("zi"), ZL)
+    ts(A("ci"), A("zi"), 15, ALU.bitwise_and)
+    cp(A("cu16"), A("ci"))
+    ts(A("nr"), A("zi"), 16.0, ALU.is_ge)
+    ts(A("bias"), A("nr"), 32.5, ALU.mult, -8.0, ALU.add)
+    ts(A("t1"), A("zi"), 63.0 * 16, ALU.is_ge, 16.0, ALU.mult)
+    ts(A("t4"), A("ci"), -1.0, ALU.mult, 15.0, ALU.add)
+    tt(A("z"), A("t1"), A("t4"), ALU.add)
+    ts(A("pos"), A("pos"), C("pm"), ALU.add)
+    tt(A("posc"), A("pos"), A("nr"), ALU.mult)
+    even = len(set(CH)) == 1
+    parts = [(0, LC, CH[0])] if even else [(c0s[k], c0s[k + 1], CH[k]) for k in range(nch)]
+    for la, lb, wc in parts:
+        ts(A("pf0", la, lb), A("pos", la, lb), 16.0 * wc, ALU.add)
+
+    def failpos():
+        for la, lb, wc in parts:
+            ts(A("t1", la, lb), A("z", la, lb), 0.0, ALU.is_equal, 16.0 * wc, ALU.mult)
+        tt(A("pf"), A("t1"), A("pf0"), ALU.add)
+    failpos()
+    ts(A("mpos"), A("mpos"), C("pm"), ALU.add)
+    cp(A("sndu"), A("sndi"))
+    ts(A("sndp"), A("sndi"), float(OWN), ALU.add)
+
+    def scale_in(e, lo, hi):
+        if e == "v":
+            ts(A("xb0", lo, hi), A("xb0", lo, hi), CB(5), ALU.mult, CB(6), ALU.add)
+        else:
+            act(A("xb0", lo, hi), A("xb0", lo, hi), ACT.Identity, bias=C("xb"), scale=C("xs"))
+
+    peers = [c for c in T.cores if c != core]
+    far = sorted(set(e for c in peers if topo.chip(c) != topo.chip(core) for e in topo.engines(core, c)))
+
+    def send(n, pairs, src, so, dst, do):
+        nfar = sum(topo.chip(T.cores[p]) != topo.chip(core) for p, _ in pairs)
+        tr, kf, kn, tot = [], 0, 0, 0
+        for p, blk in pairs:
+            dc = T.cores[p]
+            assert topo.may_write(core, dc)
+            if topo.chip(dc) != topo.chip(core):
+                w = len(far) // nfar
+                es = far[kf * w:(kf + 1) * w]; kf += 1
+            else:
+                free = [e for e in topo.engines(core, dc) if e not in far]
+                w = len(free) // (len(pairs) - nfar)
+                es = free[kn * w:(kn + 1) * w]; kn += 1
+            rid, pid, _ = topo.addr(dc)
+            tr.append(RemoteDMATransfer(dst_ids=[DstId(rid=rid, pnc=pid)], dma_engine_mask=sum(1 << e for e in es),
+                                        remote_sem=T.sem["arr%d" % n], src=T[src][:, so + blk * G:so + (blk + 1) * G],
+                                        dst=T[dst][:, do + blk * G:do + (blk + 1) * G]))
+            tot += len(es)
+        s = add("g", lambda: g.remote_dma_fused(tr, local_sem=T.sem["loc%d" % n]),
+                reg(src, so, so + H) + [("sent", 0, 1)], [("sent", 0, 1)], REMOTE_US - 1.0, "send", ("loc%d" % n, tot))
+        add("x", None, [], reg(dst, do, do + H), REMOTE_US, "arrive", ("arr%d" % n, tot, s))
+
+    scale_in(PLAN["XS"][0], GH, GH + H)
+    late[0] = 0
+    send(RO - 1, [((rank - d) % N, d - 1) for d in range(1, N)], "xb0", GH, "xb1", 0)
+    late[0] = 1
+    scale_in(PLAN["XS"][1], OWN, OWN + V // 2)
+    scale_in(PLAN["XS"][2], OWN + V // 2, GH)
+    dma("y", T.x2[:, :], T.xb0[:, OWN:GH], reg("xb0", OWN, GH), reg("x2", 0, V), 1e6)
+
+    MAG2 = 1.5 * 2 ** 31
+    sub = 0
+    for k in range(nch):
+        w = 16 * CH[k]; n = w // 2
+        for hf in range(2):
+            a = 16 * c0s[k] + hf * n; b = a + n
+            HP, WP, RP = PS(sub % 2, 0, n), PS(2 + sub % 2, 0, n), PS(4, 0, n)
+            late[0] = 0
+            act(A("wsb", a, b), IND(A("wtab"), A("cu16", a // 16, b // 16)), ACT.Identity)
+            ts(HP, A("nbt", a, b), MAG2, ALU.add, MAG2, ALU.subtract)
+            tt(A("lr", a, b), A("nbt", a, b), HP, ALU.subtract)
+            tt(A("ph", a, b), HP, A("wsb", a, b), ALU.mult)
+            act(A("pb", a, b), A("lr", a, b), ACT.Identity, bias=702.5)
+            mm([(WP, A("idn"), A("wsb", a, b), True, True)])
+            tt(A("pl", a, b), WP, A("pb", a, b), ALU.mult)
+            late[0] = 1
+            mm([(RP, A("idn"), A("lr", a, b), True, False), (RP, A("idm"), A("pb", a, b), False, True)])
+            r0 = tw0[k] + 16 + w + hf * n
+            act(A("tw", r0, r0 + n), RP, ACT.Identity, bias=C("rb"), scale=C("f1"))
+            sub += 1
+        r0 = tw0[k] + 16 + w
+        if PLAN["R1"][k] == "v":
+            ts(A("tw", r0 + w, r0 + 2 * w), A("tw", r0, r0 + w), CB(4), ALU.add)
+        else:
+            act(A("tw", r0 + w, r0 + 2 * w), A("tw", r0, r0 + w), ACT.Identity, bias=C("lev"))
+        late[0] = 0
+        for bank, band in ((5, "be"), (6, "bo")):
+            for j, src in ((1, "ph"), (0, "pl")):
+                mm(listmm(PS(bank, j * LC + c0s[k], j * LC + c0s[k + 1]), band, src, 16 * c0s[k], 16 * c0s[k + 1]))
+    OL, OH = PS(6, 0, LC), PS(6, LC, 2 * LC)
+    act(A("ee"), PS(5, 0, 2 * LC), ACT.Identity)
+    tt(A("t5"), OL, Q("ee", 0), ALU.is_gt)
+    tt(Q("li", 0), OL, Q("ee", 0), ALU.max)
+    ts(A("t5"), A("t5"), 0.5, ALU.subtract, 2.0 ** 30, ALU.mult)
+    tt(Q("li", 1), OL, Q("ee", 0), ALU.min)
+    tt(OH, OH, A("t5"), ALU.add)
+    tt(Q("li", 2), OH, Q("ee", 1), ALU.max)
+    tt(Q("li", 3), OH, Q("ee", 1), ALU.min)
+    for t in range(RO):
+        for dst, base, mask in (("qlo", 0, 255), ("qhi", 2, 127 * 64)):
+            if t > 1:
+                ts(Q(dst, t), Q("li", base + t % 2), 8 * (t // 2), ALU.arith_shift_right, mask, ALU.bitwise_and)
+            else:
+                ts(Q(dst, t), Q("li", base + t), mask, ALU.bitwise_and)
+        tt(Q("qq", t), Q("qlo", t), Q("qhi", t), ALU.add)
+        if t == 0:
+            ts(A("off"), Q("qq", 0), 176.0, ALU.subtract)
+            late[0] = 1
+        ts(Q("qq", t), Q("qq", t), 8192.0 * t - 176.0, ALU.add)
+
+    UB = 7 * 512 - c0s[2]
+    slot = [0]
+
+    def look(s, k, cur):
+        ca, cb = c0s[k], c0s[k + 1]
+        a, b = 16 * ca, 16 * cb
+        U, CC = A("ps", UB + ca, UB + cb), A("tw", tw0[k] + 16, tw0[k] + 16 + b - a)
+        if PLAN["D"][s][k] == "s":
+            n = min(512, b - a - 32)
+            pd = 1024 * slot[0] + 512 - n
+            slot[0] = (slot[0] + 1) % (2 if s == RO - 1 else 3)
+            D = A("ps", pd, pd + b - a)
+
+            def part(lo, hi):
+                act(A("dd", lo, hi), IND(A(cur, OWN, GH + H), A("off", lo // 16, hi // 16)), ACT.Identity)
+                o_ = A("ps", pd + lo - a, pd + hi - a)
+                mm([(o_, A("idm"), A(cur, OWN + lo, OWN + hi), True, False), (o_, A("idn"), A("dd", lo, hi), False, True)])
+        else:
+            n = (ca + cb) // 4 * 32 - a
+            D = A("dd", a, b)
+
+            def part(lo, hi):
+                tt(A("dd", lo, hi), IND(A(cur, OWN, GH + H), A("off", lo // 16, hi // 16)), A("x2", lo, hi), ALU.subtract)
+        return [lambda: part(a, a + n), lambda: part(a + n, b),
+                lambda: ts(A("aa", a, b), D, CB(0), ALU.add, CB(1), ALU.is_equal),
+                lambda: mm([(U, A("idb"), A("bias", ca, cb), True, False)] + listmm(U, "bv", "aa", a, b, start=False)),
+                lambda: (ts(CC, D, CB(2), ALU.max, CB(3), ALU.min) if PLAN["C"][s][k] == "v"
+                         else act(CC, D, ACT.Sign, scale=C("f1")))]
+
+    for s in range(RO):
+        cur, new = xb[s % 2], xb[(s + 1) % 2]
+        last = s == RO - 1
+        late[0] = 0
+        ns = 2 if last else 3
+        slot[0] = 0 if last else slot[0]
+        for k in range(nch):
+            ca, cb = c0s[k], c0s[k + 1]
+            a, b = 16 * ca, 16 * cb; w = b - a
+            eT, eW, eX = PLAN["T"][s][k], PLAN["W"][s][k], PLAN["X"][s][k]
+            U = A("ps", UB + ca, UB + cb)
+            if k == 0:
+                for f in look(s, 0, cur):
+                    f()
+            nxt = look(s, k + 1, cur) if k + 1 < nch else [None] * 5
+            picks = [lambda: tt(A("t2", ca, cb), U, A("posc", ca, cb), ALU.max),
+                     lambda: tt(A("t3", ca, cb), A("t2", ca, cb), A("pf", ca, cb), ALU.min),
+                     lambda: cp(A("sel", ca, cb), A("t3", ca, cb))]
+            both = [nxt[0], picks[0], nxt[1], picks[1], nxt[2], picks[2], nxt[3], nxt[4]]
+            if PLAN["SP"] == 0 or (PLAN["SP"] == 2 and k == 0):
+                both = picks
+            for f in both:
+                if f:
+                    f()
+            n = min(512, w - 32)
+            pb_ = 1024 * slot[0] + 512 - n
+            P1 = [A("ps", pb_, pb_ + n), A("ps", pb_ + n, pb_ + w)]
+            pb_ = 1024 * ((slot[0] + 1) % ns) + 512 - n
+            slot[0] = (slot[0] + 2) % ns
+            P = [A("ps", pb_, pb_ + n), A("ps", pb_ + n, pb_ + w)]
+            vw = [eW == "v" or (eW == "h" and hf == 0) for hf in range(2)]
+            vx = [eX == "v" or (eX == "h" and hf == 0) for hf in range(2)]
+            alone = [vw[hf] and vx[hf] and not last for hf in range(2)]
+            win = A("tw", tw0[k], tw0[k] + 16 + 3 * w)
+            hv = [(a, a + n), (a + n, b)]
+            for hf, (lo, hi) in enumerate(hv):
+                src = IND(win, A("sel", lo // 16, hi // 16))
+                if eT == "v" or (eT == "h" and hf == 0):
+                    ts(A("tt", lo, hi), src, CB(5), ALU.mult)
+                else:
+                    act(A("tt", lo, hi), src, ACT.Identity, scale=C("xs"))
+                late[0] = PLAN["LT"]
+                mm([(P1[hf], A("idn"), A(cur, OWN + lo, OWN + hi), True, False)])
+                mm([(P1[hf], A("idn"), A("tt", lo, hi), False, True)])
+                late[0] = 0
+            late[0] = PLAN["LT"]
+            for hf, (lo, hi) in enumerate(hv):
+                if not alone[hf]:
+                    mm([(P[hf], A("idn"), A(cur, OWN + lo, OWN + hi), True, False), (P[hf], A("idn"), A("tt", lo, hi), False, False)])
+            for hf, (lo, hi) in enumerate(hv):
+                if alone[hf]:
+                    ts(A("sg", lo, hi), P1[hf], C("wt"), ALU.is_ge, C("w80"), ALU.mult)
+                    tt(A(new, OWN + lo, OWN + hi), P1[hf], A("sg", lo, hi), ALU.add)
+                    continue
+                if vw[hf]:
+                    ts(A("sg", lo, hi), P1[hf], C("wt"), ALU.is_ge, 0.5, ALU.subtract)
+                else:
+                    act(A("sg", lo, hi), P1[hf], ACT.Sign, bias=C("wn"))
+                mm([(P[hf], A("idv" if vw[hf] else "ids"), A("sg", lo, hi), False, True)])
+            for hf, (lo, hi) in enumerate(hv):
+                if alone[hf]:
+                    continue
+                if last and vx[hf]:
+                    ts(A("yy", lo, hi), P[hf], C("ys"), ALU.mult, C("yb"), ALU.add)
+                elif last:
+                    act(A("yy", lo, hi), P[hf], ACT.Identity, bias=C("yb"), scale=C("ys"))
+                elif vx[hf]:
+                    ts(A(new, OWN + lo, OWN + hi), P[hf], C("xn"), ALU.add)
+                else:
+                    act(A(new, OWN + lo, OWN + hi), P[hf], ACT.Identity, bias=C("xn"))
+            late[0] = 0
+            if both is picks and nxt[0]:
+                for f in nxt:
+                    f()
+            if last:
+                dma("y", T.yx[:, a:b], T.yy[:, a:b], reg("yy", a, b), [], 256 * w)
+                if k >= nch - 2:
+                    k0 = 0 if k < nch - 1 else k
+                    la, lb = c0s[k0], cb
+                    ts(A("ff", la, lb), A("ps", UB + la, UB + lb), 0.0, ALU.is_gt)
+                    tt(A("z", la, lb), A("z", la, lb), A("ff", la, lb), ALU.subtract)
+                    ts(A("zi", la, lb), A("z", la, lb), -1.0, ALU.mult, 31.0, ALU.add)
+                    ts(A("ci", la, lb), A("zi", la, lb), 15, ALU.bitwise_and)
+                    cp(A("curb", la, lb), A("ci", la, lb))
+                    for j in range(k0, k + 1):
+                        h2 = CH[j] // 2
+                        for hf in range(2):
+                            mm([(A("ps", (4 + hf) * 512 + i, (4 + hf) * 512 + 16 * h2, 16, 32 * j, 32 * j + 32),
+                                 A("cu", 32 * i, 32 * i + 32), A("curb", c0s[j] + hf * h2, c0s[j] + (hf + 1) * h2), True, True)
+                                for i in range(16)])
+                    mark = [("ycs%d" % k0, 0, 1)]
+                    runs = [(k0, k + 1)] if len(set(CH[k0:k + 1])) == 1 else [(j, j + 1) for j in range(k0, k + 1)]
+                    for j0, j1 in runs:
+                        h2 = 8 * CH[j0]
+                        for hf in range(2):
+                            o_ = A("ycs", hf * h2, (hf + 1) * h2, 1, 32 * j0, 32 * j1)
+                            cp((o_[0], mark) + o_[2:], A("ps", (4 + hf) * 512, (4 + hf) * 512 + h2, 1, 32 * j0, 32 * j1))
+                    for j in range(k0, k + 1):
+                        dma("y", T.yc[:, 16 * c0s[j]:16 * c0s[j + 1]], T.ycs[32 * j:32 * j + 8, 0:16 * CH[j]], mark, [], 30e3)
+        if last:
+            break
+        for d in range(N - 1):
+            src = IND(A("tt"), A("sndu", d * G // 16, (d + 1) * G // 16))
+            if PLAN["FB"][d] == "v":
+                ts(A("mb", d * G, (d + 1) * G), src, 0.1, ALU.is_gt)
+            else:
+                act(A("mb", d * G, (d + 1) * G), src, ACT.Sign)
+        U2 = PS(6, 0, SC)
+        mm([(U2, A("idb"), A("k72"), True, False)] + listmm(U2, "bm", "mb", 0, H, start=False, stop=False))
+        for d in range(N - 1):
+            scan(A("inc", d * G, (d + 1) * G), A("mb", d * G, (d + 1) * G))
+        mm(listmm(U2, "bi", "inc", 0, H, start=False))
+        tt(A("s1"), U2, A("mpos"), ALU.max)
+        tt(A("s2"), A("s1"), A("sndp"), ALU.min)
+        cp(A("soff"), A("s2"))
+        hs = PLAN["GS"]
+        cp(A(cur, 0, 16 * hs), IND(A(new, 0, GH), A("soff", 0, hs)))
+        act(A(cur, 16 * hs, H), IND(A(new, 0, GH), A("soff", hs, SC)), ACT.Identity)
+        send(s, [((rank + d) % N, d - 1) for d in range(1, N)], cur, 0, new, GH)
+        late[0] = 1
+        for k in range(nch):
+            a, b = 16 * c0s[k], 16 * c0s[k + 1]
+            if PLAN["D"][s + 1][k] == "s":
+                continue
+            if PLAN["X2"][k] == "v":
+                cp(A("x2", a, b), A(new, OWN + a, OWN + b))
+            elif PLAN["X2"][k] == "s":
+                act(A("x2", a, b), A(new, OWN + a, OWN + b), ACT.Identity)
+            else:
+                dma("y", T.x2[:, a:b], T[new][:, OWN + a:OWN + b], reg(new, OWN + a, OWN + b), reg("x2", a, b), 256 * (b - a))
+        ts(A("ff"), A("ps", UB, UB + LC), 0.0, ALU.is_gt)
+        for t in range(RO - 1 - s):
+            tt(DL(t), A("ps", UB, UB + LC), Q("qq", t), ALU.max)
+            tt(A("zi") if s == RO - 2 else Q("qq", t), DL(t), Q("qq", t + 1), ALU.min)
+            if t == 0:
+                if s < RO - 2:
+                    cp(A("zi"), Q("qq", 0))
+                ts(A("ci"), A("zi"), 8191, ALU.bitwise_and)
+                cp(A("off"), A("ci"))
+        tt(A("z"), A("z"), A("ff"), ALU.subtract)
+        failpos()
+
+
+def depend(ops):
+    acc = {}
+    for i, o in enumerate(ops):
+        deps = set()
+        for regs, wr in ((o["r"], False), (o["w"], True)):
+            for name, lo, hi in regs:
+                for j, l2, h2, w2 in acc.get(name, []):
+                    if l2 < hi and lo < h2 and (w2 or wr or (name.startswith("ps") and ops[j]["q"] != o["q"])):
+                        deps.add(j)
+        if o["kind"] == "arrive":
+            deps = set()
+        for regs, wr in ((o["r"], False), (o["w"], True)):
+            for name, lo, hi in regs:
+                lst = acc.setdefault(name, [])
+                if wr:
+                    lst[:] = [e for e in lst if not (lo <= e[1] and e[2] <= hi)]
+                lst.append((i, lo, hi, wr))
+        o["d"] = deps
+
+
+def order(ops, shift=None):
+    n = len(ops)
+    pred = [set(o["d"]) | ({o["x"][2]} if o["kind"] == "arrive" else set()) for o in ops]
+    succ = [[] for _ in ops]
+    for i in range(n):
+        for j in pred[i]:
+            succ[j].append(i)
+    prio = [0.0] * n
+    for i in range(n - 1, -1, -1):
+        prio[i] = min([prio[j] for j in succ[i]] + [2.0 * n]) - 1e-3 if ops[i]["late"] else float(i)
+    if shift:
+        prio = [p + d for p, d in zip(prio, shift)]
+    left = [len(p) for p in pred]
+    ready = sorted((prio[i], i) for i in range(n) if not left[i])
+    free, fin, beg, can, out = {}, [0.0] * n, [0.0] * n, [0.0] * n, []
+    while ready:
+        pick = {}
+        for _, k in ready:
+            q = ops[k]["q"]
+            st = max(can[k], free.get(q, 0.0))
+            if q not in pick:
+                pick[q] = [st, k, st + PLAN["TOL"], False]
+            elif not pick[q][3] and st + ops[k]["dur"] <= pick[q][2]:
+                pick[q] = [st, k, 0.0, True]
+        st, i = min(p[:2] for p in pick.values())
+        o = ops[i]
+        ready.remove((prio[i], i))
+        beg[i] = st; fin[i] = st + o["dur"]
+        if o["q"] != "x":
+            free[o["q"]] = st + (0.1 if o["kind"] == "dma" else 1.0 if o["kind"] == "send" else o["dur"])
+        out.append(i)
+        for j in succ[i]:
+            chain = o["q"] == "p" and ops[j]["q"] == "p"
+            can[j] = max(can[j], st if ops[j]["kind"] == "arrive" else fin[i] + (0.0 if chain else LAT))
+            left[j] -= 1
+            if not left[j]:
+                ready.append((prio[j], j)); ready.sort()
+    return out, beg, fin
+
+
+def best_order(ops):
+    if not ORDER:
+        n, x = len(ops), 12345
+        shift = [0.0] * n
+        best = max(order(ops)[2])
+        for _ in range(PLAN["TRY"]):
+            z = list(shift)
+            for _ in range(2):
+                x = (x * 1103515245 + 12345) % 2 ** 31
+                z[(x >> 8) % n] += (-40, -20, -10, -5, 5, 10, 20, 40)[(x >> 4) % 8]
+            e = max(order(ops, z)[2])
+            if e <= best:
+                best, shift = e, z
+        ORDER.append(shift)
+    return order(ops, ORDER[0])
+
+
+def emit(g, T, ops, seq):
+    queue = {"v": g.vector, "s": g.scalar, "p": g.tensor, "g": g, "y": g.sync}
+    place, known, snap, waits, needed = {}, {}, {}, {}, set()
+    for n, i in enumerate(seq):
+        place[i] = n
+    for i in seq:
+        o = ops[i]
+        q = o["q"]
+        if q == "x":
+            snap[i] = {("e", i): 1}
+            continue
+        kn = known.setdefault(q, {})
+        ws = []
+        for j in sorted(o["d"], key=lambda j: -place[j]):
+            if q == "p" and ops[j]["q"] == "p":
+                continue
+            key, val = (ops[j]["q"], place[j]) if ops[j]["kind"] == "c" else (("e", j), 1)
+            if kn.get(key, -1) >= val:
+                continue
+            ws.append(j); needed.add(j)
+            for k2, v2 in snap[j].items():
+                if kn.get(k2, -1) < v2:
+                    kn[k2] = v2
+        waits[i] = ws
+        snap[i] = dict(kn)
+        if o["kind"] == "c":
+            snap[i][q] = place[i]
+        else:
+            snap[i][("e", i)] = 1
+    token, count, nd = {}, {}, 0
+    for i in seq:
+        o = ops[i]
+        if o["kind"] == "c":
+            if i in needed:
+                count[o["q"]] = count.get(o["q"], 0) + 1
+                token[i] = ("q" + o["q"], count[o["q"]])
+        elif o["kind"] == "dma":
+            token[i] = ("d%d" % nd, 16); nd += 1
+        else:
+            token[i] = o["x"][:2]
+    for i in seq:
+        o = ops[i]
+        if o["q"] == "x":
+            continue
+        for j in waits[i]:
+            queue[o["q"]].wait_ge(T.sem[token[j][0]], token[j][1])
+        ins = o["fn"]()
+        if o["kind"] == "dma":
+            ins.then_inc(T.sem[token[i][0]], 16)
+        elif o["kind"] == "c" and i in needed:
+            ins.then_inc(T.sem[token[i][0]], 1)
+    for i in seq:
+        if ops[i]["kind"] != "c" and i not in needed:
+            (g.sync if ops[i]["kind"] == "dma" else g).wait_ge(T.sem[token[i][0]], token[i][1])
+
+
+def rank_program(g, core, T, topo):
+    if T.rank_of(core) is None:
+        return
+    ops = []
+    build(g, core, T, topo, ops)
+    depend(ops)
+    emit(g, T, ops, best_order(ops)[0])

@@ -3,10 +3,12 @@ from concourse.mybir import AluOpType as ALU, ActivationFunctionType as ACT
 
 N, V, G, RO = 4, 3584, 384, 5
 H = (N - 1) * G
-LC, SC = V // 16, H // 16
+LC, SC, GC = V // 16, H // 16, G // 16
 OWN, GH = H, H + V
-CH = [56, 56, 56, 56]
-BIG = 2.0 ** 17
+NCH, CW = 4, 56
+W = 16 * CW
+TW = 16 + 3 * W
+K8 = 8192.0
 
 
 def _sb(cols, dtype):
@@ -14,34 +16,34 @@ def _sb(cols, dtype):
 
 
 SCRATCH = {"xb0": _sb(V + 2 * H, "bfloat16"), "xb1": _sb(V + 2 * H, "bfloat16"), "nbt": _sb(V, "int32"),
-           "tw": _sb(3 * V + 64, "bfloat16"), "mb": _sb(H, "bfloat16"), "inc": _sb(H, "bfloat16"), "ycs": _sb(1024, "float32"),
+           "tw": _sb(NCH * TW, "bfloat16"), "mb": _sb(H, "bfloat16"), "inc": _sb(H, "bfloat16"), "ycs": _sb(1024, "float32"),
            "pi": _sb(8, "int32"), "col": _sb(32, "float32"), "colb": _sb(16, "bfloat16"), "one": _sb(512, "bfloat16"),
-           "bt": _sb(32, "bfloat16"), "cu": _sb(512, "bfloat16"), "wi": _sb(16, "int32"), "wa": _sb(80, "float32"),
-           "wtab": _sb(16, "bfloat16"), "k72": _sb(SC, "bfloat16"), "ee": _sb(2 * LC, "float32"), "li": _sb(4 * LC, "int32"),
-           "qlo": _sb(5 * LC, "int32"), "qhi": _sb(5 * LC, "int32"), "qq": _sb(5 * LC, "float32"),
-           "sndi": _sb(SC, "int32"), "sndu": _sb(SC, "uint16"), "soff": _sb(SC, "uint16"),
-           "ps": ("psum", [128, 4096], "float32")}
-SCRATCH.update({n: _sb(V, "bfloat16") for n in ("zz", "wsb", "lr", "pb", "ph", "pl", "dd", "aa", "tt", "sg", "yy", "x2")})
+           "bt": _sb(8, "bfloat16"), "cu": _sb(512, "bfloat16"), "wi": _sb(16, "int32"), "wa": _sb(80, "float32"),
+           "wtab": _sb(16, "bfloat16"), "ee": _sb(2 * LC, "float32"), "li": _sb(4 * LC, "int32"), "mg": _sb(7 * 128, "bfloat16"),
+           "qlo": _sb(5 * LC, "int32"), "qhi": _sb(5 * LC, "int32"), "qq0": _sb(5 * LC, "float32"), "qq1": _sb(4 * LC, "float32"),
+           "gg": _sb(5 * LC, "bfloat16"), "sndi": _sb(SC, "int32"), "sndu": _sb(SC, "uint16"), "soff": _sb(SC, "uint16"),
+           "idf": _sb(128, "float32"), "ps": ("psum", [128, 4096], "float32")}
+SCRATCH.update({n: _sb(V, "bfloat16") for n in ("zc", "zl", "wsb", "hb", "lr", "pb", "ph", "pl", "dd", "aa", "tt", "sg", "x2")})
 SCRATCH.update({n: _sb(144, "bfloat16") for n in ("b0", "bv", "be", "bo", "bz", "bi", "bm")})
-SCRATCH.update({n: _sb(128, "bfloat16") for n in ("idn", "idm", "idb", "ids", "idv")})
-SCRATCH.update({n: _sb(LC, "float32") for n in ("nr", "z", "t1", "t2", "t3", "t4", "t5", "pos", "posc", "pf0", "pf", "ff")})
-SCRATCH.update({n: _sb(LC, "int32") for n in ("zi", "ci")})
+SCRATCH.update({n: _sb(128, "bfloat16") for n in ("idn", "idm", "idb", "idw", "idp", "idq", "idk", "idc", "id5", "id8", "id9", "idz")})
+SCRATCH.update({n: _sb(LC, "float32") for n in ("t3", "pf")})
 SCRATCH.update({n: _sb(LC, "uint16") for n in ("cu16", "off", "sel")})
-SCRATCH.update({n: _sb(LC, "bfloat16") for n in ("bias", "curb")})
-SCRATCH.update({n: _sb(SC, "float32") for n in ("sndp", "mpos", "s1", "s2")})
+SCRATCH.update({n: _sb(LC, "bfloat16") for n in ("bias", "curb", "nr", "pn", "posh", "c0b", "l63", "arm", "cb4", "par")})
+SCRATCH.update({n: _sb(SC, "float32") for n in ("sndp", "mpos", "s2")})
+SCRATCH.update({n: _sb(SC, "bfloat16") for n in ("ka", "kb")})
 SEMAPHORES = (["qv", "qs", "qp", "qg"] + ["d%d" % k for k in range(40)]
               + ["arr%d" % k for k in range(RO)] + ["loc%d" % k for k in range(RO)])
 
-PLAN = {"T": ["ssvs", "sshs", "sshs", "sshs", "shvs"], "W": ["ssss", "sshh", "sshh", "sshh", "sshh"],
-        "X": ["hsss", "shsv", "shsv", "shsv", "sssh"], "C": ["ssvv", "svvv", "svvv", "svvv", "svss"], "D": ["vsvv"] * 5,
-        "R1": "ssss", "XS": "sss", "X2": "ssss", "FB": "svs", "GS": 36, "TOL": 0.1, "SP": 1, "LT": 1, "TRY": 2500}
-CY, PCY, FIX, LAT, GA, TTB, REMOTE_US = 1.0e-3, 0.5e-3, 0.06, 0.10, 1.5, 1.5, 4.5
+PLAN = {"D": "svsv", "C": "ssss", "T": ["svvh"] * 5, "W": ["mmmm"] * 5, "X": ["ssss"] * 5, "X2": "ssss",
+        "DEC": 1, "R1": "ssss", "X20": "ssss", "FB": "svs", "GS": 36, "TOL": 0.1, "SP": 1, "LT": 1, "TRY": 6000, "SEED": 12345}
+CY, PCY, FIX, LAT, GA, REMOTE_US = 1.0e-3, 0.5e-3, 0.06, 0.10, 1.5, 4.5
 ORDER = []
 
 
 def build(g, core, T, topo, ops):
     rank = T.rank_of(core)
     late = [1]
+    first = [0]
 
     def reg(name, lo, hi):
         if name == "ps":
@@ -60,7 +62,8 @@ def build(g, core, T, topo, ops):
         return (win[0].indirect(offs[0]), win[1] + offs[1], 16 * offs[2], win[3], "ind")
 
     def add(q, fn, reads, writes, dur, kind="c", extra=None):
-        ops.append({"q": q, "fn": fn, "r": reads, "w": writes, "dur": dur, "kind": kind, "x": extra, "late": late[0]})
+        ops.append({"q": q, "fn": fn, "r": reads, "w": writes, "dur": dur, "kind": kind, "x": extra,
+                    "tag": len(ops) - first[0] if first[0] else -len(ops)})
         return len(ops) - 1
 
     def two(*aps):
@@ -82,7 +85,7 @@ def build(g, core, T, topo, ops):
         return add("v", fn, in0[1] + r1 + r2, out[1], vcost(out[2], f))
 
     def tt(out, in0, in1, op):
-        f = GA if in0[4] == "ind" else (1.0 if "ps" in (in0[4], in1[4]) else (TTB if two(out, in0, in1) else 2.0))
+        f = GA if in0[4] == "ind" else (1.0 if "ps" in (in0[4], in1[4]) else 2.0)
         return add("v", lambda: g.vector.tensor_tensor(out[0], in0[0], in1[0], op), in0[1] + in1[1], out[1], vcost(out[2], f))
 
     def cp(out, in0):
@@ -93,12 +96,17 @@ def build(g, core, T, topo, ops):
         return add("v", lambda: g.vector.memset(out[0], val), [], out[1], vcost(out[2], 0.5 if two(out) else 1.0))
 
     def scan(out, in0):
-        return add("v", lambda: g.vector.tensor_tensor_scan(out[0], in0[0], in0[0], 0.0, ALU.add, ALU.max), in0[1], out[1], vcost(out[2], 0.5))
+        ones = A("one", 0, out[2])
+        return add("v", lambda: g.vector.tensor_tensor_scan(out[0], ones[0], in0[0], 0.0, ALU.mult, ALU.add),
+                   in0[1] + ones[1], out[1], vcost(out[2], 0.5))
 
     def act(out, in0, func, bias=0.0, scale=1.0):
         ab, rb = sc(bias); as_, rs = sc(scale)
         f = GA if in0[4] == "ind" else 1.0
         return add("s", lambda: g.scalar.activation(out[0], in0[0], func, bias=ab, scale=as_), in0[1] + rb + rs, out[1], vcost(out[2], f))
+
+    def move(e, out, in0, plus=0.0):
+        return ts(out, in0, plus, ALU.add) if e == "v" else act(out, in0, ACT.Identity, bias=plus)
 
     def mm(items):
         def fn():
@@ -108,8 +116,15 @@ def build(g, core, T, topo, ops):
             return ins
         rd, wr, dur = [], [], FIX
         for o, l, r, st, sp in items:
-            rd += l[1] + r[1]; wr += o[1]; dur += PCY * max(min(64, l[2]), r[2])
+            rd += l[1] + r[1]; wr += o[1]; dur += PCY * max(min(64, l[2]), r[2]) * (4 if r[3] == "float32" else 1)
         return add("p", fn, sorted(set(rd)), sorted(set(wr)), dur)
+
+    def acc(out, terms, start=True, stop=True):
+        items = []
+        for n, t in enumerate(terms):
+            l, r = (A("mg", 128 * t, 128 * t + 128, p1=1), A("one", 0, out[2], p1=1)) if isinstance(t, int) else (A(t[0]), t[1])
+            items.append((out, l, r, start and n == 0, stop and n == len(terms) - 1))
+        return items
 
     def iota(out, pattern, base, cm):
         if out[3] == "int32":
@@ -137,21 +152,16 @@ def build(g, core, T, topo, ops):
     def CB(k):
         return A("colb", k, k + 1)
 
-    def DL(t):
-        return PS(6, 96, 96 + LC) if t % 2 else PS(7, 160, 160 + LC)
+    def Q(name, t, n=1):
+        return A(name, t * LC, (t + n) * LC)
 
-    def Q(name, t):
-        return A(name, t * LC, (t + 1) * LC)
-
-    nch = len(CH)
-    c0s = [sum(CH[:k]) for k in range(nch + 1)]
-    tw0 = [3 * 16 * c0s[k] + 16 * k for k in range(nch)]
     xb = ["xb0", "xb1"]
+    shift = [2.0 if PLAN["D"][k] == "v" and PLAN["C"][k] == "v" else 0.0 for k in range(NCH)]
 
     late[0] = 0
-    dma("s", T.zz[0:8, :], T.c0[:, :], [], reg("zz", 0, V), 60e3)
-    dma("s", T.zz[8:16, :], T.x[15::16, :], [], [("zz2", 0, 1)], 60e3)
-    cuts = [0, 8 * CH[0]] + [16 * c for c in c0s[1:]]
+    dma("s", T.zc[0:8, :], T.c0[:, :], [], reg("zc", 0, V), 60e3)
+    dma("s", T.zl[0:8, :], T.x[15::16, :], [], reg("zl", 0, V), 60e3)
+    cuts = [0, W // 2] + [W * k for k in range(1, NCH + 1)]
     for a, b in zip(cuts, cuts[1:]):
         dma("y", T.nbt[:, a:b], T.nb[:, a:b], [], reg("nbt", a, b), 512 * b)
     dma("y", T.xb0[:, GH:GH + H], T.gx[:, :], [], reg("xb0", GH, GH + H), 2.2e6)
@@ -162,90 +172,103 @@ def build(g, core, T, topo, ops):
     iota(A("pi", 0, 1), [[0, 1]], 0, 1)
     ts(A("pi", 1, 2), A("pi", 0, 1), 15, ALU.bitwise_and)
     ts(A("pi", 2, 3), A("pi", 0, 1), 1, ALU.bitwise_and)
-    cols.update({"pm": 0, "lev": 1, "zw": 2, "zx": 3, "ys": 23, "we": 24, "wo": 25})
+    cols.update({"pm": 0, "lev": 1, "we": 2, "wo": 3, "pw": 4, "pn": 5, "kb": 6})
     cp(C("pm"), A("pi", 1, 2))
     ts(C("lev"), A("pi", 1, 2), 15.0, ALU.is_equal)
-    ts(C("zx"), A("pi", 0, 1), 8.0, ALU.is_ge, 16.0, ALU.mult)
-    ts(C("zw"), C("zx"), 1.0, ALU.max)
-    percol = {"xs": (1.25, 1.0), "xb": (-40.0, 128.0), "f1": (1.0, 0.0), "rb": (704.0, 64.0), "xn": (-40.0, -32.0),
-              "yb": (0.0, -160.0), "wv": (-BIG, -16 * BIG), "wi": (0.0, -2 * BIG), "wm": (0.0, 400 * BIG),
-              "w80": (-80.0, -64.0), "wn": (-39.5, -191.5), "wt": (40.0, 192.0)}
-    for k, nm in enumerate(percol):
-        cols[nm] = 4 + k
-        ts(C(nm), C("lev"), percol[nm][1] - percol[nm][0], ALU.mult, percol[nm][0], ALU.add)
-    ts(C("ys"), C("lev"), 0.8, ALU.max)
     ts(C("we"), A("pi", 2, 3), -0.25, ALU.mult, 0.25, ALU.add)
     ts(C("wo"), A("pi", 2, 3), 0.25, ALU.mult)
-    MAG = 1.5 * 2 ** 27
-    for k, (f, l) in enumerate([(MAG, 0.0), (0.0, 0.0), (-1.0, 0.0), (1.0, 0.0), (0.0, 1.0), (1.25, 1.0), (-40.0, 128.0)]):
-        if k == 1:
-            ts(CB(1), CB(0), C("lev"), ALU.subtract)
-        else:
-            ts(CB(k), C("lev"), l - f, ALU.mult, f, ALU.add)
+    ts(C("pw"), A("pi", 1, 2), float(W), ALU.add)
+    ts(C("pn"), A("pi", 1, 2), -2048.0, ALU.add)
+    ts(C("kb"), A("pi", 1, 2), -1.0, ALU.mult, -8.0, ALU.add)
+    BIG, LO = 2.0 ** 14, 704.0
+    percol = {"f1": (1.0, 0.0), "wv": (-256.0, -7 * 256.0), "wi": (0.0, -BIG), "wm": (0.0, 200 * BIG)}
+    percol.update({"r%d" % s: (LO + s, 64.0 + s) for s in set(shift)})
+    looks = set(zip(PLAN["D"], PLAN["C"]))
+    if ("v", "s") in looks:
+        percol["f2"] = (-2.0, 0.0)
+    if ("s", "v") in looks:
+        percol["c1"] = (-1.0, 0.0)
+    for k, nm in enumerate(percol):
+        cols[nm] = 10 + k
+        ts(C(nm), C("lev"), percol[nm][1] - percol[nm][0], ALU.mult, percol[nm][0], ALU.add)
+    cp(CB(4), C("lev"))
+    if "v" in PLAN["D"]:
+        ts(CB(0), C("f1"), 2.0 ** 27, ALU.mult)
+        ts(CB(1), C("f1"), 2.0 ** 27, ALU.mult, 1.0, ALU.max)
+    if ("v", "v") in looks:
+        ts(CB(2), C("lev"), 1.0, ALU.add)
+        ts(CB(3), C("f1"), 2.0, ALU.add)
+    if "s" in PLAN["D"]:
+        cols.update({"a1": 7, "a2": 8})
+        ts(C("a1"), C("f1"), 1.5 * 2 ** 27, ALU.mult)
+        ts(C("a2"), C("f1"), 1.5 * 2 ** 27, ALU.mult, -1.25, ALU.add)
 
     ms(A("one"), 1.0)
     ms(A("b0"), 0.0)
     ms(A("bz"), 0.0)
-    asel(A("bt", 0, 16), A("one", 0, 16), [[-8, 2], [-1, 8]], ALU.is_equal, 0, 1)
-    tt(A("bt", 24, 32), A("bt", 0, 8), A("bt", 8, 16), ALU.add)
-    ts(A("bz", 15, 143, 16), A("bt", 24, 32), C("zw"), ALU.mult)
-    asel(A("bt", 16, 24), A("one", 0, 8), [[-16, 8]], ALU.is_ge, 0, 1)
-    asel(A("b0", 15, 143, 16), A("bt", 16, 24), [[16, 8]], ALU.is_ge, 15, -1)
+    asel(A("bz", 15, 143, 16), A("one", 0, 8), [[-1, 8]], ALU.is_equal, 0, 1)
+    asel(A("bt"), A("one", 0, 8), [[-16, 8]], ALU.is_ge, 0, 1)
+    asel(A("b0", 15, 143, 16), A("bt"), [[16, 8]], ALU.is_ge, 15, -1)
     asel(A("idn"), A("one", 0, 128), [[-1, 128]], ALU.is_equal, 0, 1)
     for nm, c in (("be", "we"), ("bo", "wo"), ("bv", "wv"), ("bi", "wi"), ("bm", "wm")):
         act(A(nm), A("b0"), ACT.Identity, scale=C(c))
-    act(A("idm"), A("idn"), ACT.Identity, scale=-1.0)
-    act(A("idb"), A("idn"), ACT.Identity, scale=BIG)
-    act(A("ids"), A("idn"), ACT.Identity, scale=C("xn"))
-    act(A("idv"), A("idn"), ACT.Identity, scale=C("w80"))
+    diag = {"idm": -1.0, "idb": BIG, "idw": -129.0 / 256, "idq": 2 * K8, "idk": -K8, "idc": -33.0 / 64, "idf": 1.0,
+            "id8": 8.0, "id9": -8.0625, "idz": 2.0 ** 29}
+    if "s" in PLAN["D"]:
+        diag.update({"idp": 1.25, "id5": -1.25})
+    for nm in diag:
+        act(A(nm), A("idn"), ACT.Identity, scale=diag[nm])
+    M64, M8K, M16 = 0, 2, 4
+    for k, val in enumerate((1.5 * 2 ** 29, -1.5 * 2 ** 29, 1.5 * 2 ** 36, -1.5 * 2 ** 36, 1.5 * 2 ** 27, -1.5 * 2 ** 27)):
+        ms(A("mg", 128 * k, 128 * k + 128, p1=32), val)
     iota(A("wi"), [[-1, 16]], 128, 1)
     ts(A("wi"), A("wi"), 15, ALU.bitwise_and)
     ts(A("wa", 0, 16), A("wi"), 1.5, ALU.is_le)
-    ts(A("wa", 16, 32), A("wi"), 3.5, ALU.is_le, 256.0, ALU.mult)
-    ts(A("wa", 32, 48), A("wi"), 1.5, ALU.is_ge)
+    ts(A("wa", 16, 32), A("wi"), 3.5, ALU.is_le, 255.0, ALU.mult)
+    ts(A("wa", 32, 48), A("wi"), 1.5, ALU.is_le, -254.0, ALU.mult)
     ts(A("wa", 48, 64), A("wi"), 4.0, ALU.is_equal, 65536.0, ALU.mult)
-    tt(A("wa", 16, 32), A("wa", 16, 32), A("wa", 32, 48), ALU.mult)
-    tt(A("wa", 0, 16), A("wa", 0, 16), A("wa", 48, 64), ALU.add)
-    tt(A("wtab"), A("wa", 0, 16), A("wa", 16, 32), ALU.add)
-    for k in range(nch):
-        iota(A("pos", c0s[k], c0s[k + 1]), [[16, CH[k]]], 16, 0)
-        ms(A("tw", tw0[k], tw0[k] + 16), 0.0)
+    tt(A("wa", 16, 32), A("wa", 16, 32), A("wa", 32, 48), ALU.add)
+    ts(A("wa", 0, 16), A("wa", 16, 32), 254.0, ALU.is_ge)
+    tt(A("wa", 16, 32), A("wa", 16, 32), A("wa", 0, 16), ALU.add)
+    tt(A("wtab"), A("wa", 16, 32), A("wa", 48, 64), ALU.add)
+    iota(A("posh"), [[0, NCH], [16, CW]], 16, 0)
+    for k in range(NCH):
+        ms(A("tw", k * TW, k * TW + 16), shift[k])
     iota(A("mpos"), [[16, SC]], 0, 0)
     asel(A("cu"), A("one"), [[-1, 16], [-16, 32]], ALU.is_equal, 0, 1)
-    ms(A("k72"), -207.0)
+    for d in range(N - 1):
+        ka, kb = A("ka", d * GC, (d + 1) * GC), A("kb", d * GC, (d + 1) * GC)
+        if PLAN["FB"][d] == "v":
+            ms(ka, -207.0); ms(kb, 0.0)
+        else:
+            iota(ka, [[-16, GC]], 0, 0)
+            act(kb, A("one", 0, GC), ACT.Identity, scale=C("kb"))
 
-    ZL = PS(7, 0, LC)
-    o = mm(listmm(ZL, "bz", "zz", 0, V, k=16))
-    ops[o]["r"] = ops[o]["r"] + [("zz2", 0, 1)]
-    cp(A("zi"), ZL)
-    ts(A("ci"), A("zi"), 15, ALU.bitwise_and)
-    cp(A("cu16"), A("ci"))
-    ts(A("nr"), A("zi"), 16.0, ALU.is_ge)
-    ts(A("bias"), A("nr"), 32.5, ALU.mult, -8.0, ALU.add)
-    ts(A("t1"), A("zi"), 63.0 * 16, ALU.is_ge, 16.0, ALU.mult)
-    ts(A("t4"), A("ci"), -1.0, ALU.mult, 15.0, ALU.add)
-    tt(A("z"), A("t1"), A("t4"), ALU.add)
-    ts(A("pos"), A("pos"), C("pm"), ALU.add)
-    tt(A("posc"), A("pos"), A("nr"), ALU.mult)
-    even = len(set(CH)) == 1
-    parts = [(0, LC, CH[0])] if even else [(c0s[k], c0s[k + 1], CH[k]) for k in range(nch)]
-    for la, lb, wc in parts:
-        ts(A("pf0", la, lb), A("pos", la, lb), 16.0 * wc, ALU.add)
+    ZC, ZL = PS(7, 0, LC), PS(7, LC, 2 * LC)
+    late[0] = 0
+    for hf in range(2):
+        la, lb = hf * LC // 2, (hf + 1) * LC // 2
+        mm(listmm(PS(7, la, lb), "bz", "zc", 16 * la, 16 * lb, k=8))
+        cp(A("cu16", la, lb), PS(7, la, lb))
+    late[0] = 1
+    act(A("c0b"), ZC, ACT.Identity)
+    mm(acc(PS(6, 0, LC), [("id9", A("c0b")), M16, M16 + 1, ("id8", A("c0b"))]))
+    act(A("par"), PS(6, 0, LC), ACT.Identity, bias=-1.0, scale=-0.25)
+    mm(listmm(ZL, "bz", "zl", 0, V, k=8))
+    act(A("nr"), ZL, ACT.Sign)
+    act(A("l63"), ZL, ACT.Relu, bias=-992.0, scale=16.0)
+    act(A("bias"), A("nr"), ACT.Identity, bias=11 * 256.0, scale=20.5 * 256)
+    act(A("pn"), A("nr"), ACT.Identity, bias=C("pn"), scale=2048.0)
 
-    def failpos():
-        for la, lb, wc in parts:
-            ts(A("t1", la, lb), A("z", la, lb), 0.0, ALU.is_equal, 16.0 * wc, ALU.mult)
-        tt(A("pf"), A("t1"), A("pf0"), ALU.add)
-    failpos()
+    def failpos(n, Z, P):
+        mm(acc(Z, [("idn", A("l63")), ("idm", A("c0b"))] + [("idm", Q("gg", j)) for j in range(n)]))
+        ts(A("arm"), Z, n / 2 - 15.0, ALU.is_equal, float(W), ALU.mult)
+        mm(acc(P, [("idn", A("posh")), ("idn", A("arm"))]))
+        act(A("pf"), P, ACT.Identity, bias=C("pw"))
+    failpos(0, ZC, ZL)
     ts(A("mpos"), A("mpos"), C("pm"), ALU.add)
     cp(A("sndu"), A("sndi"))
     ts(A("sndp"), A("sndi"), float(OWN), ALU.add)
-
-    def scale_in(e, lo, hi):
-        if e == "v":
-            ts(A("xb0", lo, hi), A("xb0", lo, hi), CB(5), ALU.mult, CB(6), ALU.add)
-        else:
-            act(A("xb0", lo, hi), A("xb0", lo, hi), ACT.Identity, bias=C("xb"), scale=C("xs"))
 
     peers = [c for c in T.cores if c != core]
     far = sorted(set(e for c in peers if topo.chip(c) != topo.chip(core) for e in topo.engines(core, c)))
@@ -272,234 +295,216 @@ def build(g, core, T, topo, ops):
                 reg(src, so, so + H) + [("sent", 0, 1)], [("sent", 0, 1)], REMOTE_US - 1.0, "send", ("loc%d" % n, tot))
         add("x", None, [], reg(dst, do, do + H), REMOTE_US, "arrive", ("arr%d" % n, tot, s))
 
-    scale_in(PLAN["XS"][0], GH, GH + H)
     late[0] = 0
     send(RO - 1, [((rank - d) % N, d - 1) for d in range(1, N)], "xb0", GH, "xb1", 0)
     late[0] = 1
-    scale_in(PLAN["XS"][1], OWN, OWN + V // 2)
-    scale_in(PLAN["XS"][2], OWN + V // 2, GH)
-    dma("y", T.x2[:, :], T.xb0[:, OWN:GH], reg("xb0", OWN, GH), reg("x2", 0, V), 1e6)
 
-    MAG2 = 1.5 * 2 ** 31
-    sub = 0
-    for k in range(nch):
-        w = 16 * CH[k]; n = w // 2
-        for hf in range(2):
-            a = 16 * c0s[k] + hf * n; b = a + n
-            HP, WP, RP = PS(sub % 2, 0, n), PS(2 + sub % 2, 0, n), PS(4, 0, n)
-            late[0] = 0
-            act(A("wsb", a, b), IND(A("wtab"), A("cu16", a // 16, b // 16)), ACT.Identity)
-            ts(HP, A("nbt", a, b), MAG2, ALU.add, MAG2, ALU.subtract)
-            tt(A("lr", a, b), A("nbt", a, b), HP, ALU.subtract)
-            tt(A("ph", a, b), HP, A("wsb", a, b), ALU.mult)
-            act(A("pb", a, b), A("lr", a, b), ACT.Identity, bias=702.5)
-            mm([(WP, A("idn"), A("wsb", a, b), True, True)])
-            tt(A("pl", a, b), WP, A("pb", a, b), ALU.mult)
-            late[0] = 1
-            mm([(RP, A("idn"), A("lr", a, b), True, False), (RP, A("idm"), A("pb", a, b), False, True)])
-            r0 = tw0[k] + 16 + w + hf * n
-            act(A("tw", r0, r0 + n), RP, ACT.Identity, bias=C("rb"), scale=C("f1"))
-            sub += 1
-        r0 = tw0[k] + 16 + w
-        if PLAN["R1"][k] == "v":
-            ts(A("tw", r0 + w, r0 + 2 * w), A("tw", r0, r0 + w), CB(4), ALU.add)
-        else:
-            act(A("tw", r0 + w, r0 + 2 * w), A("tw", r0, r0 + w), ACT.Identity, bias=C("lev"))
-        late[0] = 0
-        for bank, band in ((5, "be"), (6, "bo")):
-            for j, src in ((1, "ph"), (0, "pl")):
-                mm(listmm(PS(bank, j * LC + c0s[k], j * LC + c0s[k + 1]), band, src, 16 * c0s[k], 16 * c0s[k + 1]))
-    OL, OH = PS(6, 0, LC), PS(6, LC, 2 * LC)
-    act(A("ee"), PS(5, 0, 2 * LC), ACT.Identity)
-    tt(A("t5"), OL, Q("ee", 0), ALU.is_gt)
-    tt(Q("li", 0), OL, Q("ee", 0), ALU.max)
-    ts(A("t5"), A("t5"), 0.5, ALU.subtract, 2.0 ** 30, ALU.mult)
-    tt(Q("li", 1), OL, Q("ee", 0), ALU.min)
-    tt(OH, OH, A("t5"), ALU.add)
-    tt(Q("li", 2), OH, Q("ee", 1), ALU.max)
-    tt(Q("li", 3), OH, Q("ee", 1), ALU.min)
-    for t in range(RO):
-        for dst, base, mask in (("qlo", 0, 255), ("qhi", 2, 127 * 64)):
+    def shifted(e, k, src):
+        if PLAN["D"][k] == "v":
+            move(e, A("x2", k * W, (k + 1) * W), A(src, OWN + k * W, OWN + (k + 1) * W), -2.0)
+    for k in range(NCH):
+        shifted(PLAN["X20"][k], k, "xb0")
+
+    n = W // 2
+    for sub in range(2 * NCH):
+        k, hf = sub // 2, sub % 2
+        a, b = sub * n, (sub + 1) * n
+        HP, WP, RP = PS(sub % 2, 0, n), PS(2, 0, n), PS(3, 0, n)
+        r0 = k * TW + 16 + W + hf * n
+        act(A("wsb", a, b), IND(A("wtab"), A("cu16", a // 16, b // 16)), ACT.Identity)
+        ts(HP, A("nbt", a, b), 1.5 * 2 ** 31, ALU.add, 1.5 * 2 ** 31, ALU.subtract)
+        tt(A("lr", a, b), A("nbt", a, b), HP, ALU.subtract)
+        tt(A("ph", a, b), HP, A("wsb", a, b), ALU.mult)
+        act(A("pb", a, b), A("lr", a, b), ACT.Identity, bias=LO - 1.5)
+        mm(acc(WP, [("idn", A("wsb", a, b))]))
+        tt(A("pl", a, b), WP, A("pb", a, b), ALU.mult)
+        mm(acc(RP, [("idn", A("lr", a, b)), ("idm", A("pb", a, b))]))
+        act(A("tw", r0, r0 + n), RP, ACT.Identity, bias=C("r%d" % shift[k]), scale=C("f1"))
+        if not hf:
+            continue
+        r0 -= n
+        move(PLAN["R1"][k], A("tw", r0 + W, r0 + 2 * W), A("tw", r0, r0 + W), CB(4))
+        per = NCH // PLAN["DEC"]
+        h, m = k // per, per * CW
+        bank, la = 4 + h % 2, h * m
+
+        def sums(j):
+            return PS(bank, j * m, (j + 1) * m)
+        for j, (band, src) in enumerate((("be", "ph"), ("bo", "ph"), ("be", "pl"), ("bo", "pl"))):
+            out = PS(bank, j * m + (k % per) * CW, j * m + (k % per + 1) * CW) if m <= 128 else PS(4 + j % 2, j // 2 * m + k * CW, j // 2 * m + (k + 1) * CW)
+            mm(listmm(out, band, src, k * W, (k + 1) * W, stop=j != 1)
+               + (acc(out, [("idz", A("par", k * CW, (k + 1) * CW))], start=False) if j == 1 else []))
+        if k % per < per - 1:
+            continue
+        for j in range(2):
+            ee = A("ee", j * LC + la, j * LC + la + m)
+            act(ee, sums(2 * j) if m <= 128 else PS(4, j * m, (j + 1) * m), ACT.Identity)
+            for t in range(2):
+                tt(A("li", (2 * t + j) * LC + la, (2 * t + j) * LC + la + m), sums(2 * j + 1) if m <= 128 else PS(5, j * m, (j + 1) * m), ee,
+                   ALU.min if t else ALU.max)
+        for dst, j, mask in (("qhi", 0, 127 * 64), ("qlo", 1, 255)):
+            ts(A(dst, la, la + m), A("li", j * LC + la, j * LC + la + m), mask, ALU.bitwise_and)
+        tt(A("qq0", la, la + m), A("qlo", la, la + m), A("qhi", la, la + m), ALU.add)
+        ts(A("off", la, la + m), A("qq0", la, la + m), LO / 4, ALU.subtract)
+    for t in range(1, RO):
+        for dst, j, mask in (("qhi", 0, 127 * 64), ("qlo", 1, 255)):
             if t > 1:
-                ts(Q(dst, t), Q("li", base + t % 2), 8 * (t // 2), ALU.arith_shift_right, mask, ALU.bitwise_and)
+                ts(Q(dst, t), Q("li", 2 * (t % 2) + j), 8 * (t // 2), ALU.arith_shift_right, mask, ALU.bitwise_and)
             else:
-                ts(Q(dst, t), Q("li", base + t), mask, ALU.bitwise_and)
-        tt(Q("qq", t), Q("qlo", t), Q("qhi", t), ALU.add)
-        if t == 0:
-            ts(A("off"), Q("qq", 0), 176.0, ALU.subtract)
-            late[0] = 1
-        ts(Q("qq", t), Q("qq", t), 8192.0 * t - 176.0, ALU.add)
+                ts(Q(dst, t), Q("li", 2 * t + j), mask, ALU.bitwise_and)
+        tt(Q("qq0", t), Q("qlo", t), Q("qhi", t), ALU.add)
 
-    UB = 7 * 512 - c0s[2]
+    UB = 7 * 512 - 2 * CW
     slot = [0]
+    n = W // 2
 
-    def look(s, k, cur):
-        ca, cb = c0s[k], c0s[k + 1]
+    def pair(ns):
+        p = 1024 * slot[0] + 512 - n
+        slot[0] = (slot[0] + 1) % ns
+        return p
+
+    def look(s, k, cur, ns):
+        ca, cb = k * CW, (k + 1) * CW
         a, b = 16 * ca, 16 * cb
-        U, CC = A("ps", UB + ca, UB + cb), A("tw", tw0[k] + 16, tw0[k] + 16 + b - a)
-        if PLAN["D"][s][k] == "s":
-            n = min(512, b - a - 32)
-            pd = 1024 * slot[0] + 512 - n
-            slot[0] = (slot[0] + 1) % (2 if s == RO - 1 else 3)
-            D = A("ps", pd, pd + b - a)
+        U, CC = A("ps", UB + ca, UB + cb), A("tw", k * TW + 16, k * TW + 16 + W)
+        if PLAN["D"][k] == "s":
+            pd = pair(ns)
+            D = A("ps", pd, pd + W)
 
             def part(lo, hi):
                 act(A("dd", lo, hi), IND(A(cur, OWN, GH + H), A("off", lo // 16, hi // 16)), ACT.Identity)
-                o_ = A("ps", pd + lo - a, pd + hi - a)
-                mm([(o_, A("idm"), A(cur, OWN + lo, OWN + hi), True, False), (o_, A("idn"), A("dd", lo, hi), False, True)])
+                mm(acc(A("ps", pd + lo - a, pd + hi - a), [("id5", A(cur, OWN + lo, OWN + hi)), ("idp", A("dd", lo, hi))]))
+            near = lambda: ts(A("aa", a, b), D, C("a1"), ALU.add, C("a2"), ALU.is_equal)
+            step = lambda: (ts(CC, D, C("c1"), ALU.max, C("f1"), ALU.min) if PLAN["C"][k] == "v" else act(CC, D, ACT.Sign, scale=C("f1")))
         else:
-            n = (ca + cb) // 4 * 32 - a
             D = A("dd", a, b)
 
             def part(lo, hi):
                 tt(A("dd", lo, hi), IND(A(cur, OWN, GH + H), A("off", lo // 16, hi // 16)), A("x2", lo, hi), ALU.subtract)
-        return [lambda: part(a, a + n), lambda: part(a + n, b),
-                lambda: ts(A("aa", a, b), D, CB(0), ALU.add, CB(1), ALU.is_equal),
-                lambda: mm([(U, A("idb"), A("bias", ca, cb), True, False)] + listmm(U, "bv", "aa", a, b, start=False)),
-                lambda: (ts(CC, D, CB(2), ALU.max, CB(3), ALU.min) if PLAN["C"][s][k] == "v"
-                         else act(CC, D, ACT.Sign, scale=C("f1")))]
+            near = lambda: ts(A("aa", a, b), D, CB(0), ALU.add, CB(1), ALU.is_equal)
+            step = lambda: (ts(CC, D, CB(2), ALU.max, CB(3), ALU.min) if PLAN["C"][k] == "v"
+                            else act(CC, D, ACT.Sign, bias=C("f2"), scale=C("f1")))
+        votes = lambda: mm(acc(U, [("idn", A("bias", ca, cb))], stop=False) + listmm(U, "bv", "aa", a, b, start=False, stop=False)
+                           + acc(U, [M8K, M8K + 1, ("idn", A("posh", ca, cb)), ("idn", A("pn", ca, cb))], start=False))
+        return [lambda: part(a, a + n), lambda: part(a + n, b), near, votes, step]
 
     for s in range(RO):
         cur, new = xb[s % 2], xb[(s + 1) % 2]
         last = s == RO - 1
-        late[0] = 0
+        first[0] = 0 if last else len(ops)
         ns = 2 if last else 3
         slot[0] = 0 if last else slot[0]
-        for k in range(nch):
-            ca, cb = c0s[k], c0s[k + 1]
-            a, b = 16 * ca, 16 * cb; w = b - a
+        for k in range(NCH):
+            ca, cb = k * CW, (k + 1) * CW
+            a, b = 16 * ca, 16 * cb
             eT, eW, eX = PLAN["T"][s][k], PLAN["W"][s][k], PLAN["X"][s][k]
-            U = A("ps", UB + ca, UB + cb)
             if k == 0:
-                for f in look(s, 0, cur):
+                for f in look(s, 0, cur, ns):
                     f()
-            nxt = look(s, k + 1, cur) if k + 1 < nch else [None] * 5
-            picks = [lambda: tt(A("t2", ca, cb), U, A("posc", ca, cb), ALU.max),
-                     lambda: tt(A("t3", ca, cb), A("t2", ca, cb), A("pf", ca, cb), ALU.min),
+            nxt = look(s, k + 1, cur, ns) if k + 1 < NCH else [None] * 5
+            picks = [lambda: tt(A("t3", ca, cb), A("ps", UB + ca, UB + cb), A("pf", ca, cb), ALU.min),
                      lambda: cp(A("sel", ca, cb), A("t3", ca, cb))]
-            both = [nxt[0], picks[0], nxt[1], picks[1], nxt[2], picks[2], nxt[3], nxt[4]]
+            both = [nxt[0], picks[0], nxt[1], picks[1], nxt[2], nxt[3], nxt[4]]
             if PLAN["SP"] == 0 or (PLAN["SP"] == 2 and k == 0):
                 both = picks
             for f in both:
                 if f:
                     f()
-            n = min(512, w - 32)
-            pb_ = 1024 * slot[0] + 512 - n
-            P1 = [A("ps", pb_, pb_ + n), A("ps", pb_ + n, pb_ + w)]
-            pb_ = 1024 * ((slot[0] + 1) % ns) + 512 - n
-            slot[0] = (slot[0] + 2) % ns
-            P = [A("ps", pb_, pb_ + n), A("ps", pb_ + n, pb_ + w)]
-            vw = [eW == "v" or (eW == "h" and hf == 0) for hf in range(2)]
-            vx = [eX == "v" or (eX == "h" and hf == 0) for hf in range(2)]
-            alone = [vw[hf] and vx[hf] and not last for hf in range(2)]
-            win = A("tw", tw0[k], tw0[k] + 16 + 3 * w)
-            hv = [(a, a + n), (a + n, b)]
-            for hf, (lo, hi) in enumerate(hv):
-                src = IND(win, A("sel", lo // 16, hi // 16))
-                if eT == "v" or (eT == "h" and hf == 0):
-                    ts(A("tt", lo, hi), src, CB(5), ALU.mult)
-                else:
-                    act(A("tt", lo, hi), src, ACT.Identity, scale=C("xs"))
-                late[0] = PLAN["LT"]
-                mm([(P1[hf], A("idn"), A(cur, OWN + lo, OWN + hi), True, False)])
-                mm([(P1[hf], A("idn"), A("tt", lo, hi), False, True)])
+            pb_ = pair(ns)
+            win = A("tw", k * TW, (k + 1) * TW)
+            for hf, (lo, hi) in enumerate([(a, a + n), (a + n, b)]):
+                P = A("ps", pb_ + lo - a, pb_ + hi - a)
+                src, own, t_ = IND(win, A("sel", lo // 16, hi // 16)), A(cur, OWN + lo, OWN + hi), A("tt", lo, hi)
+                out = A(new, OWN + lo, OWN + hi)
+                xv = eX == "v" or (eX == "h" and hf == 0)
                 late[0] = 0
-            late[0] = PLAN["LT"]
-            for hf, (lo, hi) in enumerate(hv):
-                if not alone[hf]:
-                    mm([(P[hf], A("idn"), A(cur, OWN + lo, OWN + hi), True, False), (P[hf], A("idn"), A("tt", lo, hi), False, False)])
-            for hf, (lo, hi) in enumerate(hv):
-                if alone[hf]:
-                    ts(A("sg", lo, hi), P1[hf], C("wt"), ALU.is_ge, C("w80"), ALU.mult)
-                    tt(A(new, OWN + lo, OWN + hi), P1[hf], A("sg", lo, hi), ALU.add)
-                    continue
-                if vw[hf]:
-                    ts(A("sg", lo, hi), P1[hf], C("wt"), ALU.is_ge, 0.5, ALU.subtract)
+                if eT == "v" or (eT == "h" and hf == 0):
+                    tt(t_, src, A("x2", lo, hi) if shift[k] else own, ALU.add)
+                    late[0] = PLAN["LT"]
+                    if eW == "m":
+                        ts(A("sg", lo, hi), t_, 64.0, ALU.is_ge, -64.0, ALU.mult)
+                        mm(acc(P, [("idn", A("sg", lo, hi))] + ([] if xv else [("idn", t_)])))
+                    else:
+                        mm(acc(P, [("idw", t_), M64, M64 + 1] + ([] if xv else [("idn", t_)])))
+                    if xv:
+                        tt(out, P, t_, ALU.add)
+                    else:
+                        act(out, P, ACT.Identity)
                 else:
-                    act(A("sg", lo, hi), P1[hf], ACT.Sign, bias=C("wn"))
-                mm([(P[hf], A("idv" if vw[hf] else "ids"), A("sg", lo, hi), False, True)])
-            for hf, (lo, hi) in enumerate(hv):
-                if alone[hf]:
-                    continue
-                if last and vx[hf]:
-                    ts(A("yy", lo, hi), P[hf], C("ys"), ALU.mult, C("yb"), ALU.add)
-                elif last:
-                    act(A("yy", lo, hi), P[hf], ACT.Identity, bias=C("yb"), scale=C("ys"))
-                elif vx[hf]:
-                    ts(A(new, OWN + lo, OWN + hi), P[hf], C("xn"), ALU.add)
-                else:
-                    act(A(new, OWN + lo, OWN + hi), P[hf], ACT.Identity, bias=C("xn"))
+                    act(t_, src, ACT.Identity, bias=-shift[k])
+                    late[0] = PLAN["LT"]
+                    mm(acc(P, [("idw", own)], stop=False))
+                    mm(acc(P, [("idw", t_), M64, M64 + 1, ("idn", t_)] + ([] if xv else [("idn", own)]), start=False))
+                    if xv:
+                        tt(out, P, own, ALU.add)
+                    else:
+                        act(out, P, ACT.Identity)
             late[0] = 0
             if both is picks and nxt[0]:
                 for f in nxt:
                     f()
             if last:
-                dma("y", T.yx[:, a:b], T.yy[:, a:b], reg("yy", a, b), [], 256 * w)
-                if k >= nch - 2:
-                    k0 = 0 if k < nch - 1 else k
-                    la, lb = c0s[k0], cb
-                    ts(A("ff", la, lb), A("ps", UB + la, UB + lb), 0.0, ALU.is_gt)
-                    tt(A("z", la, lb), A("z", la, lb), A("ff", la, lb), ALU.subtract)
-                    ts(A("zi", la, lb), A("z", la, lb), -1.0, ALU.mult, 31.0, ALU.add)
-                    ts(A("ci", la, lb), A("zi", la, lb), 15, ALU.bitwise_and)
-                    cp(A("curb", la, lb), A("ci", la, lb))
+                dma("y", T.yx[:, a:b], T[new][:, OWN + a:OWN + b], reg(new, OWN + a, OWN + b), [], 256 * W)
+                if k >= NCH - 2:
+                    k0 = 0 if k < NCH - 1 else k
+                    la, lb = k0 * CW, cb
+                    gl, cl, Z = A("gg", s * LC + la, s * LC + lb), A("cb4", la, lb), PS(6, la, lb)
+                    ts(gl, A("ps", UB + la, UB + lb), K8 / 2, ALU.is_ge, 0.5, ALU.subtract)
+                    mm(acc(Z, [("idc", cl), ("idc", gl), M16, M16 + 1, ("idn", cl), ("idn", gl)]))
+                    cp(A("curb", la, lb), Z)
                     for j in range(k0, k + 1):
-                        h2 = CH[j] // 2
                         for hf in range(2):
-                            mm([(A("ps", (4 + hf) * 512 + i, (4 + hf) * 512 + 16 * h2, 16, 32 * j, 32 * j + 32),
-                                 A("cu", 32 * i, 32 * i + 32), A("curb", c0s[j] + hf * h2, c0s[j] + (hf + 1) * h2), True, True)
-                                for i in range(16)])
+                            mm([(A("ps", (4 + hf) * 512 + i, (4 + hf) * 512 + n, 16, 32 * j, 32 * j + 32), A("cu", 32 * i, 32 * i + 32),
+                                 A("curb", j * CW + hf * CW // 2, j * CW + (hf + 1) * CW // 2), True, True) for i in range(16)])
                     mark = [("ycs%d" % k0, 0, 1)]
-                    runs = [(k0, k + 1)] if len(set(CH[k0:k + 1])) == 1 else [(j, j + 1) for j in range(k0, k + 1)]
-                    for j0, j1 in runs:
-                        h2 = 8 * CH[j0]
-                        for hf in range(2):
-                            o_ = A("ycs", hf * h2, (hf + 1) * h2, 1, 32 * j0, 32 * j1)
-                            cp((o_[0], mark) + o_[2:], A("ps", (4 + hf) * 512, (4 + hf) * 512 + h2, 1, 32 * j0, 32 * j1))
+                    for hf in range(2):
+                        o_ = A("ycs", hf * n, (hf + 1) * n, 1, 32 * k0, 32 * k + 32)
+                        cp((o_[0], mark) + o_[2:], A("ps", (4 + hf) * 512, (4 + hf) * 512 + n, 1, 32 * k0, 32 * k + 32))
                     for j in range(k0, k + 1):
-                        dma("y", T.yc[:, 16 * c0s[j]:16 * c0s[j + 1]], T.ycs[32 * j:32 * j + 8, 0:16 * CH[j]], mark, [], 30e3)
+                        dma("y", T.yc[:, j * W:(j + 1) * W], T.ycs[32 * j:32 * j + 8, 0:W], mark, [], 30e3)
         if last:
             break
         for d in range(N - 1):
-            src = IND(A("tt"), A("sndu", d * G // 16, (d + 1) * G // 16))
+            src = IND(A("tt"), A("sndu", d * GC, (d + 1) * GC))
             if PLAN["FB"][d] == "v":
-                ts(A("mb", d * G, (d + 1) * G), src, 0.1, ALU.is_gt)
+                ts(A("mb", d * G, (d + 1) * G), src, 63.5, ALU.is_ge, 2.0, ALU.mult)
             else:
-                act(A("mb", d * G, (d + 1) * G), src, ACT.Sign)
+                act(A("mb", d * G, (d + 1) * G), src, ACT.Sign, bias=-63.5)
         U2 = PS(6, 0, SC)
-        mm([(U2, A("idb"), A("k72"), True, False)] + listmm(U2, "bm", "mb", 0, H, start=False, stop=False))
+        mm(acc(U2, [("idb", A("ka")), ("idb", A("kb"))], stop=False) + listmm(U2, "bm", "mb", 0, H, start=False, stop=False))
         for d in range(N - 1):
             scan(A("inc", d * G, (d + 1) * G), A("mb", d * G, (d + 1) * G))
         mm(listmm(U2, "bi", "inc", 0, H, start=False))
-        tt(A("s1"), U2, A("mpos"), ALU.max)
-        tt(A("s2"), A("s1"), A("sndp"), ALU.min)
+        tt(U2, U2, A("mpos"), ALU.max)
+        tt(A("s2"), U2, A("sndp"), ALU.min)
         cp(A("soff"), A("s2"))
         hs = PLAN["GS"]
         cp(A(cur, 0, 16 * hs), IND(A(new, 0, GH), A("soff", 0, hs)))
         act(A(cur, 16 * hs, H), IND(A(new, 0, GH), A("soff", hs, SC)), ACT.Identity)
         send(s, [((rank + d) % N, d - 1) for d in range(1, N)], cur, 0, new, GH)
         late[0] = 1
-        for k in range(nch):
-            a, b = 16 * c0s[k], 16 * c0s[k + 1]
-            if PLAN["D"][s + 1][k] == "s":
-                continue
-            if PLAN["X2"][k] == "v":
-                cp(A("x2", a, b), A(new, OWN + a, OWN + b))
-            elif PLAN["X2"][k] == "s":
-                act(A("x2", a, b), A(new, OWN + a, OWN + b), ACT.Identity)
-            else:
-                dma("y", T.x2[:, a:b], T[new][:, OWN + a:OWN + b], reg(new, OWN + a, OWN + b), reg("x2", a, b), 256 * (b - a))
-        ts(A("ff"), A("ps", UB, UB + LC), 0.0, ALU.is_gt)
-        for t in range(RO - 1 - s):
-            tt(DL(t), A("ps", UB, UB + LC), Q("qq", t), ALU.max)
-            tt(A("zi") if s == RO - 2 else Q("qq", t), DL(t), Q("qq", t + 1), ALU.min)
-            if t == 0:
-                if s < RO - 2:
-                    cp(A("zi"), Q("qq", 0))
-                ts(A("ci"), A("zi"), 8191, ALU.bitwise_and)
-                cp(A("off"), A("ci"))
-        tt(A("z"), A("z"), A("ff"), ALU.subtract)
-        failpos()
+        for k in range(NCH):
+            shifted(PLAN["X2"][k], k, new)
+        ts(Q("gg", s), A("ps", UB, UB + LC), K8 / 2, ALU.is_ge, 0.5, ALU.subtract)
+        first[0] = 0
+        q0, q1, left = "qq%d" % (s % 2), "qq%d" % ((s + 1) % 2), RO - 1 - s
+        p0, p1 = 1024 * slot[0], 1024 * ((slot[0] + 1) % 3)
+        for t0, t1 in ((0, 1), (1, left)):
+            for t in range(t0, t1):
+                cut = [t * LC] + ([512] if t * LC < 512 < (t + 1) * LC else []) + [(t + 1) * LC]
+                for lo, hi in zip(cut, cut[1:]):
+                    mm(acc(A("ps", p0 + lo, p0 + hi), [("idf", A(q0, lo, hi)), ("idq", A("gg", (s - t) * LC + lo, (s - t) * LC + hi))]))
+            if t1 > t0:
+                tt(Q(q1, t0, t1 - t0), A("ps", p0 + t0 * LC, p0 + t1 * LC), Q(q0, t0 + 1, t1 - t0), ALU.min)
+            if t0 == 0:
+                OF = A("ps", p1, p1 + LC)
+                mm(acc(OF, [("idf", Q(q1, 0))] + [("idk", Q("gg", j)) for j in range(s + 1)]))
+                ts(A("off"), OF, K8 * (s + 1) / 2 - LO / 4, ALU.add)
+        failpos(s + 1, A("ps", p1 + 512, p1 + 512 + LC), A("ps", p1 + 512 + LC, p1 + 512 + 2 * LC))
+        if s == RO - 2:
+            Z = A("ps", p1 + LC, p1 + 2 * LC)
+            mm(acc(Z, [("idn", A("c0b"))] + [("idn", Q("gg", j)) for j in range(s + 1)]))
+            act(A("cb4"), Z, ACT.Identity, bias=RO / 2)
 
 
 def depend(ops):
@@ -522,60 +527,73 @@ def depend(ops):
         o["d"] = deps
 
 
-def order(ops, shift=None):
+def order(ops, prio):
     n = len(ops)
-    pred = [set(o["d"]) | ({o["x"][2]} if o["kind"] == "arrive" else set()) for o in ops]
-    succ = [[] for _ in ops]
+    left = [len(o["p"]) for o in ops]
+    ready = {}
     for i in range(n):
-        for j in pred[i]:
-            succ[j].append(i)
-    prio = [0.0] * n
-    for i in range(n - 1, -1, -1):
-        prio[i] = min([prio[j] for j in succ[i]] + [2.0 * n]) - 1e-3 if ops[i]["late"] else float(i)
-    if shift:
-        prio = [p + d for p, d in zip(prio, shift)]
-    left = [len(p) for p in pred]
-    ready = sorted((prio[i], i) for i in range(n) if not left[i])
-    free, fin, beg, can, out = {}, [0.0] * n, [0.0] * n, [0.0] * n, []
-    while ready:
-        pick = {}
-        for _, k in ready:
-            q = ops[k]["q"]
-            st = max(can[k], free.get(q, 0.0))
-            if q not in pick:
-                pick[q] = [st, k, st + PLAN["TOL"], False]
-            elif not pick[q][3] and st + ops[k]["dur"] <= pick[q][2]:
-                pick[q] = [st, k, 0.0, True]
-        st, i = min(p[:2] for p in pick.values())
+        if not left[i]:
+            ready.setdefault(ops[i]["q"], []).append(i)
+    free, fin, can, out, tol = {}, [0.0] * n, [0.0] * n, [], PLAN["TOL"]
+    while len(out) < n:
+        st, i = 1e9, -1
+        for q in ready:
+            if ready[q]:
+                f = free.get(q, 0.0)
+                k = min(ready[q], key=prio.get)
+                t = max(can[k], f)
+                if t > f:
+                    fit = [j for j in ready[q] if max(can[j], f) + ops[j]["hold"] <= t + tol]
+                    if fit:
+                        k = min(fit, key=prio.get)
+                        t = max(can[k], f)
+                if t < st:
+                    st, i = t, k
         o = ops[i]
-        ready.remove((prio[i], i))
-        beg[i] = st; fin[i] = st + o["dur"]
-        if o["q"] != "x":
-            free[o["q"]] = st + (0.1 if o["kind"] == "dma" else 1.0 if o["kind"] == "send" else o["dur"])
+        ready[o["q"]].remove(i)
+        fin[i] = st + o["dur"]
+        free[o["q"]] = st + o["hold"]
         out.append(i)
-        for j in succ[i]:
-            chain = o["q"] == "p" and ops[j]["q"] == "p"
-            can[j] = max(can[j], st if ops[j]["kind"] == "arrive" else fin[i] + (0.0 if chain else LAT))
+        for j, lat in o["s"]:
+            can[j] = max(can[j], st + lat)
             left[j] -= 1
             if not left[j]:
-                ready.append((prio[j], j)); ready.sort()
-    return out, beg, fin
+                ready.setdefault(ops[j]["q"], []).append(j)
+    return out, fin
 
 
 def best_order(ops):
+    n = len(ops)
+    like = {}
+    for i, o in enumerate(ops):
+        o["p"], o["s"] = set(o["d"]) | ({o["x"][2]} if o["kind"] == "arrive" else set()), []
+        o["hold"] = {"dma": 0.1, "send": 1.0, "arrive": 0.0}.get(o["kind"], o["dur"])
+        like.setdefault(o["tag"], []).append(i)
+    for j, o in enumerate(ops):
+        for i in o["p"]:
+            chain = o["q"] == "p" and ops[i]["q"] == "p"
+            ops[i]["s"].append((j, 0.0 if o["kind"] == "arrive" else ops[i]["dur"] + (0.0 if chain else LAT)))
     if not ORDER:
-        n, x = len(ops), 12345
-        shift = [0.0] * n
-        best = max(order(ops)[2])
+        prio = {}
+        for i in range(n - 1, -1, -1):
+            prio[i] = min([prio[j] - lat for j, lat in ops[i]["s"]] + [-ops[i]["dur"]])
+        marks = [i for i, o in enumerate(ops) if o["kind"] != "c"]
+
+        def cost(z):
+            fin = order(ops, z)[1]
+            return max(fin) + 0.02 * sum(fin[i] for i in marks) + 1e-4 * sum(fin)
+        best, x = cost(prio), PLAN["SEED"]
         for _ in range(PLAN["TRY"]):
-            z = list(shift)
+            z = dict(prio)
             for _ in range(2):
                 x = (x * 1103515245 + 12345) % 2 ** 31
-                z[(x >> 8) % n] += (-40, -20, -10, -5, 5, 10, 20, 40)[(x >> 4) % 8]
-            e = max(order(ops, z)[2])
+                i = (x >> 8) % n
+                for j in (like[ops[i]["tag"]] if (x >> 7) % 2 else [i]):
+                    z[j] += (-4, -2, -1, -0.5, 0.5, 1, 2, 4)[(x >> 4) % 8]
+            e = cost(z)
             if e <= best:
-                best, shift = e, z
-        ORDER.append(shift)
+                best, prio = e, z
+        ORDER.append(prio)
     return order(ops, ORDER[0])
 
 

@@ -15,34 +15,37 @@ def _sb(cols, dtype):
     return ("sbuf", [128, cols], dtype)
 
 
+DIAG = {"idm": -1.0, "idb": 2 * K8, "idw": -129.0 / 256, "idq": K8, "idk": -K8 / 2, "idc": -33.0 / 64, "idd": -33.0 / 128,
+        "idh": 0.5, "idg": -0.5, "id8": 8.0, "id9": -8.0625, "idz": 2.0 ** 29, "idp": 1.25, "id5": -1.25, "ids": -32.0}
 SCRATCH = {"xb0": _sb(V + 2 * H, "bfloat16"), "xb1": _sb(V + 2 * H, "bfloat16"), "nbt": _sb(V, "int32"),
            "tw": _sb(NCH * TW, "bfloat16"), "mb": _sb(H, "bfloat16"), "inc": _sb(H, "bfloat16"), "ycs": _sb(1024, "float32"),
            "pi": _sb(8, "int32"), "col": _sb(32, "float32"), "colb": _sb(16, "bfloat16"), "one": _sb(512, "bfloat16"),
-           "bt": _sb(8, "bfloat16"), "cu": _sb(512, "bfloat16"), "wi": _sb(16, "int32"), "wa": _sb(80, "float32"),
-           "wtab": _sb(16, "bfloat16"), "ee": _sb(2 * LC, "float32"), "li": _sb(4 * LC, "int32"), "mg": _sb(7 * 128, "bfloat16"),
+           "bt": _sb(8, "bfloat16"), "cu": _sb(512, "bfloat16"), "wi": _sb(16, "int32"), "wa": _sb(48, "float32"),
+           "wtab": _sb(16, "bfloat16"), "ee": _sb(2 * LC, "float32"), "li": _sb(4 * LC, "int32"), "mg": _sb(8 * 128, "bfloat16"),
+           "run": _sb(G, "bfloat16"),
            "qlo": _sb(5 * LC, "int32"), "qhi": _sb(5 * LC, "int32"), "qq0": _sb(5 * LC, "float32"), "qq1": _sb(4 * LC, "float32"),
            "gg": _sb(5 * LC, "bfloat16"), "sndi": _sb(SC, "int32"), "sndu": _sb(SC, "uint16"), "soff": _sb(SC, "uint16"),
-           "idf": _sb(128, "float32"), "ps": ("psum", [128, 4096], "float32")}
-SCRATCH.update({n: _sb(V, "bfloat16") for n in ("zc", "zl", "wsb", "hb", "lr", "pb", "ph", "pl", "dd", "aa", "tt", "sg", "x2")})
+           "lv": _sb(2 * W, "bfloat16"), "idn": _sb(128, "bfloat16"), "idf": _sb(128, "float32"),
+           "ps": ("psum", [128, 4096], "float32")}
+SCRATCH.update({n: _sb(V, "bfloat16") for n in ("zc", "zl", "wsb", "lr", "pb", "ph", "pl", "dd", "aa", "tt", "sg", "x2")})
 SCRATCH.update({n: _sb(144, "bfloat16") for n in ("b0", "bv", "be", "bo", "bz", "bi", "bm")})
-SCRATCH.update({n: _sb(128, "bfloat16") for n in ("idn", "idm", "idb", "idw", "idp", "idq", "idk", "idc", "id5", "id8", "id9", "idz")})
+SCRATCH.update({n: _sb(128, "bfloat16") for n in DIAG})
 SCRATCH.update({n: _sb(LC, "float32") for n in ("t3", "pf")})
 SCRATCH.update({n: _sb(LC, "uint16") for n in ("cu16", "off", "sel")})
 SCRATCH.update({n: _sb(LC, "bfloat16") for n in ("bias", "curb", "nr", "pn", "posh", "c0b", "l63", "arm", "cb4", "par")})
 SCRATCH.update({n: _sb(SC, "float32") for n in ("sndp", "mpos", "s2")})
 SCRATCH.update({n: _sb(SC, "bfloat16") for n in ("ka", "kb")})
-SEMAPHORES = (["qv", "qs", "qp", "qg"] + ["d%d" % k for k in range(40)]
-              + ["arr%d" % k for k in range(RO)] + ["loc%d" % k for k in range(RO)])
+SEMAPHORES = (["qv", "qs", "qp", "qg"] + ["d%d" % k for k in range(48)]
+              + ["arr%d" % k for k in range(2 * RO)] + ["loc%d" % k for k in range(2 * RO)])
 
-PLAN = {"D": "svsv", "C": "ssss", "T": ["svvh"] * 5, "W": ["mmmm"] * 5, "X": ["ssss"] * 5, "X2": "ssss",
-        "DEC": 1, "R1": "ssss", "X20": "ssss", "FB": "svs", "GS": 36, "TOL": 0.1, "SP": 1, "LT": 1, "TRY": 6000, "SEED": 12345}
-CY, PCY, FIX, LAT, GA, REMOTE_US = 1.0e-3, 0.5e-3, 0.06, 0.10, 1.5, 4.5
+PLAN = {"D": "svsv", "C": "ssss", "T": ["svvh"] * 5, "W": ["vvsv"] * 5, "X": ["svss"] * 5, "X2": "ssss", "PK": 2, "VK": 1, "QP": "ppp",
+        "DEC": 1, "YC": "sss", "R1": "dddd", "X20": "ssss", "FB": "svh", "SPLIT": 1, "GS": [24, 12], "TRY": 10000, "SHAKE": 8, "NEAR": 20, "FAST": 1, "HEAT": 0.0, "SEED": 12345}
+CY, PCY, FIX, LAT, GA, FAR_US, NEAR_US = 1.0e-3, 0.5e-3, 0.06, 0.10, 1.5, 4.5, 3.5
 ORDER = []
 
 
 def build(g, core, T, topo, ops):
     rank = T.rank_of(core)
-    late = [1]
     first = [0]
 
     def reg(name, lo, hi):
@@ -96,7 +99,7 @@ def build(g, core, T, topo, ops):
         return add("v", lambda: g.vector.memset(out[0], val), [], out[1], vcost(out[2], 0.5 if two(out) else 1.0))
 
     def scan(out, in0):
-        ones = A("one", 0, out[2])
+        ones = A("run")
         return add("v", lambda: g.vector.tensor_tensor_scan(out[0], ones[0], in0[0], 0.0, ALU.mult, ALU.add),
                    in0[1] + ones[1], out[1], vcost(out[2], 0.5))
 
@@ -119,9 +122,16 @@ def build(g, core, T, topo, ops):
             rd += l[1] + r[1]; wr += o[1]; dur += PCY * max(min(64, l[2]), r[2]) * (4 if r[3] == "float32" else 1)
         return add("p", fn, sorted(set(rd)), sorted(set(wr)), dur)
 
+    made = set()
+
     def acc(out, terms, start=True, stop=True):
         items = []
         for n, t in enumerate(terms):
+            if not isinstance(t, int) and t[0] in DIAG and t[0] not in made:
+                made.add(t[0])
+                keep, first[0] = first[0], 0
+                act(A(t[0]), A("idn"), ACT.Identity, scale=DIAG[t[0]])
+                first[0] = keep + 1 if keep else 0
             l, r = (A("mg", 128 * t, 128 * t + 128, p1=1), A("one", 0, out[2], p1=1)) if isinstance(t, int) else (A(t[0]), t[1])
             items.append((out, l, r, start and n == 0, stop and n == len(terms) - 1))
         return items
@@ -132,6 +142,9 @@ def build(g, core, T, topo, ops):
         else:
             fn = lambda: g.iota(out[0], pattern, base, cm, allow_small_or_imprecise_dtypes=True)
         return add("g", fn, [], out[1], 0.13 + 2 * CY * out[2])
+
+    def fill(out, val):
+        return iota(out, [[0, out[2]]], int(val), 0)
 
     def asel(out, in0, pattern, cmp_, base, cm):
         return add("g", lambda: g.affine_select(out[0], in0[0], pattern, cmp_, 0.0, base, cm), in0[1], out[1], 0.17 + 2 * CY * out[2])
@@ -158,16 +171,24 @@ def build(g, core, T, topo, ops):
     xb = ["xb0", "xb1"]
     shift = [2.0 if PLAN["D"][k] == "v" and PLAN["C"][k] == "v" else 0.0 for k in range(NCH)]
 
-    late[0] = 0
-    dma("s", T.zc[0:8, :], T.c0[:, :], [], reg("zc", 0, V), 60e3)
-    dma("s", T.zl[0:8, :], T.x[15::16, :], [], reg("zl", 0, V), 60e3)
+    def leaves(r, d):
+        return topo.chip(T.cores[r]) != topo.chip(T.cores[(r + d) % N])
+
+    def blocks(r):
+        return sorted(range(N - 1), key=lambda b: not leaves(r, b + 1))
+    nfar = sum(leaves(rank, d) for d in range(1, N))
+    sends = [(0, nfar), (nfar, N - 1)] if PLAN["SPLIT"] else [(0, N - 1)]
+
+    dma("s", T.zc[0:8, :], T.c0[:, :], [], reg("zc", 0, V), 20e3)
+    dma("s", T.zl[0:8, :], T.x[15::16, :], [], reg("zl", 0, V), 20e3)
     cuts = [0, W // 2] + [W * k for k in range(1, NCH + 1)]
-    for a, b in zip(cuts, cuts[1:]):
-        dma("y", T.nbt[:, a:b], T.nb[:, a:b], [], reg("nbt", a, b), 512 * b)
-    dma("y", T.xb0[:, GH:GH + H], T.gx[:, :], [], reg("xb0", GH, GH + H), 2.2e6)
-    dma("y", T.sndi[:, :], T.snd[:, :], [], reg("sndi", 0, SC), 2.2e6)
-    dma("y", T.xb0[:, OWN:GH], T.x[:, :], [], reg("xb0", OWN, GH), 3.1e6)
-    late[0] = 1
+    loads = [dma("y", T.nbt[:, a:b], T.nb[:, a:b], [], reg("nbt", a, b), 512 * (b - a)) for a, b in zip(cuts, cuts[1:])]
+    loads.append(dma("y", T.xb0[:, OWN:GH], T.x[:, :], [], reg("xb0", OWN, GH), 256 * V))
+    loads.append(dma("y", T.xb0[:, GH:GH + H], T.gx[:, :], [], reg("xb0", GH, GH + H), 256 * H))
+    for j, b in enumerate(blocks(rank)):
+        loads.append(dma("y", T.sndi[:, j * GC:(j + 1) * GC], T.snd[:, b * GC:(b + 1) * GC], [], reg("sndi", j * GC, (j + 1) * GC), 20e3))
+    for a, b in zip(loads, loads[1:]):
+        ops[b]["behind"] = a
 
     iota(A("pi", 0, 1), [[0, 1]], 0, 1)
     ts(A("pi", 1, 2), A("pi", 0, 1), 15, ALU.bitwise_and)
@@ -179,10 +200,10 @@ def build(g, core, T, topo, ops):
     ts(C("wo"), A("pi", 2, 3), 0.25, ALU.mult)
     ts(C("pw"), A("pi", 1, 2), float(W), ALU.add)
     ts(C("pn"), A("pi", 1, 2), -2048.0, ALU.add)
-    ts(C("kb"), A("pi", 1, 2), -1.0, ALU.mult, -8.0, ALU.add)
-    BIG, LO = 2.0 ** 14, 704.0
-    percol = {"f1": (1.0, 0.0), "wv": (-256.0, -7 * 256.0), "wi": (0.0, -BIG), "wm": (0.0, 200 * BIG)}
-    percol.update({"r%d" % s: (LO + s, 64.0 + s) for s in set(shift)})
+    ts(C("kb"), A("pi", 1, 2), -1.0, ALU.mult, -18.0, ALU.add)
+    BIG, LO = DIAG["idb"], 704.0
+    percol = {"f1": (1.0, 0.0), "wv": (-256.0, -7 * 256.0), "wi": (14 * BIG, -BIG)}
+    percol.update({"r%d%d" % (shift[k], PLAN["R1"][k] == "d"): (LO + 64 + shift[k], 64.0 + shift[k] + (PLAN["R1"][k] == "d")) for k in range(NCH)})
     looks = set(zip(PLAN["D"], PLAN["C"]))
     if ("v", "s") in looks:
         percol["f2"] = (-2.0, 0.0)
@@ -191,7 +212,8 @@ def build(g, core, T, topo, ops):
     for k, nm in enumerate(percol):
         cols[nm] = 10 + k
         ts(C(nm), C("lev"), percol[nm][1] - percol[nm][0], ALU.mult, percol[nm][0], ALU.add)
-    cp(CB(4), C("lev"))
+    if set(PLAN["R1"]) != {"d"}:
+        cp(CB(4), C("lev"))
     if "v" in PLAN["D"]:
         ts(CB(0), C("f1"), 2.0 ** 27, ALU.mult)
         ts(CB(1), C("f1"), 2.0 ** 27, ALU.mult, 1.0, ALU.max)
@@ -204,53 +226,50 @@ def build(g, core, T, topo, ops):
         ts(C("a2"), C("f1"), 1.5 * 2 ** 27, ALU.mult, -1.25, ALU.add)
 
     ms(A("one"), 1.0)
-    ms(A("b0"), 0.0)
-    ms(A("bz"), 0.0)
+    fill(A("bz"), 0)
     asel(A("bz", 15, 143, 16), A("one", 0, 8), [[-1, 8]], ALU.is_equal, 0, 1)
+    fill(A("b0"), 0)
     asel(A("bt"), A("one", 0, 8), [[-16, 8]], ALU.is_ge, 0, 1)
     asel(A("b0", 15, 143, 16), A("bt"), [[16, 8]], ALU.is_ge, 15, -1)
     asel(A("idn"), A("one", 0, 128), [[-1, 128]], ALU.is_equal, 0, 1)
-    for nm, c in (("be", "we"), ("bo", "wo"), ("bv", "wv"), ("bi", "wi"), ("bm", "wm")):
+    if "p" in PLAN["QP"]:
+        asel(A("idf"), A("one", 0, 128), [[-1, 128]], ALU.is_equal, 0, 1)
+    for nm, c in (("be", "we"), ("bo", "wo"), ("bv", "wv"), ("bi", "wi")):
         act(A(nm), A("b0"), ACT.Identity, scale=C(c))
-    diag = {"idm": -1.0, "idb": BIG, "idw": -129.0 / 256, "idq": 2 * K8, "idk": -K8, "idc": -33.0 / 64, "idf": 1.0,
-            "id8": 8.0, "id9": -8.0625, "idz": 2.0 ** 29}
-    if "s" in PLAN["D"]:
-        diag.update({"idp": 1.25, "id5": -1.25})
-    for nm in diag:
-        act(A(nm), A("idn"), ACT.Identity, scale=diag[nm])
-    M64, M8K, M16 = 0, 2, 4
-    for k, val in enumerate((1.5 * 2 ** 29, -1.5 * 2 ** 29, 1.5 * 2 ** 36, -1.5 * 2 ** 36, 1.5 * 2 ** 27, -1.5 * 2 ** 27)):
+    act(A("run"), A("one", 0, G), ACT.Identity, scale=C("lev"))
+    M64, M8K, M16, MID, MSG = 0, 2, 4, 6, 7
+    for k, val in enumerate((1.5 * 2 ** 29, -1.5 * 2 ** 29, 1.5 * 2 ** 36, -1.5 * 2 ** 36, 1.5 * 2 ** 27, -1.5 * 2 ** 27, 31.5, 12288.0)):
         ms(A("mg", 128 * k, 128 * k + 128, p1=32), val)
     iota(A("wi"), [[-1, 16]], 128, 1)
     ts(A("wi"), A("wi"), 15, ALU.bitwise_and)
-    ts(A("wa", 0, 16), A("wi"), 1.5, ALU.is_le)
-    ts(A("wa", 16, 32), A("wi"), 3.5, ALU.is_le, 255.0, ALU.mult)
-    ts(A("wa", 32, 48), A("wi"), 1.5, ALU.is_le, -254.0, ALU.mult)
-    ts(A("wa", 48, 64), A("wi"), 4.0, ALU.is_equal, 65536.0, ALU.mult)
-    tt(A("wa", 16, 32), A("wa", 16, 32), A("wa", 32, 48), ALU.add)
-    ts(A("wa", 0, 16), A("wa", 16, 32), 254.0, ALU.is_ge)
-    tt(A("wa", 16, 32), A("wa", 16, 32), A("wa", 0, 16), ALU.add)
-    tt(A("wtab"), A("wa", 16, 32), A("wa", 48, 64), ALU.add)
+    ts(A("wa", 0, 16), A("wi"), 1.5, ALU.is_le, -255.0, ALU.mult)
+    ts(A("wa", 16, 32), A("wi"), 3.5, ALU.is_le, 256.0, ALU.mult)
+    ts(A("wa", 32, 48), A("wi"), 4.0, ALU.is_equal, 65536.0, ALU.mult)
+    tt(A("wa", 0, 16), A("wa", 0, 16), A("wa", 16, 32), ALU.add)
+    tt(A("wtab"), A("wa", 0, 16), A("wa", 32, 48), ALU.add)
     iota(A("posh"), [[0, NCH], [16, CW]], 16, 0)
     for k in range(NCH):
-        ms(A("tw", k * TW, k * TW + 16), shift[k])
+        fill(A("tw", k * TW, k * TW + 16), shift[k])
+    for s in sorted(set(shift[k] for k in range(NCH) if PLAN["R1"][k] == "d")):
+        fill(A("lv", int(s) // 2 * W, int(s) // 2 * W + W), 64 + s)
     iota(A("mpos"), [[16, SC]], 0, 0)
     asel(A("cu"), A("one"), [[-1, 16], [-16, 32]], ALU.is_equal, 0, 1)
+    marks = []
     for d in range(N - 1):
-        ka, kb = A("ka", d * GC, (d + 1) * GC), A("kb", d * GC, (d + 1) * GC)
-        if PLAN["FB"][d] == "v":
-            ms(ka, -207.0); ms(kb, 0.0)
-        else:
-            iota(ka, [[-16, GC]], 0, 0)
-            act(kb, A("one", 0, GC), ACT.Identity, scale=C("kb"))
+        cut = {"v": GC, "s": 0, "h": GC // 2}[PLAN["FB"][d]]
+        marks.append([m for m in (("v", d * GC, d * GC + cut), ("s", d * GC + cut, (d + 1) * GC)) if m[2] > m[1]])
+        for e, la, lb in marks[d]:
+            if e == "v":
+                fill(A("ka", la, lb), -227); fill(A("kb", la, lb), 0)
+            else:
+                iota(A("ka", la, lb), [[-16, lb - la]], 0, 0)
+                act(A("kb", la, lb), A("one", 0, lb - la), ACT.Identity, scale=C("kb"))
 
     ZC, ZL = PS(7, 0, LC), PS(7, LC, 2 * LC)
-    late[0] = 0
     for hf in range(2):
         la, lb = hf * LC // 2, (hf + 1) * LC // 2
         mm(listmm(PS(7, la, lb), "bz", "zc", 16 * la, 16 * lb, k=8))
         cp(A("cu16", la, lb), PS(7, la, lb))
-    late[0] = 1
     act(A("c0b"), ZC, ACT.Identity)
     mm(acc(PS(6, 0, LC), [("id9", A("c0b")), M16, M16 + 1, ("id8", A("c0b"))]))
     act(A("par"), PS(6, 0, LC), ACT.Identity, bias=-1.0, scale=-0.25)
@@ -261,7 +280,7 @@ def build(g, core, T, topo, ops):
     act(A("pn"), A("nr"), ACT.Identity, bias=C("pn"), scale=2048.0)
 
     def failpos(n, Z, P):
-        mm(acc(Z, [("idn", A("l63")), ("idm", A("c0b"))] + [("idm", Q("gg", j)) for j in range(n)]))
+        mm(acc(Z, [("idn", A("l63")), ("idm", A("c0b"))] + [("idg", Q("gg", j)) for j in range(n)]))
         ts(A("arm"), Z, n / 2 - 15.0, ALU.is_equal, float(W), ALU.mult)
         mm(acc(P, [("idn", A("posh")), ("idn", A("arm"))]))
         act(A("pf"), P, ACT.Identity, bias=C("pw"))
@@ -273,31 +292,28 @@ def build(g, core, T, topo, ops):
     peers = [c for c in T.cores if c != core]
     far = sorted(set(e for c in peers if topo.chip(c) != topo.chip(core) for e in topo.engines(core, c)))
 
-    def send(n, pairs, src, so, dst, do):
-        nfar = sum(topo.chip(T.cores[p]) != topo.chip(core) for p, _ in pairs)
-        tr, kf, kn, tot = [], 0, 0, 0
-        for p, blk in pairs:
+    def send(n, trips, src, dst):
+        off = [p for p, _, _ in trips if topo.chip(T.cores[p]) != topo.chip(core)]
+        tr, kf, kn, tot, rd, wr = [], 0, 0, 0, [], []
+        for p, so, do in trips:
             dc = T.cores[p]
             assert topo.may_write(core, dc)
-            if topo.chip(dc) != topo.chip(core):
-                w = len(far) // nfar
+            if p in off:
+                w = len(far) // len(off)
                 es = far[kf * w:(kf + 1) * w]; kf += 1
             else:
                 free = [e for e in topo.engines(core, dc) if e not in far]
-                w = len(free) // (len(pairs) - nfar)
+                w = len(free) // (len(trips) - len(off))
                 es = free[kn * w:(kn + 1) * w]; kn += 1
             rid, pid, _ = topo.addr(dc)
             tr.append(RemoteDMATransfer(dst_ids=[DstId(rid=rid, pnc=pid)], dma_engine_mask=sum(1 << e for e in es),
-                                        remote_sem=T.sem["arr%d" % n], src=T[src][:, so + blk * G:so + (blk + 1) * G],
-                                        dst=T[dst][:, do + blk * G:do + (blk + 1) * G]))
-            tot += len(es)
-        s = add("g", lambda: g.remote_dma_fused(tr, local_sem=T.sem["loc%d" % n]),
-                reg(src, so, so + H) + [("sent", 0, 1)], [("sent", 0, 1)], REMOTE_US - 1.0, "send", ("loc%d" % n, tot))
-        add("x", None, [], reg(dst, do, do + H), REMOTE_US, "arrive", ("arr%d" % n, tot, s))
+                                        remote_sem=T.sem["arr%d" % n], src=T[src][:, so:so + G], dst=T[dst][:, do:do + G]))
+            tot += len(es); rd += reg(src, so, so + G); wr += reg(dst, do, do + G)
+        us = FAR_US if off else NEAR_US
+        s = add("g", lambda: g.remote_dma_fused(tr, local_sem=T.sem["loc%d" % n]), rd, [], us - 1.0, "send", ("loc%d" % n, tot))
+        add("x", None, [], wr, us, "arrive", ("arr%d" % n, tot, s))
 
-    late[0] = 0
-    send(RO - 1, [((rank - d) % N, d - 1) for d in range(1, N)], "xb0", GH, "xb1", 0)
-    late[0] = 1
+    send(2 * RO - 1, [((rank - b - 1) % N, GH + b * G, blocks((rank - b - 1) % N).index(b) * G) for b in range(N - 1)], "xb0", "xb1")
 
     def shifted(e, k, src):
         if PLAN["D"][k] == "v":
@@ -310,7 +326,8 @@ def build(g, core, T, topo, ops):
         k, hf = sub // 2, sub % 2
         a, b = sub * n, (sub + 1) * n
         HP, WP, RP = PS(sub % 2, 0, n), PS(2, 0, n), PS(3, 0, n)
-        r0 = k * TW + 16 + W + hf * n
+        byd = PLAN["R1"][k] == "d"
+        r0 = k * TW + 16 + W
         act(A("wsb", a, b), IND(A("wtab"), A("cu16", a // 16, b // 16)), ACT.Identity)
         ts(HP, A("nbt", a, b), 1.5 * 2 ** 31, ALU.add, 1.5 * 2 ** 31, ALU.subtract)
         tt(A("lr", a, b), A("nbt", a, b), HP, ALU.subtract)
@@ -319,29 +336,31 @@ def build(g, core, T, topo, ops):
         mm(acc(WP, [("idn", A("wsb", a, b))]))
         tt(A("pl", a, b), WP, A("pb", a, b), ALU.mult)
         mm(acc(RP, [("idn", A("lr", a, b)), ("idm", A("pb", a, b))]))
-        act(A("tw", r0, r0 + n), RP, ACT.Identity, bias=C("r%d" % shift[k]), scale=C("f1"))
+        act(A("tw", r0 + byd * W + hf * n, r0 + byd * W + hf * n + n), RP, ACT.Identity, bias=C("r%d%d" % (shift[k], byd)), scale=C("f1"))
         if not hf:
             continue
-        r0 -= n
-        move(PLAN["R1"][k], A("tw", r0 + W, r0 + 2 * W), A("tw", r0, r0 + W), CB(4))
+        if byd:
+            lv = int(shift[k]) // 2 * W
+            dma("y", T.tw[:, r0:r0 + W], T.tw[:, r0 + W:r0 + 2 * W], reg("tw", r0 + W, r0 + 2 * W), reg("tw", r0, r0 + W), 256 * W)
+            dma("y", T.tw[15::16, r0:r0 + W], T.lv[15::16, lv:lv + W], reg("lv", lv, lv + W), reg("tw", r0, r0 + W), 16 * W)
+        else:
+            move(PLAN["R1"][k], A("tw", r0 + W, r0 + 2 * W), A("tw", r0, r0 + W), CB(4))
         per = NCH // PLAN["DEC"]
-        h, m = k // per, per * CW
-        bank, la = 4 + h % 2, h * m
+        m, la = per * CW, k // per * per * CW
 
-        def sums(j):
-            return PS(bank, j * m, (j + 1) * m)
+        def sums(j, lo, hi):
+            return PS(4 + k // per % 2, j * m + lo, j * m + hi) if 4 * m <= 512 else PS(4 + j % 2, j // 2 * m + lo, j // 2 * m + hi)
         for j, (band, src) in enumerate((("be", "ph"), ("bo", "ph"), ("be", "pl"), ("bo", "pl"))):
-            out = PS(bank, j * m + (k % per) * CW, j * m + (k % per + 1) * CW) if m <= 128 else PS(4 + j % 2, j // 2 * m + k * CW, j // 2 * m + (k + 1) * CW)
+            out = sums(j, k % per * CW, (k % per + 1) * CW)
             mm(listmm(out, band, src, k * W, (k + 1) * W, stop=j != 1)
                + (acc(out, [("idz", A("par", k * CW, (k + 1) * CW))], start=False) if j == 1 else []))
         if k % per < per - 1:
             continue
         for j in range(2):
             ee = A("ee", j * LC + la, j * LC + la + m)
-            act(ee, sums(2 * j) if m <= 128 else PS(4, j * m, (j + 1) * m), ACT.Identity)
+            act(ee, sums(2 * j, 0, m), ACT.Identity)
             for t in range(2):
-                tt(A("li", (2 * t + j) * LC + la, (2 * t + j) * LC + la + m), sums(2 * j + 1) if m <= 128 else PS(5, j * m, (j + 1) * m), ee,
-                   ALU.min if t else ALU.max)
+                tt(A("li", (2 * t + j) * LC + la, (2 * t + j) * LC + la + m), sums(2 * j + 1, 0, m), ee, ALU.min if t else ALU.max)
         for dst, j, mask in (("qhi", 0, 127 * 64), ("qlo", 1, 255)):
             ts(A(dst, la, la + m), A("li", j * LC + la, j * LC + la + m), mask, ALU.bitwise_and)
         tt(A("qq0", la, la + m), A("qlo", la, la + m), A("qhi", la, la + m), ALU.add)
@@ -356,136 +375,135 @@ def build(g, core, T, topo, ops):
 
     UB = 7 * 512 - 2 * CW
     slot = [0]
-    n = W // 2
 
-    def pair(ns):
+    def pair():
         p = 1024 * slot[0] + 512 - n
-        slot[0] = (slot[0] + 1) % ns
+        slot[0] = (slot[0] + 1) % 3
         return p
 
-    def look(s, k, cur, ns):
+    def look(k, cur):
         ca, cb = k * CW, (k + 1) * CW
         a, b = 16 * ca, 16 * cb
-        U, CC = A("ps", UB + ca, UB + cb), A("tw", k * TW + 16, k * TW + 16 + W)
+        CC = A("tw", k * TW + 16, k * TW + 16 + W)
+        pd = pair() if PLAN["D"][k] == "s" else 0
+        for lo, hi in ((a, a + n), (a + n, b)):
+            src = IND(A(cur, OWN, GH + H), A("off", lo // 16, hi // 16))
+            if PLAN["D"][k] == "s":
+                act(A("dd", lo, hi), src, ACT.Identity)
+                mm(acc(A("ps", pd + lo - a, pd + hi - a), [("id5", A(cur, OWN + lo, OWN + hi))], stop=False))
+                mm(acc(A("ps", pd + lo - a, pd + hi - a), [("idp", A("dd", lo, hi))], start=False))
+            else:
+                tt(A("dd", lo, hi), src, A("x2", lo, hi), ALU.subtract)
         if PLAN["D"][k] == "s":
-            pd = pair(ns)
             D = A("ps", pd, pd + W)
-
-            def part(lo, hi):
-                act(A("dd", lo, hi), IND(A(cur, OWN, GH + H), A("off", lo // 16, hi // 16)), ACT.Identity)
-                mm(acc(A("ps", pd + lo - a, pd + hi - a), [("id5", A(cur, OWN + lo, OWN + hi)), ("idp", A("dd", lo, hi))]))
-            near = lambda: ts(A("aa", a, b), D, C("a1"), ALU.add, C("a2"), ALU.is_equal)
-            step = lambda: (ts(CC, D, C("c1"), ALU.max, C("f1"), ALU.min) if PLAN["C"][k] == "v" else act(CC, D, ACT.Sign, scale=C("f1")))
+            ts(A("aa", a, b), D, C("a1"), ALU.add, C("a2"), ALU.is_equal)
+            ts(CC, D, C("c1"), ALU.max, C("f1"), ALU.min) if PLAN["C"][k] == "v" else act(CC, D, ACT.Sign, scale=C("f1"))
         else:
             D = A("dd", a, b)
+            ts(A("aa", a, b), D, CB(0), ALU.add, CB(1), ALU.is_equal)
+            ts(CC, D, CB(2), ALU.max, CB(3), ALU.min) if PLAN["C"][k] == "v" else act(CC, D, ACT.Sign, bias=C("f2"), scale=C("f1"))
 
-            def part(lo, hi):
-                tt(A("dd", lo, hi), IND(A(cur, OWN, GH + H), A("off", lo // 16, hi // 16)), A("x2", lo, hi), ALU.subtract)
-            near = lambda: ts(A("aa", a, b), D, CB(0), ALU.add, CB(1), ALU.is_equal)
-            step = lambda: (ts(CC, D, CB(2), ALU.max, CB(3), ALU.min) if PLAN["C"][k] == "v"
-                            else act(CC, D, ACT.Sign, bias=C("f2"), scale=C("f1")))
-        votes = lambda: mm(acc(U, [("idn", A("bias", ca, cb))], stop=False) + listmm(U, "bv", "aa", a, b, start=False, stop=False)
-                           + acc(U, [M8K, M8K + 1, ("idn", A("posh", ca, cb)), ("idn", A("pn", ca, cb))], start=False))
-        return [lambda: part(a, a + n), lambda: part(a + n, b), near, votes, step]
+    def votes(ca, cb):
+        U = A("ps", UB + ca, UB + cb)
+        mm(acc(U, [("idn", A("bias", ca, cb))], stop=False) + listmm(U, "bv", "aa", 16 * ca, 16 * cb, start=False, stop=False)
+           + acc(U, [M8K, M8K + 1, ("idn", A("posh", ca, cb)), ("idn", A("pn", ca, cb))], start=False))
+
+    def change(s, k, cur, new):
+        a = k * W
+        eT, eW, eX = PLAN["T"][s][k], PLAN["W"][s][k], PLAN["X"][s][k]
+        pb_ = pair()
+        for hf, (lo, hi) in enumerate([(a, a + n), (a + n, a + W)]):
+            P = A("ps", pb_ + lo - a, pb_ + hi - a)
+            src = IND(A("tw", k * TW, (k + 1) * TW), A("sel", lo // 16, hi // 16))
+            own, t_, sg, out = A(cur, OWN + lo, OWN + hi), A("tt", lo, hi), A("sg", lo, hi), A(new, OWN + lo, OWN + hi)
+            xv, plus = eX == "v" or (eX == "h" and hf == 0), 0.0
+            if eT == "v" or (eT == "h" and hf == 0):
+                tt(t_, src, A("x2", lo, hi) if shift[k] else own, ALU.add)
+                rest = t_
+                if eW == "r":
+                    mm(acc(P, [MID], stop=False))
+                    mm(acc(P, [("idm", t_), M64, M64 + 1] + ([] if xv else [("idn", t_)]), start=False))
+                else:
+                    move(eW, sg, t_, 12288 - 31.5)
+                    plus = 12288.0
+                    if xv:
+                        mm(acc(P, [MSG], stop=False))
+                    mm(acc(P, [("idm", sg)] + ([] if xv else [("idn", t_)]), start=not xv))
+            else:
+                act(t_, src, ACT.Identity, bias=32.5 - shift[k])
+                rest, plus = own, 31.5
+                mm(acc(P, [("idm", own)], stop=False))
+                mm(acc(P, [("idm", t_), M64, M64 + 1, ("idn", t_), MID if xv else ("idn", own)], start=False))
+            if xv:
+                tt(out, P, rest, ALU.add)
+            else:
+                act(out, P, ACT.Identity, bias=plus)
+            if s == RO - 1:
+                dma("y", T.yx[:, lo:hi], T[new][:, OWN + lo:OWN + hi], out[1], [], 256 * n)
+
+    def cursors(s, h):
+        la, lb = h * LC // 2, (h + 1) * LC // 2
+        gl, cl, Z = A("gg", s * LC + la, s * LC + lb), A("cb4", la, lb), PS(6 + h, 128, 128 + LC // 2)
+        act(gl, A("ps", UB + la, UB + lb), ACT.Sign, bias=-K8 / 2)
+        mm(acc(Z, [("idc", cl), ("idd", gl), M16, M16 + 1, ("idn", cl), ("idh", gl)]))
+        move(PLAN["YC"][2], A("curb", la, lb), Z)
+        for j in range(4):
+            mm([(A("ps", (6 + h) * 512 + i, (6 + h) * 512 + n, 16, 32 * j, 32 * j + 32), A("cu", 32 * i, 32 * i + 32),
+                 A("curb", la + j * CW // 2, la + (j + 1) * CW // 2), True, True) for i in range(16)])
+        move(PLAN["YC"][h], A("ycs", h * n, (h + 1) * n), PS(6 + h, 0, n))
+        for j in range(4):
+            dma("y", T.yc[:, 16 * la + j * n:16 * la + (j + 1) * n], T.ycs[32 * j:32 * j + 8, h * n:(h + 1) * n],
+                reg("ycs", h * n, (h + 1) * n), [], 15e3)
 
     for s in range(RO):
         cur, new = xb[s % 2], xb[(s + 1) % 2]
         last = s == RO - 1
         first[0] = 0 if last else len(ops)
-        ns = 2 if last else 3
-        slot[0] = 0 if last else slot[0]
+        todo = []
         for k in range(NCH):
-            ca, cb = k * CW, (k + 1) * CW
-            a, b = 16 * ca, 16 * cb
-            eT, eW, eX = PLAN["T"][s][k], PLAN["W"][s][k], PLAN["X"][s][k]
-            if k == 0:
-                for f in look(s, 0, cur, ns):
-                    f()
-            nxt = look(s, k + 1, cur, ns) if k + 1 < NCH else [None] * 5
-            picks = [lambda: tt(A("t3", ca, cb), A("ps", UB + ca, UB + cb), A("pf", ca, cb), ALU.min),
-                     lambda: cp(A("sel", ca, cb), A("t3", ca, cb))]
-            both = [nxt[0], picks[0], nxt[1], picks[1], nxt[2], nxt[3], nxt[4]]
-            if PLAN["SP"] == 0 or (PLAN["SP"] == 2 and k == 0):
-                both = picks
-            for f in both:
-                if f:
-                    f()
-            pb_ = pair(ns)
-            win = A("tw", k * TW, (k + 1) * TW)
-            for hf, (lo, hi) in enumerate([(a, a + n), (a + n, b)]):
-                P = A("ps", pb_ + lo - a, pb_ + hi - a)
-                src, own, t_ = IND(win, A("sel", lo // 16, hi // 16)), A(cur, OWN + lo, OWN + hi), A("tt", lo, hi)
-                out = A(new, OWN + lo, OWN + hi)
-                xv = eX == "v" or (eX == "h" and hf == 0)
-                late[0] = 0
-                if eT == "v" or (eT == "h" and hf == 0):
-                    tt(t_, src, A("x2", lo, hi) if shift[k] else own, ALU.add)
-                    late[0] = PLAN["LT"]
-                    if eW == "m":
-                        ts(A("sg", lo, hi), t_, 64.0, ALU.is_ge, -64.0, ALU.mult)
-                        mm(acc(P, [("idn", A("sg", lo, hi))] + ([] if xv else [("idn", t_)])))
-                    else:
-                        mm(acc(P, [("idw", t_), M64, M64 + 1] + ([] if xv else [("idn", t_)])))
-                    if xv:
-                        tt(out, P, t_, ALU.add)
-                    else:
-                        act(out, P, ACT.Identity)
-                else:
-                    act(t_, src, ACT.Identity, bias=-shift[k])
-                    late[0] = PLAN["LT"]
-                    mm(acc(P, [("idw", own)], stop=False))
-                    mm(acc(P, [("idw", t_), M64, M64 + 1, ("idn", t_)] + ([] if xv else [("idn", own)]), start=False))
-                    if xv:
-                        tt(out, P, own, ALU.add)
-                    else:
-                        act(out, P, ACT.Identity)
-            late[0] = 0
-            if both is picks and nxt[0]:
-                for f in nxt:
-                    f()
-            if last:
-                dma("y", T.yx[:, a:b], T[new][:, OWN + a:OWN + b], reg(new, OWN + a, OWN + b), [], 256 * W)
-                if k >= NCH - 2:
-                    k0 = 0 if k < NCH - 1 else k
-                    la, lb = k0 * CW, cb
-                    gl, cl, Z = A("gg", s * LC + la, s * LC + lb), A("cb4", la, lb), PS(6, la, lb)
-                    ts(gl, A("ps", UB + la, UB + lb), K8 / 2, ALU.is_ge, 0.5, ALU.subtract)
-                    mm(acc(Z, [("idc", cl), ("idc", gl), M16, M16 + 1, ("idn", cl), ("idn", gl)]))
-                    cp(A("curb", la, lb), Z)
-                    for j in range(k0, k + 1):
-                        for hf in range(2):
-                            mm([(A("ps", (4 + hf) * 512 + i, (4 + hf) * 512 + n, 16, 32 * j, 32 * j + 32), A("cu", 32 * i, 32 * i + 32),
-                                 A("curb", j * CW + hf * CW // 2, j * CW + (hf + 1) * CW // 2), True, True) for i in range(16)])
-                    mark = [("ycs%d" % k0, 0, 1)]
-                    for hf in range(2):
-                        o_ = A("ycs", hf * n, (hf + 1) * n, 1, 32 * k0, 32 * k + 32)
-                        cp((o_[0], mark) + o_[2:], A("ps", (4 + hf) * 512, (4 + hf) * 512 + n, 1, 32 * k0, 32 * k + 32))
-                    for j in range(k0, k + 1):
-                        dma("y", T.yc[:, j * W:(j + 1) * W], T.ycs[32 * j:32 * j + 8, 0:W], mark, [], 30e3)
+            look(k, cur)
+            if (k + 1) % PLAN["VK"] == 0:
+                votes((k + 1 - PLAN["VK"]) * CW, (k + 1) * CW)
+            while todo:
+                change(s, todo.pop(0), cur, new)
+            if (k + 1) % PLAN["PK"] == 0:
+                ca, cb = (k + 1 - PLAN["PK"]) * CW, (k + 1) * CW
+                tt(A("t3", ca, cb), A("ps", UB + ca, UB + cb), A("pf", ca, cb), ALU.min)
+                cp(A("sel", ca, cb), A("t3", ca, cb))
+                todo = list(range(k + 1 - PLAN["PK"], k + 1))
+            if last and k % 2:
+                cursors(s, k // 2)
+        if not last:
+            act(Q("gg", s), A("ps", UB, UB + LC), ACT.Sign, bias=-K8 / 2)
+        for k in todo:
+            change(s, k, cur, new)
         if last:
             break
-        for d in range(N - 1):
-            src = IND(A("tt"), A("sndu", d * GC, (d + 1) * GC))
-            if PLAN["FB"][d] == "v":
-                ts(A("mb", d * G, (d + 1) * G), src, 63.5, ALU.is_ge, 2.0, ALU.mult)
-            else:
-                act(A("mb", d * G, (d + 1) * G), src, ACT.Sign, bias=-63.5)
-        U2 = PS(6, 0, SC)
-        mm(acc(U2, [("idb", A("ka")), ("idb", A("kb"))], stop=False) + listmm(U2, "bm", "mb", 0, H, start=False, stop=False))
-        for d in range(N - 1):
-            scan(A("inc", d * G, (d + 1) * G), A("mb", d * G, (d + 1) * G))
-        mm(listmm(U2, "bi", "inc", 0, H, start=False))
-        tt(U2, U2, A("mpos"), ALU.max)
-        tt(A("s2"), U2, A("sndp"), ALU.min)
-        cp(A("soff"), A("s2"))
-        hs = PLAN["GS"]
-        cp(A(cur, 0, 16 * hs), IND(A(new, 0, GH), A("soff", 0, hs)))
-        act(A(cur, 16 * hs, H), IND(A(new, 0, GH), A("soff", hs, SC)), ACT.Identity)
-        send(s, [((rank + d) % N, d - 1) for d in range(1, N)], cur, 0, new, GH)
-        late[0] = 1
+        for j, (d0, d1) in enumerate(sends):
+            la, lb = d0 * GC, d1 * GC
+            for d in range(d0, d1):
+                for e, ma, mb in marks[d]:
+                    src = IND(A("tt"), A("sndu", ma, mb))
+                    if e == "v":
+                        ts(A("mb", 16 * ma, 16 * mb), src, 63.5, ALU.is_ge, 2.0, ALU.mult)
+                    else:
+                        act(A("mb", 16 * ma, 16 * mb), src, ACT.Sign, bias=-63.5)
+            U2 = PS(6 + j, 128 * j + la, 128 * j + lb)
+            mm(acc(U2, [("idb", A("ka", la, lb)), ("idb", A("kb", la, lb))], stop=False))
+            for d in range(d0, d1):
+                scan(A("inc", d * G, (d + 1) * G), A("mb", d * G, (d + 1) * G))
+            mm(listmm(U2, "bi", "inc", 16 * la, 16 * lb, start=False))
+            tt(U2, U2, A("mpos", la, lb), ALU.max)
+            tt(A("s2", la, lb), U2, A("sndp", la, lb), ALU.min)
+            cp(A("soff", la, lb), A("s2", la, lb))
+            hs = la + PLAN["GS"][j]
+            if hs > la:
+                cp(A(cur, 16 * la, 16 * hs), IND(A(new, 0, GH), A("soff", la, hs)))
+            if lb > hs:
+                act(A(cur, 16 * hs, 16 * lb), IND(A(new, 0, GH), A("soff", hs, lb)), ACT.Identity)
+            send(2 * s + j, [((rank + b + 1) % N, d * G, GH + b * G) for d, b in enumerate(blocks(rank)) if d0 <= d < d1], cur, new)
         for k in range(NCH):
             shifted(PLAN["X2"][k], k, new)
-        ts(Q("gg", s), A("ps", UB, UB + LC), K8 / 2, ALU.is_ge, 0.5, ALU.subtract)
         first[0] = 0
         q0, q1, left = "qq%d" % (s % 2), "qq%d" % ((s + 1) % 2), RO - 1 - s
         p0, p1 = 1024 * slot[0], 1024 * ((slot[0] + 1) % 3)
@@ -493,17 +511,23 @@ def build(g, core, T, topo, ops):
             for t in range(t0, t1):
                 cut = [t * LC] + ([512] if t * LC < 512 < (t + 1) * LC else []) + [(t + 1) * LC]
                 for lo, hi in zip(cut, cut[1:]):
-                    mm(acc(A("ps", p0 + lo, p0 + hi), [("idf", A(q0, lo, hi)), ("idq", A("gg", (s - t) * LC + lo, (s - t) * LC + hi))]))
+                    mm(acc(A("ps", p0 + lo, p0 + hi), ([("idf", A(q0, lo, hi))] if PLAN["QP"][t0 > 0] == "p" else [])
+                           + [("idq", A("gg", (s - t) * LC + lo, (s - t) * LC + hi))]))
             if t1 > t0:
-                tt(Q(q1, t0, t1 - t0), A("ps", p0 + t0 * LC, p0 + t1 * LC), Q(q0, t0 + 1, t1 - t0), ALU.min)
+                QP = A("ps", p0 + t0 * LC, p0 + t1 * LC)
+                if PLAN["QP"][t0 > 0] == "v":
+                    tt(QP, QP, Q(q0, t0, t1 - t0), ALU.add)
+                tt(Q(q1, t0, t1 - t0), QP, Q(q0, t0 + 1, t1 - t0), ALU.min)
             if t0 == 0:
                 OF = A("ps", p1, p1 + LC)
-                mm(acc(OF, [("idf", Q(q1, 0))] + [("idk", Q("gg", j)) for j in range(s + 1)]))
+                mm(acc(OF, ([("idf", Q(q1, 0))] if PLAN["QP"][2] == "p" else []) + [("idk", Q("gg", j)) for j in range(s + 1)]))
+                if PLAN["QP"][2] == "v":
+                    tt(OF, OF, Q(q1, 0), ALU.add)
                 ts(A("off"), OF, K8 * (s + 1) / 2 - LO / 4, ALU.add)
         failpos(s + 1, A("ps", p1 + 512, p1 + 512 + LC), A("ps", p1 + 512 + LC, p1 + 512 + 2 * LC))
         if s == RO - 2:
             Z = A("ps", p1 + LC, p1 + 2 * LC)
-            mm(acc(Z, [("idn", A("c0b"))] + [("idn", Q("gg", j)) for j in range(s + 1)]))
+            mm(acc(Z, [("idn", A("c0b"))] + [("idh", Q("gg", j)) for j in range(s + 1)]))
             act(A("cb4"), Z, ACT.Identity, bias=RO / 2)
 
 
@@ -527,74 +551,68 @@ def depend(ops):
         o["d"] = deps
 
 
-def order(ops, prio):
+def lay(ops, before, after, first, key):
     n = len(ops)
-    left = [len(o["p"]) for o in ops]
-    ready = {}
-    for i in range(n):
-        if not left[i]:
-            ready.setdefault(ops[i]["q"], []).append(i)
-    free, fin, can, out, tol = {}, [0.0] * n, [0.0] * n, [], PLAN["TOL"]
-    while len(out) < n:
-        st, i = 1e9, -1
-        for q in ready:
-            if ready[q]:
-                f = free.get(q, 0.0)
-                k = min(ready[q], key=prio.get)
-                t = max(can[k], f)
-                if t > f:
-                    fit = [j for j in ready[q] if max(can[j], f) + ops[j]["hold"] <= t + tol]
-                    if fit:
-                        k = min(fit, key=prio.get)
-                        t = max(can[k], f)
-                if t < st:
-                    st, i = t, k
-        o = ops[i]
-        ready[o["q"]].remove(i)
-        fin[i] = st + o["dur"]
-        free[o["q"]] = st + o["hold"]
-        out.append(i)
-        for j, lat in o["s"]:
-            can[j] = max(can[j], st + lat)
+    left = [len(before[i]) for i in range(n)]
+    can, at, busy = list(first), [0.0] * n, {}
+    ready = sorted((key[i], i) for i in range(n) if not left[i])
+    while ready:
+        i = ready.pop(0)[1]
+        t, h, line = can[i], ops[i]["hold"], busy.setdefault(ops[i]["q"], [])
+        k = len(line)
+        while k and line[k - 1][1] > t:
+            k -= 1
+        while k < len(line) and line[k][0] < t + h - 1e-9:
+            t = max(t, line[k][1]); k += 1
+        line.insert(k, (t, t + h))
+        at[i] = t
+        for j, lat in after[i]:
+            if can[j] < t + lat:
+                can[j] = t + lat
             left[j] -= 1
             if not left[j]:
-                ready.setdefault(ops[j]["q"], []).append(j)
-    return out, fin
+                ready.append((key[j], j)); ready.sort()
+    return at
 
 
 def best_order(ops):
     n = len(ops)
-    like = {}
+    succ, pred, like = [[] for _ in ops], [[] for _ in ops], {}
     for i, o in enumerate(ops):
-        o["p"], o["s"] = set(o["d"]) | ({o["x"][2]} if o["kind"] == "arrive" else set()), []
-        o["hold"] = {"dma": 0.1, "send": 1.0, "arrive": 0.0}.get(o["kind"], o["dur"])
+        o["hold"] = {"dma": max(0.1, o["dur"] - 2.0), "send": 1.0, "arrive": 0.0}.get(o["kind"], o["dur"])
         like.setdefault(o["tag"], []).append(i)
     for j, o in enumerate(ops):
-        for i in o["p"]:
-            chain = o["q"] == "p" and ops[i]["q"] == "p"
-            ops[i]["s"].append((j, 0.0 if o["kind"] == "arrive" else ops[i]["dur"] + (0.0 if chain else LAT)))
-    if not ORDER:
-        prio = {}
-        for i in range(n - 1, -1, -1):
-            prio[i] = min([prio[j] - lat for j, lat in ops[i]["s"]] + [-ops[i]["dur"]])
-        marks = [i for i, o in enumerate(ops) if o["kind"] != "c"]
+        edges = [(i, ops[i]["dur"] + (0.0 if o["q"] == "p" and ops[i]["q"] == "p" else LAT)) for i in o["d"]]
+        if o["kind"] == "arrive":
+            edges.append((o["x"][2], 0.0))
+        if "behind" in o:
+            edges.append((o["behind"], ops[o["behind"]]["hold"]))
+        for i, lat in edges:
+            succ[i].append((j, lat)); pred[j].append((i, lat + o["hold"] - ops[i]["hold"]))
+    zero, rest = [0.0] * n, [o["dur"] - o["hold"] for o in ops]
 
-        def cost(z):
-            fin = order(ops, z)[1]
-            return max(fin) + 0.02 * sum(fin[i] for i in marks) + 1e-4 * sum(fin)
-        best, x = cost(prio), PLAN["SEED"]
-        for _ in range(PLAN["TRY"]):
-            z = dict(prio)
-            for _ in range(2):
+    def turn(at):
+        back = lay(ops, succ, pred, rest, [-at[i] - ops[i]["hold"] for i in range(n)])
+        at = lay(ops, pred, succ, zero, [-back[i] - ops[i]["hold"] for i in range(n)])
+        return max(at[i] + ops[i]["dur"] for i in range(n)) + 1e-5 * sum(at), at
+    if not ORDER:
+        best, at = turn(lay(ops, pred, succ, zero, list(range(n))))
+        x, now, kept = PLAN["SEED"], best, at
+        for r in range(PLAN["TRY"]):
+            z, seq = list(at), sorted(range(n), key=lambda i: at[i])
+            mid = (x >> 6) % n
+            for _ in range(PLAN["SHAKE"]):
                 x = (x * 1103515245 + 12345) % 2 ** 31
-                i = (x >> 8) % n
-                for j in (like[ops[i]["tag"]] if (x >> 7) % 2 else [i]):
-                    z[j] += (-4, -2, -1, -0.5, 0.5, 1, 2, 4)[(x >> 4) % 8]
-            e = cost(z)
-            if e <= best:
-                best, prio = e, z
-        ORDER.append(prio)
-    return order(ops, ORDER[0])
+                for j in like[ops[seq[min(n - 1, max(0, mid + (x >> 8) % (2 * PLAN["NEAR"]) - PLAN["NEAR"]))]]["tag"]]:
+                    z[j] += (-2, -1, -0.5, -0.25, 0.25, 0.5, 1, 2)[(x >> 4) % 8]
+            e, z = turn(z if PLAN["FAST"] else lay(ops, pred, succ, zero, z))
+            if e <= now + PLAN["HEAT"] * (1 - r / PLAN["TRY"]) * ((x >> 12) % 64) / 64:
+                now, at = e, z
+            if e < best:
+                best, kept = e, z
+        ORDER.append(kept)
+    at = ORDER[0]
+    return sorted(range(n), key=lambda i: (at[i], i)), [at[i] + ops[i]["dur"] for i in range(n)]
 
 
 def emit(g, T, ops, seq):

@@ -1,3 +1,4 @@
+import math
 from concourse.bass import DstId, RemoteDMATransfer
 from concourse.mybir import AluOpType as ALU, ActivationFunctionType as ACT
 
@@ -15,17 +16,18 @@ def _sb(cols, dtype):
     return ("sbuf", [128, cols], dtype)
 
 
-DIAG = {"idm": -1.0, "idb": 2 * K8, "idw": -129.0 / 256, "idq": K8, "idk": -K8 / 2, "idc": -33.0 / 64, "idd": -33.0 / 128,
+DIAG = {"idm": -1.0, "idq": K8, "idk": -K8 / 2, "idc": -33.0 / 64, "idd": -33.0 / 128,
         "idh": 0.5, "idg": -0.5, "id8": 8.0, "id9": -8.0625, "idz": 2.0 ** 29, "idp": 1.25, "id5": -1.25, "ids": -32.0}
+EARLY = ("idm", "id8", "id9", "idz")
 SCRATCH = {"xb0": _sb(V + 2 * H, "bfloat16"), "xb1": _sb(V + 2 * H, "bfloat16"), "nbt": _sb(V, "int32"),
            "tw": _sb(NCH * TW, "bfloat16"), "mb": _sb(H, "bfloat16"), "inc": _sb(H, "bfloat16"), "ycs": _sb(1024, "float32"),
            "pi": _sb(8, "int32"), "col": _sb(32, "float32"), "colb": _sb(16, "bfloat16"), "one": _sb(512, "bfloat16"),
-           "bt": _sb(8, "bfloat16"), "cu": _sb(512, "bfloat16"), "wi": _sb(16, "int32"), "wa": _sb(48, "float32"),
+           "bt": _sb(8, "bfloat16"), "cu": _sb(516, "bfloat16"), "wi": _sb(16, "int32"), "wa": _sb(48, "float32"),
            "wtab": _sb(16, "bfloat16"), "ee": _sb(2 * LC, "float32"), "li": _sb(4 * LC, "int32"), "mg": _sb(8 * 128, "bfloat16"),
            "run": _sb(G, "bfloat16"),
-           "qlo": _sb(5 * LC, "int32"), "qhi": _sb(5 * LC, "int32"), "qq0": _sb(5 * LC, "float32"), "qq1": _sb(4 * LC, "float32"),
+           "qlo": _sb(5 * LC, "int32"), "qhi": _sb(5 * LC, "int32"), "qq": _sb(15 * LC, "float32"),
            "gg": _sb(5 * LC, "bfloat16"), "sndi": _sb(SC, "int32"), "sndu": _sb(SC, "uint16"), "soff": _sb(SC, "uint16"),
-           "lv": _sb(2 * W, "bfloat16"), "idn": _sb(128, "bfloat16"), "idf": _sb(128, "float32"),
+           "less": _sb(W, "bfloat16"), "lv": _sb(2 * LC, "bfloat16"), "idn": _sb(128, "bfloat16"), "nil": _sb(128, "bfloat16"), "idf": _sb(128, "float32"),
            "ps": ("psum", [128, 4096], "float32")}
 SCRATCH.update({n: _sb(V, "bfloat16") for n in ("zc", "zl", "wsb", "lr", "pb", "ph", "pl", "dd", "aa", "tt", "sg", "x2")})
 SCRATCH.update({n: _sb(144, "bfloat16") for n in ("b0", "bv", "be", "bo", "bz", "bi", "bm")})
@@ -33,14 +35,19 @@ SCRATCH.update({n: _sb(128, "bfloat16") for n in DIAG})
 SCRATCH.update({n: _sb(LC, "float32") for n in ("t3", "pf")})
 SCRATCH.update({n: _sb(LC, "uint16") for n in ("cu16", "off", "sel")})
 SCRATCH.update({n: _sb(LC, "bfloat16") for n in ("bias", "curb", "nr", "pn", "posh", "c0b", "l63", "arm", "cb4", "par")})
-SCRATCH.update({n: _sb(SC, "float32") for n in ("sndp", "mpos", "s2")})
-SCRATCH.update({n: _sb(SC, "bfloat16") for n in ("ka", "kb")})
-SEMAPHORES = (["qv", "qs", "qp", "qg"] + ["d%d" % k for k in range(48)]
+SCRATCH.update({n: _sb(SC, "float32") for n in ("sndp", "s2")})
+SCRATCH.update({n: _sb(SC, "bfloat16") for n in ("ka", "kb", "mph", "mpl")})
+SEMAPHORES = (["qv", "qs", "qp", "qg"] + ["d%d" % k for k in range(72)]
               + ["arr%d" % k for k in range(2 * RO)] + ["loc%d" % k for k in range(2 * RO)])
 
-PLAN = {"D": "svsv", "C": "ssss", "T": ["svvh"] * 5, "W": ["vvsv"] * 5, "X": ["svss"] * 5, "X2": "ssss", "PK": 2, "VK": 1, "QP": "ppp",
-        "DEC": 1, "YC": "sss", "R1": "dddd", "X20": "ssss", "FB": "svh", "SPLIT": 1, "GS": [24, 12], "TRY": 10000, "SHAKE": 8, "NEAR": 20, "FAST": 1, "HEAT": 0.0, "SEED": 12345}
-CY, PCY, FIX, LAT, GA, FAR_US, NEAR_US = 1.0e-3, 0.5e-3, 0.06, 0.10, 1.5, 4.5, 3.5
+PLAN = {"D": "svsv", "C": "ssss", "T": ["svvh"] * 4 + ["vvvh"], "W": ["vvsv"] * 5, "X": ["svss"] * 4 + ["hsss"], "X2": ["ssss"] * 4,
+        "PK": ["-2-2"] * 5, "WH": [["", "WD", "", ""]] * 4 + [["", "WDT", "T", ""]], "SAFE": 1, "DQ": "gggyyyy", "BANK": "012021", "ARM": "v", "VK": ["1111"] * 5, "QV": [],
+        "DEC": 2, "SW": "2222", "YC": "svs", "R1": "dddd", "X20": "svsv", "FB": "svh", "SPLIT": 1, "GS": [24, 12], "TRY": 1000, "SHAKE": 8, "NEAR": 20, "FAST": 1, "HEAT": [0.08, 0.04, 0.03, 0.02, 0.02, 0.015],
+        "ROUNDS": 6, "STEPS": [7000] * 6, "SEED": 12345}
+BETWEEN = [[(-1, 1), (0, 0)], [(-1, 2), (0, 1), (1, 0), (-1, 3)], [(0, 2), (1, 1), (2, 0), (-1, 4), (0, 3)], [(1, 2), (2, 1), (3, 0)]]
+CY, PCY, FIX, LAT, GA, FAR_US, NEAR_US = 0.92e-3, 0.46e-3, 0.042, 0.12, 1.58, 3.0, 2.2
+SFX, MFX, GT, GFX, ADD_US = 0.015, 0.0, 1.0, 0.1, 2.3
+SPEEDS = [(0.92, 1.2), (1.28, 1.95)]
 ORDER = []
 
 
@@ -64,8 +71,8 @@ def build(g, core, T, topo, ops):
     def IND(win, offs):
         return (win[0].indirect(offs[0]), win[1] + offs[1], 16 * offs[2], win[3], "ind")
 
-    def add(q, fn, reads, writes, dur, kind="c", extra=None):
-        ops.append({"q": q, "fn": fn, "r": reads, "w": writes, "dur": dur, "kind": kind, "x": extra,
+    def add(q, fn, reads, writes, dur, kind="c", extra=None, ind=False):
+        ops.append({"q": q, "fn": fn, "r": reads, "w": writes, "dur": dur, "kind": kind, "x": extra, "ind": ind,
                     "tag": len(ops) - first[0] if first[0] else -len(ops)})
         return len(ops) - 1
 
@@ -85,15 +92,16 @@ def build(g, core, T, topo, ops):
             fn = lambda: g.vector.tensor_scalar(out[0], in0[0], a1, None, op0)
         else:
             fn = lambda: g.vector.tensor_scalar(out[0], in0[0], a1, a2, op0, op1)
-        return add("v", fn, in0[1] + r1 + r2, out[1], vcost(out[2], f))
+        return add("v", fn, in0[1] + r1 + r2, out[1], vcost(out[2], f), ind=in0[4] == "ind")
 
     def tt(out, in0, in1, op):
-        f = GA if in0[4] == "ind" else (1.0 if "ps" in (in0[4], in1[4]) else 2.0)
-        return add("v", lambda: g.vector.tensor_tensor(out[0], in0[0], in1[0], op), in0[1] + in1[1], out[1], vcost(out[2], f))
+        f = max(GA, GT) if in0[4] == "ind" else (1.0 if "ps" in (in0[4], in1[4]) else 2.0)
+        return add("v", lambda: g.vector.tensor_tensor(out[0], in0[0], in1[0], op), in0[1] + in1[1], out[1], vcost(out[2], f),
+                   ind=in0[4] == "ind")
 
     def cp(out, in0):
         f = GA if in0[4] == "ind" else (0.5 if two(out, in0) else 1.0)
-        return add("v", lambda: g.vector.tensor_copy(out[0], in0[0]), in0[1], out[1], vcost(out[2], f))
+        return add("v", lambda: g.vector.tensor_copy(out[0], in0[0]), in0[1], out[1], vcost(out[2], f), ind=in0[4] == "ind")
 
     def ms(out, val):
         return add("v", lambda: g.vector.memset(out[0], val), [], out[1], vcost(out[2], 0.5 if two(out) else 1.0))
@@ -106,7 +114,8 @@ def build(g, core, T, topo, ops):
     def act(out, in0, func, bias=0.0, scale=1.0):
         ab, rb = sc(bias); as_, rs = sc(scale)
         f = GA if in0[4] == "ind" else 1.0
-        return add("s", lambda: g.scalar.activation(out[0], in0[0], func, bias=ab, scale=as_), in0[1] + rb + rs, out[1], vcost(out[2], f))
+        return add("s", lambda: g.scalar.activation(out[0], in0[0], func, bias=ab, scale=as_), in0[1] + rb + rs, out[1],
+                   vcost(out[2], f) + SFX, ind=in0[4] == "ind")
 
     def move(e, out, in0, plus=0.0):
         return ts(out, in0, plus, ALU.add) if e == "v" else act(out, in0, ACT.Identity, bias=plus)
@@ -119,7 +128,7 @@ def build(g, core, T, topo, ops):
             return ins
         rd, wr, dur = [], [], FIX
         for o, l, r, st, sp in items:
-            rd += l[1] + r[1]; wr += o[1]; dur += PCY * max(min(64, l[2]), r[2]) * (4 if r[3] == "float32" else 1)
+            rd += l[1] + r[1]; wr += o[1]; dur += MFX + PCY * max(min(64, l[2]), r[2]) * (4 if r[3] == "float32" else 1)
         return add("p", fn, sorted(set(rd)), sorted(set(wr)), dur)
 
     made = set()
@@ -130,7 +139,10 @@ def build(g, core, T, topo, ops):
             if not isinstance(t, int) and t[0] in DIAG and t[0] not in made:
                 made.add(t[0])
                 keep, first[0] = first[0], 0
-                act(A(t[0]), A("idn"), ACT.Identity, scale=DIAG[t[0]])
+                if t[0] in EARLY:
+                    act(A(t[0]), A("idn"), ACT.Identity, scale=DIAG[t[0]])
+                else:
+                    asel(A(t[0]), A("nil"), [[-1, 128]], ALU.not_equal, 0, 1, DIAG[t[0]])
                 first[0] = keep + 1 if keep else 0
             l, r = (A("mg", 128 * t, 128 * t + 128, p1=1), A("one", 0, out[2], p1=1)) if isinstance(t, int) else (A(t[0]), t[1])
             items.append((out, l, r, start and n == 0, stop and n == len(terms) - 1))
@@ -141,15 +153,17 @@ def build(g, core, T, topo, ops):
             fn = lambda: g.iota(out[0], pattern, base, cm)
         else:
             fn = lambda: g.iota(out[0], pattern, base, cm, allow_small_or_imprecise_dtypes=True)
-        return add("g", fn, [], out[1], 0.13 + 2 * CY * out[2])
+        return add("g", fn, [], out[1], GFX + 0.13 + 2 * CY * out[2])
 
     def fill(out, val):
         return iota(out, [[0, out[2]]], int(val), 0)
 
-    def asel(out, in0, pattern, cmp_, base, cm):
-        return add("g", lambda: g.affine_select(out[0], in0[0], pattern, cmp_, 0.0, base, cm), in0[1], out[1], 0.17 + 2 * CY * out[2])
+    def asel(out, in0, pattern, cmp_, base, cm, other=0.0):
+        return add("g", lambda: g.affine_select(out[0], in0[0], pattern, cmp_, other, base, cm), in0[1], out[1], GFX + 0.17 + 2 * CY * out[2])
 
     def dma(q, out, in_, reads, writes, nbytes):
+        if q == "g":
+            return add(q, lambda: g.dma_start(out, in_), reads, writes, 2.5 + nbytes / 200e3, "gdma")
         eng = g.sync if q == "y" else g.scalar
         return add(q, lambda: eng.dma_start(out, in_), reads, writes, 2.0 + nbytes / 200e3, "dma")
 
@@ -181,8 +195,10 @@ def build(g, core, T, topo, ops):
 
     dma("s", T.zc[0:8, :], T.c0[:, :], [], reg("zc", 0, V), 20e3)
     dma("s", T.zl[0:8, :], T.x[15::16, :], [], reg("zl", 0, V), 20e3)
-    cuts = [0, W // 2] + [W * k for k in range(1, NCH + 1)]
-    loads = [dma("y", T.nbt[:, a:b], T.nb[:, a:b], [], reg("nbt", a, b), 512 * (b - a)) for a, b in zip(cuts, cuts[1:])]
+    cuts = {"1": (0, W), "2": (0, W // 2, W), "3": (0, W // 4, W // 2, W)}
+    pieces = [[(k * W + a, k * W + b) for a, b in zip(cuts[c], cuts[c][1:])] for k, c in enumerate(PLAN["SW"])]
+    loads = [dma("y", T.nbt[:, a:b], T.nb[:, a:b], [], reg("nbt", a, b), 512 * (b - a))
+             for a, b in pieces[0] + pieces[1] + [(2 * W, 3 * W), (3 * W, V)]]
     loads.append(dma("y", T.xb0[:, OWN:GH], T.x[:, :], [], reg("xb0", OWN, GH), 256 * V))
     loads.append(dma("y", T.xb0[:, GH:GH + H], T.gx[:, :], [], reg("xb0", GH, GH + H), 256 * H))
     for j, b in enumerate(blocks(rank)):
@@ -198,48 +214,55 @@ def build(g, core, T, topo, ops):
     ts(C("lev"), A("pi", 1, 2), 15.0, ALU.is_equal)
     ts(C("we"), A("pi", 2, 3), -0.25, ALU.mult, 0.25, ALU.add)
     ts(C("wo"), A("pi", 2, 3), 0.25, ALU.mult)
-    ts(C("pw"), A("pi", 1, 2), float(W), ALU.add)
-    ts(C("pn"), A("pi", 1, 2), -2048.0, ALU.add)
-    ts(C("kb"), A("pi", 1, 2), -1.0, ALU.mult, -18.0, ALU.add)
-    BIG, LO = DIAG["idb"], 704.0
+    act(C("pw"), C("pm"), ACT.Identity, bias=float(W))
+    act(C("pn"), C("pm"), ACT.Identity, bias=-2048.0)
+    act(C("kb"), C("pm"), ACT.Identity, bias=-18.0, scale=-1.0)
+    BIG, LO = DIAG["id8"], 704.0
     percol = {"f1": (1.0, 0.0), "wv": (-256.0, -7 * 256.0), "wi": (14 * BIG, -BIG)}
     percol.update({"r%d%d" % (shift[k], PLAN["R1"][k] == "d"): (LO + 64 + shift[k], 64.0 + shift[k] + (PLAN["R1"][k] == "d")) for k in range(NCH)})
-    looks = set(zip(PLAN["D"], PLAN["C"]))
+    assert ("e", "v") not in zip(PLAN["D"], PLAN["C"])
+    looks = set(zip(PLAN["D"].replace("e", "v"), PLAN["C"]))
     if ("v", "s") in looks:
         percol["f2"] = (-2.0, 0.0)
     if ("s", "v") in looks:
         percol["c1"] = (-1.0, 0.0)
     for k, nm in enumerate(percol):
         cols[nm] = 10 + k
-        ts(C(nm), C("lev"), percol[nm][1] - percol[nm][0], ALU.mult, percol[nm][0], ALU.add)
+        act(C(nm), C("lev"), ACT.Identity, bias=percol[nm][0], scale=percol[nm][1] - percol[nm][0])
     if set(PLAN["R1"]) != {"d"}:
-        cp(CB(4), C("lev"))
-    if "v" in PLAN["D"]:
-        ts(CB(0), C("f1"), 2.0 ** 27, ALU.mult)
-        ts(CB(1), C("f1"), 2.0 ** 27, ALU.mult, 1.0, ALU.max)
+        act(CB(4), C("lev"), ACT.Identity)
+    if set(PLAN["D"]) != {"s"}:
+        act(CB(0), C("f1"), ACT.Identity, scale=2.0 ** 27)
+        act(CB(1), C("f1"), ACT.Identity, bias=1.0, scale=2.0 ** 27)
     if ("v", "v") in looks:
-        ts(CB(2), C("lev"), 1.0, ALU.add)
-        ts(CB(3), C("f1"), 2.0, ALU.add)
+        act(CB(2), C("lev"), ACT.Identity, bias=1.0)
+        act(CB(3), C("f1"), ACT.Identity, bias=2.0)
     if "s" in PLAN["D"]:
         cols.update({"a1": 7, "a2": 8})
-        ts(C("a1"), C("f1"), 1.5 * 2 ** 27, ALU.mult)
-        ts(C("a2"), C("f1"), 1.5 * 2 ** 27, ALU.mult, -1.25, ALU.add)
+        act(C("a1"), C("f1"), ACT.Identity, scale=1.5 * 2 ** 27)
+        act(C("a2"), C("f1"), ACT.Identity, bias=-1.25, scale=1.5 * 2 ** 27)
 
     ms(A("one"), 1.0)
+    ms(A("nil"), 0.0)
     fill(A("bz"), 0)
     asel(A("bz", 15, 143, 16), A("one", 0, 8), [[-1, 8]], ALU.is_equal, 0, 1)
     fill(A("b0"), 0)
     asel(A("bt"), A("one", 0, 8), [[-16, 8]], ALU.is_ge, 0, 1)
     asel(A("b0", 15, 143, 16), A("bt"), [[16, 8]], ALU.is_ge, 15, -1)
     asel(A("idn"), A("one", 0, 128), [[-1, 128]], ALU.is_equal, 0, 1)
-    if "p" in PLAN["QP"]:
+    if True:
         asel(A("idf"), A("one", 0, 128), [[-1, 128]], ALU.is_equal, 0, 1)
     for nm, c in (("be", "we"), ("bo", "wo"), ("bv", "wv"), ("bi", "wi")):
         act(A(nm), A("b0"), ACT.Identity, scale=C(c))
     act(A("run"), A("one", 0, G), ACT.Identity, scale=C("lev"))
     M64, M8K, M16, MID, MSG = 0, 2, 4, 6, 7
     for k, val in enumerate((1.5 * 2 ** 29, -1.5 * 2 ** 29, 1.5 * 2 ** 36, -1.5 * 2 ** 36, 1.5 * 2 ** 27, -1.5 * 2 ** 27, 31.5, 12288.0)):
-        ms(A("mg", 128 * k, 128 * k + 128, p1=32), val)
+        if k == MID and not any(t != "v" and x != "s" or t != "s" and w == "r" for p in zip(PLAN["T"], PLAN["W"], PLAN["X"]) for t, w, x in zip(*p)):
+            continue
+        if k // 2 * 2 == M16:
+            ms(A("mg", 128 * k, 128 * k + 128, p1=32), val)
+        else:
+            asel(A("mg", 128 * k, 128 * k + 128, p1=32), A("nil", p1=32), [[0, 128]], ALU.is_gt, 0, 0, val)
     iota(A("wi"), [[-1, 16]], 128, 1)
     ts(A("wi"), A("wi"), 15, ALU.bitwise_and)
     ts(A("wa", 0, 16), A("wi"), 1.5, ALU.is_le, -255.0, ALU.mult)
@@ -251,23 +274,24 @@ def build(g, core, T, topo, ops):
     for k in range(NCH):
         fill(A("tw", k * TW, k * TW + 16), shift[k])
     for s in sorted(set(shift[k] for k in range(NCH) if PLAN["R1"][k] == "d")):
-        fill(A("lv", int(s) // 2 * W, int(s) // 2 * W + W), 64 + s)
-    iota(A("mpos"), [[16, SC]], 0, 0)
-    asel(A("cu"), A("one"), [[-1, 16], [-16, 32]], ALU.is_equal, 0, 1)
+        fill(A("lv", int(s) // 2 * LC, int(s) // 2 * LC + LC), 64 + s)
+    iota(A("mph"), [[16, SC]], 0, 0)
+    act(A("mpl"), A("one", 0, SC), ACT.Identity, scale=C("pm"))
+    fill(A("cu", 0, 4), 0)
+    asel(A("cu", 4, 516), A("one"), [[-1, 16], [-16, 8], [-128, 4]], ALU.is_equal, 0, 1)
     marks = []
     for d in range(N - 1):
         cut = {"v": GC, "s": 0, "h": GC // 2}[PLAN["FB"][d]]
         marks.append([m for m in (("v", d * GC, d * GC + cut), ("s", d * GC + cut, (d + 1) * GC)) if m[2] > m[1]])
         for e, la, lb in marks[d]:
             if e == "v":
-                fill(A("ka", la, lb), -227); fill(A("kb", la, lb), 0)
+                fill(A("ka", la, lb), 284); fill(A("kb", la, lb), 1)
             else:
-                iota(A("ka", la, lb), [[-16, lb - la]], 0, 0)
+                iota(A("ka", la, lb), [[-16, lb - la]], 512, 0)
                 act(A("kb", la, lb), A("one", 0, lb - la), ACT.Identity, scale=C("kb"))
 
     ZC, ZL = PS(7, 0, LC), PS(7, LC, 2 * LC)
-    for hf in range(2):
-        la, lb = hf * LC // 2, (hf + 1) * LC // 2
+    for la, lb in ((0, CW), (CW, LC)):
         mm(listmm(PS(7, la, lb), "bz", "zc", 16 * la, 16 * lb, k=8))
         cp(A("cu16", la, lb), PS(7, la, lb))
     act(A("c0b"), ZC, ACT.Identity)
@@ -281,11 +305,14 @@ def build(g, core, T, topo, ops):
 
     def failpos(n, Z, P):
         mm(acc(Z, [("idn", A("l63")), ("idm", A("c0b"))] + [("idg", Q("gg", j)) for j in range(n)]))
-        ts(A("arm"), Z, n / 2 - 15.0, ALU.is_equal, float(W), ALU.mult)
+        if PLAN["ARM"] == "v":
+            ts(A("arm"), Z, n / 2 - 15.0, ALU.is_equal, float(W), ALU.mult)
+        else:
+            act(A("arm"), Z, ACT.Abs, bias=15.0 - n / 2)
+            act(A("arm"), A("arm"), ACT.Relu, bias=float(W), scale=-float(W))
         mm(acc(P, [("idn", A("posh")), ("idn", A("arm"))]))
         act(A("pf"), P, ACT.Identity, bias=C("pw"))
     failpos(0, ZC, ZL)
-    ts(A("mpos"), A("mpos"), C("pm"), ALU.add)
     cp(A("sndu"), A("sndi"))
     ts(A("sndp"), A("sndi"), float(OWN), ALU.add)
 
@@ -310,39 +337,49 @@ def build(g, core, T, topo, ops):
                                         remote_sem=T.sem["arr%d" % n], src=T[src][:, so:so + G], dst=T[dst][:, do:do + G]))
             tot += len(es); rd += reg(src, so, so + G); wr += reg(dst, do, do + G)
         us = FAR_US if off else NEAR_US
-        s = add("g", lambda: g.remote_dma_fused(tr, local_sem=T.sem["loc%d" % n]), rd, [], us - 1.0, "send", ("loc%d" % n, tot))
+        s = add("g", lambda: g.remote_dma_fused(tr, local_sem=T.sem["loc%d" % n]), rd + [("added", 0, NCH)], [], us - 1.0, "send", ("loc%d" % n, tot))
         add("x", None, [], wr, us, "arrive", ("arr%d" % n, tot, s))
 
     send(2 * RO - 1, [((rank - b - 1) % N, GH + b * G, blocks((rank - b - 1) % N).index(b) * G) for b in range(N - 1)], "xb0", "xb1")
 
     def shifted(e, k, src):
-        if PLAN["D"][k] == "v":
-            move(e, A("x2", k * W, (k + 1) * W), A(src, OWN + k * W, OWN + (k + 1) * W), -2.0)
+        a, b = k * W, (k + 1) * W
+        if PLAN["D"][k] == "v" and e != "d":
+            move(e, A("x2", a, b), A(src, OWN + a, OWN + b), -2.0)
+        elif PLAN["D"][k] == "v":
+            dma("y", T.x2[:, a:b], T.less[:, :], reg("less", 0, W), reg("x2", a, b), 256 * W)
+            add("g", lambda: g.dma_start(T.x2[:, a:b], T[src][:, OWN + a:OWN + b], accum_op=ALU.add), reg(src, OWN + a, OWN + b),
+                reg("x2", a, b) + ([("added", k, k + 1)] if PLAN["SAFE"] else []), 2.0 + ADD_US, "gdma")
+    if "d" in PLAN["X20"] + "".join(PLAN["X2"]):
+        fill(A("less"), -2)
     for k in range(NCH):
         shifted(PLAN["X20"][k], k, "xb0")
 
     n = W // 2
-    for sub in range(2 * NCH):
-        k, hf = sub // 2, sub % 2
-        a, b = sub * n, (sub + 1) * n
-        HP, WP, RP = PS(sub % 2, 0, n), PS(2, 0, n), PS(3, 0, n)
+    for k in range(NCH):
         byd = PLAN["R1"][k] == "d"
         r0 = k * TW + 16 + W
-        act(A("wsb", a, b), IND(A("wtab"), A("cu16", a // 16, b // 16)), ACT.Identity)
-        ts(HP, A("nbt", a, b), 1.5 * 2 ** 31, ALU.add, 1.5 * 2 ** 31, ALU.subtract)
-        tt(A("lr", a, b), A("nbt", a, b), HP, ALU.subtract)
-        tt(A("ph", a, b), HP, A("wsb", a, b), ALU.mult)
-        act(A("pb", a, b), A("lr", a, b), ACT.Identity, bias=LO - 1.5)
-        mm(acc(WP, [("idn", A("wsb", a, b))]))
-        tt(A("pl", a, b), WP, A("pb", a, b), ALU.mult)
-        mm(acc(RP, [("idn", A("lr", a, b)), ("idm", A("pb", a, b))]))
-        act(A("tw", r0 + byd * W + hf * n, r0 + byd * W + hf * n + n), RP, ACT.Identity, bias=C("r%d%d" % (shift[k], byd)), scale=C("f1"))
-        if not hf:
-            continue
+        halves = [(k * W, k * W + n), (k * W + n, (k + 1) * W)]
+        for a, b in pieces[k]:
+            HP, WP = A("ps", 512 - n + a - k * W, 512 - n + b - k * W), A("ps", 1536 - n + a - k * W, 1536 - n + b - k * W)
+            act(A("wsb", a, b), IND(A("wtab"), A("cu16", a // 16, b // 16)), ACT.Identity)
+            ts(HP, A("nbt", a, b), 1.5 * 2 ** 31, ALU.add, 1.5 * 2 ** 31, ALU.subtract)
+            tt(A("lr", a, b), A("nbt", a, b), HP, ALU.subtract)
+            tt(A("ph", a, b), HP, A("wsb", a, b), ALU.mult)
+            act(A("pb", a, b), A("lr", a, b), ACT.Identity, bias=LO - 1.5)
+            for lo in range(a, b, n):
+                hi = min(b, lo + n)
+                mm(acc(A("ps", 1536 - n + lo - k * W, 1536 - n + hi - k * W), [("idn", A("wsb", lo, hi))]))
+            tt(A("pl", a, b), WP, A("pb", a, b), ALU.mult)
+        for a, b in halves:
+            RP, r1 = PS(7, 0, n), r0 + byd * W + a - k * W
+            mm(acc(RP, [("idn", A("lr", a, b)), ("idm", A("pb", a, b))]))
+            act(A("tw", r1, r1 + n), RP, ACT.Identity, bias=C("r%d%d" % (shift[k], byd)), scale=C("f1"))
         if byd:
-            lv = int(shift[k]) // 2 * W
+            lv = int(shift[k]) // 2 * LC
             dma("y", T.tw[:, r0:r0 + W], T.tw[:, r0 + W:r0 + 2 * W], reg("tw", r0 + W, r0 + 2 * W), reg("tw", r0, r0 + W), 256 * W)
-            dma("y", T.tw[15::16, r0:r0 + W], T.lv[15::16, lv:lv + W], reg("lv", lv, lv + W), reg("tw", r0, r0 + W), 16 * W)
+            ops[-1]["behind"] = loads[-1]
+            dma(PLAN["DQ"][0], T.tw[15::16, r0:r0 + W], T.lv[0:32, lv:lv + LC], reg("lv", lv, lv + LC), reg("tw", r0, r0 + W), 16 * W)
         else:
             move(PLAN["R1"][k], A("tw", r0 + W, r0 + 2 * W), A("tw", r0, r0 + W), CB(4))
         per = NCH // PLAN["DEC"]
@@ -360,40 +397,49 @@ def build(g, core, T, topo, ops):
             ee = A("ee", j * LC + la, j * LC + la + m)
             act(ee, sums(2 * j, 0, m), ACT.Identity)
             for t in range(2):
-                tt(A("li", (2 * t + j) * LC + la, (2 * t + j) * LC + la + m), sums(2 * j + 1, 0, m), ee, ALU.min if t else ALU.max)
+                tt(A("li", (2 * j + t) * LC + la, (2 * j + t) * LC + la + m), sums(2 * j + 1, 0, m), ee, ALU.min if t else ALU.max)
         for dst, j, mask in (("qhi", 0, 127 * 64), ("qlo", 1, 255)):
-            ts(A(dst, la, la + m), A("li", j * LC + la, j * LC + la + m), mask, ALU.bitwise_and)
-        tt(A("qq0", la, la + m), A("qlo", la, la + m), A("qhi", la, la + m), ALU.add)
-        ts(A("off", la, la + m), A("qq0", la, la + m), LO / 4, ALU.subtract)
-    for t in range(1, RO):
+            ts(A(dst, la, la + m), A("li", 2 * j * LC + la, 2 * j * LC + la + m), mask, ALU.bitwise_and)
+        tt(A("qq", la, la + m), A("qlo", la, la + m), A("qhi", la, la + m), ALU.add)
+        ts(A("off", la, la + m), A("qq", la, la + m), LO / 4, ALU.subtract)
+
+    def kept(r, t):
+        return Q("qq", r * RO - r * (r - 1) // 2 + t)
+
+    def place(t):
         for dst, j, mask in (("qhi", 0, 127 * 64), ("qlo", 1, 255)):
             if t > 1:
-                ts(Q(dst, t), Q("li", 2 * (t % 2) + j), 8 * (t // 2), ALU.arith_shift_right, mask, ALU.bitwise_and)
+                ts(Q(dst, t), Q("li", 2 * j + t % 2), 8 * (t // 2), ALU.arith_shift_right, mask, ALU.bitwise_and)
             else:
-                ts(Q(dst, t), Q("li", 2 * t + j), mask, ALU.bitwise_and)
-        tt(Q("qq0", t), Q("qlo", t), Q("qhi", t), ALU.add)
+                ts(Q(dst, t), Q("li", 2 * j + t), mask, ALU.bitwise_and)
+        tt(kept(0, t), Q("qlo", t), Q("qhi", t), ALU.add)
 
     UB = 7 * 512 - 2 * CW
     slot = [0]
 
     def pair():
-        p = 1024 * slot[0] + 512 - n
-        slot[0] = (slot[0] + 1) % 3
-        return p
+        slot[0] += 1
+        return 1024 * int(PLAN["BANK"][slot[0] - 1]) + 512 - n
 
-    def look(k, cur):
+    def look(s, k, cur):
         ca, cb = k * CW, (k + 1) * CW
         a, b = 16 * ca, 16 * cb
         CC = A("tw", k * TW + 16, k * TW + 16 + W)
-        pd = pair() if PLAN["D"][k] == "s" else 0
-        for lo, hi in ((a, a + n), (a + n, b)):
+        pd = pair() if PLAN["D"][k] != "v" else 0
+        for lo, hi in ([(a, b)] if "D" in PLAN["WH"][s][k] else [(a, a + n), (a + n, b)]):
             src = IND(A(cur, OWN, GH + H), A("off", lo // 16, hi // 16))
-            if PLAN["D"][k] == "s":
+            if PLAN["D"][k] != "v":
                 act(A("dd", lo, hi), src, ACT.Identity)
-                mm(acc(A("ps", pd + lo - a, pd + hi - a), [("id5", A(cur, OWN + lo, OWN + hi))], stop=False))
-                mm(acc(A("ps", pd + lo - a, pd + hi - a), [("idp", A("dd", lo, hi))], start=False))
             else:
                 tt(A("dd", lo, hi), src, A("x2", lo, hi), ALU.subtract)
+        if PLAN["D"][k] != "v":
+            less, plus = ("id5", "idp") if PLAN["D"][k] == "s" else ("idm", "idn")
+            for lo, hi in ((a, a + n), (a + n, b)):
+                mm(acc(A("ps", pd + lo - a, pd + hi - a), [(less, A(cur, OWN + lo, OWN + hi))], stop=False))
+                mm(acc(A("ps", pd + lo - a, pd + hi - a), [(plus, A("dd", lo, hi))], start=False))
+        if PLAN["D"][k] == "e":
+            for lo, hi in ([(a, b)] if "E" in PLAN["WH"][s][k] else [(a, a + n), (a + n, b)]):
+                act(A("dd", lo, hi), A("ps", pd + lo - a, pd + hi - a), ACT.Identity, bias=2.0)
         if PLAN["D"][k] == "s":
             D = A("ps", pd, pd + W)
             ts(A("aa", a, b), D, C("a1"), ALU.add, C("a2"), ALU.is_equal)
@@ -412,34 +458,43 @@ def build(g, core, T, topo, ops):
         a = k * W
         eT, eW, eX = PLAN["T"][s][k], PLAN["W"][s][k], PLAN["X"][s][k]
         pb_ = pair()
-        for hf, (lo, hi) in enumerate([(a, a + n), (a + n, a + W)]):
-            P = A("ps", pb_ + lo - a, pb_ + hi - a)
+        halves = [(a, a + n), (a + n, a + W)]
+
+        def parts(stage, e):
+            if stage in PLAN["WH"][s][k] and "h" not in (e, eT):
+                return [(a, a + W, e == "v")]
+            return [(lo, hi, e == "v" or (e == "h" and lo == a)) for lo, hi in halves]
+        fused = [eT == "v" or (eT == "h" and lo == a) for lo, _ in halves]
+        for lo, hi, byv in parts("T", eT):
             src = IND(A("tw", k * TW, (k + 1) * TW), A("sel", lo // 16, hi // 16))
-            own, t_, sg, out = A(cur, OWN + lo, OWN + hi), A("tt", lo, hi), A("sg", lo, hi), A(new, OWN + lo, OWN + hi)
-            xv, plus = eX == "v" or (eX == "h" and hf == 0), 0.0
-            if eT == "v" or (eT == "h" and hf == 0):
-                tt(t_, src, A("x2", lo, hi) if shift[k] else own, ALU.add)
-                rest = t_
-                if eW == "r":
-                    mm(acc(P, [MID], stop=False))
-                    mm(acc(P, [("idm", t_), M64, M64 + 1] + ([] if xv else [("idn", t_)]), start=False))
-                else:
-                    move(eW, sg, t_, 12288 - 31.5)
-                    plus = 12288.0
-                    if xv:
-                        mm(acc(P, [MSG], stop=False))
-                    mm(acc(P, [("idm", sg)] + ([] if xv else [("idn", t_)]), start=not xv))
+            if byv:
+                tt(A("tt", lo, hi), src, A("x2", lo, hi) if shift[k] else A(cur, OWN + lo, OWN + hi), ALU.add)
             else:
-                act(t_, src, ACT.Identity, bias=32.5 - shift[k])
-                rest, plus = own, 31.5
+                act(A("tt", lo, hi), src, ACT.Identity, bias=32.5 - shift[k])
+        for lo, hi, byv in parts("W", eW):
+            if eW != "r" and fused[lo > a]:
+                move(eW, A("sg", lo, hi), A("tt", lo, hi), 12288 - 31.5)
+        for hf, (lo, hi) in enumerate(halves):
+            P = A("ps", pb_ + lo - a, pb_ + hi - a)
+            own, t_, xv = A(cur, OWN + lo, OWN + hi), A("tt", lo, hi), eX == "v" or (eX == "h" and hf == 0)
+            if not fused[hf]:
                 mm(acc(P, [("idm", own)], stop=False))
                 mm(acc(P, [("idm", t_), M64, M64 + 1, ("idn", t_), MID if xv else ("idn", own)], start=False))
-            if xv:
-                tt(out, P, rest, ALU.add)
+            elif eW == "r":
+                mm(acc(P, [MID], stop=False))
+                mm(acc(P, [("idm", t_), M64, M64 + 1] + ([] if xv else [("idn", t_)]), start=False))
             else:
-                act(out, P, ACT.Identity, bias=plus)
+                if xv:
+                    mm(acc(P, [MSG], stop=False))
+                mm(acc(P, [("idm", A("sg", lo, hi))] + ([] if xv else [("idn", t_)]), start=not xv))
+        for lo, hi, byv in parts("X", eX):
+            P, out = A("ps", pb_ + lo - a, pb_ + hi - a), A(new, OWN + lo, OWN + hi)
+            if byv:
+                tt(out, P, A("tt", lo, hi) if fused[lo > a] else A(cur, OWN + lo, OWN + hi), ALU.add)
+            else:
+                act(out, P, ACT.Identity, bias=31.5 if not fused[lo > a] else 0.0 if eW == "r" else 12288.0)
             if s == RO - 1:
-                dma("y", T.yx[:, lo:hi], T[new][:, OWN + lo:OWN + hi], out[1], [], 256 * n)
+                dma(PLAN["DQ"][3 + k], T.yx[:, lo:hi], T[new][:, OWN + lo:OWN + hi], out[1], [], 256 * (hi - lo))
 
     def cursors(s, h):
         la, lb = h * LC // 2, (h + 1) * LC // 2
@@ -447,30 +502,29 @@ def build(g, core, T, topo, ops):
         act(gl, A("ps", UB + la, UB + lb), ACT.Sign, bias=-K8 / 2)
         mm(acc(Z, [("idc", cl), ("idd", gl), M16, M16 + 1, ("idn", cl), ("idh", gl)]))
         move(PLAN["YC"][2], A("curb", la, lb), Z)
-        for j in range(4):
-            mm([(A("ps", (6 + h) * 512 + i, (6 + h) * 512 + n, 16, 32 * j, 32 * j + 32), A("cu", 32 * i, 32 * i + 32),
-                 A("curb", la + j * CW // 2, la + (j + 1) * CW // 2), True, True) for i in range(16)])
-        move(PLAN["YC"][h], A("ycs", h * n, (h + 1) * n), PS(6 + h, 0, n))
-        for j in range(4):
-            dma("y", T.yc[:, 16 * la + j * n:16 * la + (j + 1) * n], T.ycs[32 * j:32 * j + 8, h * n:(h + 1) * n],
-                reg("ycs", h * n, (h + 1) * n), [], 15e3)
+        for i0 in range(0, 16, 4):
+            mm([(A("ps", (6 + h) * 512 + i, (6 + h) * 512 + n, 16, 0, 32), A("cu", 4 + 32 * i - j, 36 + 32 * i - j),
+                 A("curb", la + j * CW // 2, la + (j + 1) * CW // 2), j == 0, j == 3) for i in range(i0, i0 + 4) for j in range(4)])
+        move(PLAN["YC"][h], A("ycs", h * n, (h + 1) * n, p1=32), A("ps", (6 + h) * 512, (6 + h) * 512 + n, p1=32))
+        dma(PLAN["DQ"][1 + h], T.yc[:, 16 * la:16 * lb], T.ycs[0:32, h * n:(h + 1) * n], reg("ycs", h * n, (h + 1) * n), [], 60e3)
 
     for s in range(RO):
         cur, new = xb[s % 2], xb[(s + 1) % 2]
         last = s == RO - 1
         first[0] = 0 if last else len(ops)
-        todo = []
+        todo, slot[0] = [], 0
         for k in range(NCH):
-            look(k, cur)
-            if (k + 1) % PLAN["VK"] == 0:
-                votes((k + 1 - PLAN["VK"]) * CW, (k + 1) * CW)
+            look(s, k, cur)
+            if PLAN["VK"][s][k] != "-":
+                votes((k + 1 - int(PLAN["VK"][s][k])) * CW, (k + 1) * CW)
             while todo:
                 change(s, todo.pop(0), cur, new)
-            if (k + 1) % PLAN["PK"] == 0:
-                ca, cb = (k + 1 - PLAN["PK"]) * CW, (k + 1) * CW
+            if PLAN["PK"][s][k] != "-":
+                k0 = k + 1 - int(PLAN["PK"][s][k])
+                ca, cb = k0 * CW, (k + 1) * CW
                 tt(A("t3", ca, cb), A("ps", UB + ca, UB + cb), A("pf", ca, cb), ALU.min)
                 cp(A("sel", ca, cb), A("t3", ca, cb))
-                todo = list(range(k + 1 - PLAN["PK"], k + 1))
+                todo = list(range(k0, k + 1))
             if last and k % 2:
                 cursors(s, k // 2)
         if not last:
@@ -479,6 +533,8 @@ def build(g, core, T, topo, ops):
             change(s, k, cur, new)
         if last:
             break
+        for k in range(NCH):
+            shifted(PLAN["X2"][s][k], k, new)
         for j, (d0, d1) in enumerate(sends):
             la, lb = d0 * GC, d1 * GC
             for d in range(d0, d1):
@@ -489,11 +545,11 @@ def build(g, core, T, topo, ops):
                     else:
                         act(A("mb", 16 * ma, 16 * mb), src, ACT.Sign, bias=-63.5)
             U2 = PS(6 + j, 128 * j + la, 128 * j + lb)
-            mm(acc(U2, [("idb", A("ka", la, lb)), ("idb", A("kb", la, lb))], stop=False))
+            mm(acc(U2, [("id8", A("ka", la, lb)), ("id8", A("kb", la, lb))], stop=False))
             for d in range(d0, d1):
                 scan(A("inc", d * G, (d + 1) * G), A("mb", d * G, (d + 1) * G))
-            mm(listmm(U2, "bi", "inc", 16 * la, 16 * lb, start=False))
-            tt(U2, U2, A("mpos", la, lb), ALU.max)
+            mm(listmm(U2, "bi", "inc", 16 * la, 16 * lb, start=False, stop=False)
+               + acc(U2, [M8K, M8K + 1, ("idn", A("mph", la, lb)), ("idn", A("mpl", la, lb))], start=False))
             tt(A("s2", la, lb), U2, A("sndp", la, lb), ALU.min)
             cp(A("soff", la, lb), A("s2", la, lb))
             hs = la + PLAN["GS"][j]
@@ -502,33 +558,28 @@ def build(g, core, T, topo, ops):
             if lb > hs:
                 act(A(cur, 16 * hs, 16 * lb), IND(A(new, 0, GH), A("soff", hs, lb)), ACT.Identity)
             send(2 * s + j, [((rank + b + 1) % N, d * G, GH + b * G) for d, b in enumerate(blocks(rank)) if d0 <= d < d1], cur, new)
-        for k in range(NCH):
-            shifted(PLAN["X2"][k], k, new)
         first[0] = 0
-        q0, q1, left = "qq%d" % (s % 2), "qq%d" % ((s + 1) % 2), RO - 1 - s
-        p0, p1 = 1024 * slot[0], 1024 * ((slot[0] + 1) % 3)
-        for t0, t1 in ((0, 1), (1, left)):
-            for t in range(t0, t1):
-                cut = [t * LC] + ([512] if t * LC < 512 < (t + 1) * LC else []) + [(t + 1) * LC]
-                for lo, hi in zip(cut, cut[1:]):
-                    mm(acc(A("ps", p0 + lo, p0 + hi), ([("idf", A(q0, lo, hi))] if PLAN["QP"][t0 > 0] == "p" else [])
-                           + [("idq", A("gg", (s - t) * LC + lo, (s - t) * LC + hi))]))
-            if t1 > t0:
-                QP = A("ps", p0 + t0 * LC, p0 + t1 * LC)
-                if PLAN["QP"][t0 > 0] == "v":
-                    tt(QP, QP, Q(q0, t0, t1 - t0), ALU.add)
-                tt(Q(q1, t0, t1 - t0), QP, Q(q0, t0 + 1, t1 - t0), ALU.min)
-            if t0 == 0:
-                OF = A("ps", p1, p1 + LC)
-                mm(acc(OF, ([("idf", Q(q1, 0))] if PLAN["QP"][2] == "p" else []) + [("idk", Q("gg", j)) for j in range(s + 1)]))
-                if PLAN["QP"][2] == "v":
-                    tt(OF, OF, Q(q1, 0), ALU.add)
-                ts(A("off"), OF, K8 * (s + 1) / 2 - LO / 4, ALU.add)
-        failpos(s + 1, A("ps", p1 + 512, p1 + 512 + LC), A("ps", p1 + 512 + LC, p1 + 512 + 2 * LC))
+        free = 2 * int(PLAN["BANK"][2])
+        spare = [PS(free, 0, LC), PS(free + 1, 0, LC), PS(7, LC, 2 * LC), PS(6, 128, 128 + LC)]
+        failpos(s + 1, spare[3], spare[3])
+        for j, (r, t) in enumerate(BETWEEN[s]):
+            P = spare[j % 3]
+            if r < 0:
+                place(t)
+                continue
+            if (r, t) in PLAN["QV"]:
+                mm(acc(P, [("idq", Q("gg", r))]))
+                tt(P, P, kept(r, t), ALU.add)
+            else:
+                mm(acc(P, [("idf", kept(r, t)), ("idq", Q("gg", r))]))
+            tt(kept(r + 1, t), P, kept(r, t + 1), ALU.min)
+            if t == 0:
+                P = spare[(j + 1) % 3]
+                mm(acc(P, [("idf", kept(r + 1, 0))] + [("idk", Q("gg", j)) for j in range(s + 1)]))
+                ts(A("off"), P, K8 * (s + 1) / 2 - LO / 4, ALU.add)
         if s == RO - 2:
-            Z = A("ps", p1 + LC, p1 + 2 * LC)
-            mm(acc(Z, [("idn", A("c0b"))] + [("idh", Q("gg", j)) for j in range(s + 1)]))
-            act(A("cb4"), Z, ACT.Identity, bias=RO / 2)
+            mm(acc(spare[3], [("idn", A("c0b"))] + [("idh", Q("gg", j)) for j in range(s + 1)]))
+            act(A("cb4"), spare[3], ACT.Identity, bias=RO / 2)
 
 
 def depend(ops):
@@ -551,35 +602,133 @@ def depend(ops):
         o["d"] = deps
 
 
-def lay(ops, before, after, first, key):
+def lay(ops, before, after, first, key, held={}):
     n = len(ops)
     left = [len(before[i]) for i in range(n)]
-    can, at, busy = list(first), [0.0] * n, {}
-    ready = sorted((key[i], i) for i in range(n) if not left[i])
+    can, at, busy = list(first), [0.0] * n, {q: list(held[q]) for q in held}
+    ready = sorted(((key[i], i) for i in range(n) if not left[i]), reverse=True)
     while ready:
-        i = ready.pop(0)[1]
-        t, h, line = can[i], ops[i]["hold"], busy.setdefault(ops[i]["q"], [])
-        k = len(line)
+        i = ready.pop()[1]
+        o = ops[i]
+        t, h = can[i], o["hold"]
+        line = busy.get(o["q"])
+        if line is None:
+            line = busy[o["q"]] = []
+        k = m = len(line)
         while k and line[k - 1][1] > t:
             k -= 1
-        while k < len(line) and line[k][0] < t + h - 1e-9:
-            t = max(t, line[k][1]); k += 1
+        while k < m and line[k][0] < t + h - 1e-9:
+            if line[k][1] > t:
+                t = line[k][1]
+            k += 1
         line.insert(k, (t, t + h))
         at[i] = t
+        more = False
         for j, lat in after[i]:
             if can[j] < t + lat:
                 can[j] = t + lat
             left[j] -= 1
             if not left[j]:
-                ready.append((key[j], j)); ready.sort()
+                ready.append((key[j], j)); more = True
+        if more:
+            ready.sort(reverse=True)
     return at
+
+
+def replay(ops, succ, at, c):
+    can, free = [0.0] * len(ops), {}
+    for i in sorted(range(len(ops)), key=lambda i: (at[i], i)):
+        o = ops[i]
+        can[i] = max(can[i], free.get(o["q"], 0.0))
+        free[o["q"]] = can[i] + o["hold"] + o["more"][c]
+        for j, lat in succ[i]:
+            can[j] = max(can[j], can[i] + lat + o["more"][c])
+    return can
+
+
+def anneal(ops, succ, at, t0, t1, end, x, steps, heat):
+    mine = [i for i in range(len(ops)) if t0 <= at[i] < t1]
+    place = {i: k for k, i in enumerate(mine)}
+    part, n = [ops[i] for i in mine], len(mine)
+    first, due, after, before, held, nxt = [t0] * n, [end - o["dur"] for o in part], [[] for _ in mine], [[] for _ in mine], {}, {}
+    for i, o in enumerate(ops):
+        if at[i] < t0 < at[i] + o["hold"]:
+            held[o["q"]] = [(at[i], at[i] + o["hold"])]
+        if at[i] >= t1:
+            nxt[o["q"]] = min(nxt.get(o["q"], end), at[i])
+        for j, lat in succ[i]:
+            if i in place and j in place:
+                after[place[i]].append((place[j], lat)); before[place[j]].append(place[i])
+            elif i in place:
+                due[place[i]] = min(due[place[i]], at[j] - lat)
+            elif j in place:
+                first[place[j]] = max(first[place[j]], at[i] + lat)
+    for k, o in enumerate(part):
+        due[k] = min(due[k], nxt.get(o["q"], end) - o["hold"])
+
+    other = []
+    for c in range(len(SPEEDS)):
+        so = replay(ops, succ, at, c)
+        stop = max(so[i] + o["dur"] + o["more"][c] for i, o in enumerate(ops))
+        f2, d2, free, nx2 = [0.0] * n, [stop - o["dur"] - o["more"][c] for o in part], {}, {}
+        for i, o in enumerate(ops):
+            if at[i] < t0:
+                free[o["q"]] = max(free.get(o["q"], 0.0), so[i] + o["hold"] + o["more"][c])
+            elif at[i] >= t1:
+                nx2[o["q"]] = min(nx2.get(o["q"], stop), so[i])
+            for j, lat in succ[i]:
+                if i in place and j not in place:
+                    d2[place[i]] = min(d2[place[i]], so[j] - lat - o["more"][c])
+                elif j in place and i not in place:
+                    f2[place[j]] = max(f2[place[j]], so[i] + lat + o["more"][c])
+        for k, o in enumerate(part):
+            d2[k] = min(d2[k], nx2.get(o["q"], stop) - o["hold"] - o["more"][c])
+        other.append((f2, d2, free, [(o["q"], o["hold"] + o["more"][c], [(j, lat + o["more"][c]) for j, lat in after[k]]) for k, o in enumerate(part)]))
+
+    def late(key):
+        z = lay(part, before, after, first, key, held)
+        e = max(z[k] - due[k] for k in range(n)) + 1e-3 * sum(z) / n
+        seq = sorted(range(n), key=lambda k: (z[k], k))
+        for c, (f2, d2, free, step) in enumerate(other):
+            can, free, worst = list(f2), dict(free), -1e9
+            for k in seq:
+                q, h, nb = step[k]
+                t = can[k]
+                if free.get(q, 0.0) > t:
+                    t = free[q]
+                free[q] = t + h
+                if t - d2[k] > worst:
+                    worst = t - d2[k]
+                for j, lat in nb:
+                    if can[j] < t + lat:
+                        can[j] = t + lat
+            e += worst / SPEEDS[c][0]
+        return e / (1 + len(other)), z
+    now, z = late([at[i] for i in mine])
+    best, kept = now, z
+    for r in range(steps):
+        key = list(z)
+        for _ in range(1 + r % 3):
+            x = (x * 1103515245 + 12345) % 2 ** 31
+            key[(x >> 8) % n] += (-3, -2, -1, -0.6, -0.3, 0.3, 0.6, 1, 2, 3)[(x >> 20) % 10]
+        e, y = late(key)
+        x = (x * 1103515245 + 12345) % 2 ** 31
+        if e <= now - (heat * (1 - r / steps) + 0.003) * math.log(((x >> 8) % 4096 + 1) / 4096):
+            now, z = e, y
+        if now < best:
+            best, kept = now, z
+    out = list(at)
+    for k, i in enumerate(mine):
+        out[i] = kept[k]
+    return out, x
 
 
 def best_order(ops):
     n = len(ops)
     succ, pred, like = [[] for _ in ops], [[] for _ in ops], {}
     for i, o in enumerate(ops):
-        o["hold"] = {"dma": max(0.1, o["dur"] - 2.0), "send": 1.0, "arrive": 0.0}.get(o["kind"], o["dur"])
+        o["hold"] = {"dma": max(0.5, o["dur"] - 2.0), "gdma": 1.0, "send": 1.0, "arrive": 0.0}.get(o["kind"], o["dur"])
+        o["more"] = [(f * (FIX + (o["dur"] - FIX) * (ga / GA if o["ind"] else 1.0)) - o["dur"]) * (o["kind"] == "c") for f, ga in SPEEDS]
         like.setdefault(o["tag"], []).append(i)
     for j, o in enumerate(ops):
         edges = [(i, ops[i]["dur"] + (0.0 if o["q"] == "p" and ops[i]["q"] == "p" else LAT)) for i in o["d"]]
@@ -587,6 +736,10 @@ def best_order(ops):
             edges.append((o["x"][2], 0.0))
         if "behind" in o:
             edges.append((o["behind"], ops[o["behind"]]["hold"]))
+        if o["kind"] == "gdma":
+            edges.append((min(i for i, p in enumerate(ops) if p["kind"] == "send"), 3.0))
+        if o["kind"] == "send":
+            edges += [(i, p["hold"]) for i, p in enumerate(ops) if p["q"] == "g" and p["kind"] == "c"]
         for i, lat in edges:
             succ[i].append((j, lat)); pred[j].append((i, lat + o["hold"] - ops[i]["hold"]))
     zero, rest = [0.0] * n, [o["dur"] - o["hold"] for o in ops]
@@ -595,22 +748,43 @@ def best_order(ops):
         back = lay(ops, succ, pred, rest, [-at[i] - ops[i]["hold"] for i in range(n)])
         at = lay(ops, pred, succ, zero, [-back[i] - ops[i]["hold"] for i in range(n)])
         return max(at[i] + ops[i]["dur"] for i in range(n)) + 1e-5 * sum(at), at
+
+    lead = [i for i, o in enumerate(ops) if o["kind"] == "send"][1::len(PLAN["GS"])]
+
+    def whole(at):
+        return max(at[i] + ops[i]["dur"] for i in range(n)) + sum(
+            max(t + o["dur"] + o["more"][c] for t, o in zip(replay(ops, succ, at, c), ops)) / SPEEDS[c][0] for c in range(len(SPEEDS)))
     if not ORDER:
         best, at = turn(lay(ops, pred, succ, zero, list(range(n))))
-        x, now, kept = PLAN["SEED"], best, at
+        x = PLAN["SEED"]
         for r in range(PLAN["TRY"]):
             z, seq = list(at), sorted(range(n), key=lambda i: at[i])
-            mid = (x >> 6) % n
+            mid = (x >> 6) % n if r % 4 else n - 1 - (x >> 6) % (n // 7)
             for _ in range(PLAN["SHAKE"]):
                 x = (x * 1103515245 + 12345) % 2 ** 31
                 for j in like[ops[seq[min(n - 1, max(0, mid + (x >> 8) % (2 * PLAN["NEAR"]) - PLAN["NEAR"]))]]["tag"]]:
                     z[j] += (-2, -1, -0.5, -0.25, 0.25, 0.5, 1, 2)[(x >> 4) % 8]
             e, z = turn(z if PLAN["FAST"] else lay(ops, pred, succ, zero, z))
-            if e <= now + PLAN["HEAT"] * (1 - r / PLAN["TRY"]) * ((x >> 12) % 64) / 64:
-                now, at = e, z
-            if e < best:
-                best, kept = e, z
-        ORDER.append(kept)
+            if e <= best:
+                best, at = e, z
+        for r in range(PLAN["ROUNDS"]):
+            ends = sorted(at[i] + o["dur"] for i, o in enumerate(ops) if o["kind"] == "arrive")[len(PLAN["GS"])::len(PLAN["GS"])]
+            cuts = [(0.0, ends[0] / 2), (ends[0] / 4, 3 * ends[0] / 4), (ends[0] / 2, ends[0])] + list(zip(ends, ends[1:] + [best + 1]))
+            for w in range(len(cuts) - 1, -1, -1):
+                z, x = anneal(ops, succ, at, cuts[w][0], cuts[w][1], best, x, PLAN["STEPS"][r], PLAN["HEAT"][r])
+                z = lay(ops, pred, succ, zero, z)
+                if whole(z) <= whole(at):
+                    best, at = max(z[i] + ops[i]["dur"] for i in range(n)), z
+                for v in range(2, len(cuts) - 1):
+                    if 2 < w < len(cuts) - 1 and v != w:
+                        z = list(at)
+                        for same in like.values():
+                            if len(same) == RO - 1:
+                                z[same[v - 2]] = at[same[w - 2]] - at[lead[w - 2]] + at[lead[v - 2]]
+                        z = lay(ops, pred, succ, zero, z)
+                        if whole(z) <= whole(at):
+                            best, at = max(z[i] + ops[i]["dur"] for i in range(n)), z
+        ORDER.append(at)
     at = ORDER[0]
     return sorted(range(n), key=lambda i: (at[i], i)), [at[i] + ops[i]["dur"] for i in range(n)]
 
@@ -651,7 +825,7 @@ def emit(g, T, ops, seq):
             if i in needed:
                 count[o["q"]] = count.get(o["q"], 0) + 1
                 token[i] = ("q" + o["q"], count[o["q"]])
-        elif o["kind"] == "dma":
+        elif o["kind"] in ("dma", "gdma"):
             token[i] = ("d%d" % nd, 16); nd += 1
         else:
             token[i] = o["x"][:2]
@@ -662,7 +836,7 @@ def emit(g, T, ops, seq):
         for j in waits[i]:
             queue[o["q"]].wait_ge(T.sem[token[j][0]], token[j][1])
         ins = o["fn"]()
-        if o["kind"] == "dma":
+        if o["kind"] in ("dma", "gdma"):
             ins.then_inc(T.sem[token[i][0]], 16)
         elif o["kind"] == "c" and i in needed:
             ins.then_inc(T.sem[token[i][0]], 1)

import math
from concourse.bass import DstId, RemoteDMATransfer
from concourse.mybir import AluOpType as ALU, ActivationFunctionType as ACT

N, V, G, RO = 4, 3584, 384, 5
H = (N - 1) * G
LC, SC, GC = V // 16, H // 16, G // 16
OWN, GH = H, H + V
NCH, CW = 4, 56
W = 16 * CW
TW = 16 + 3 * W
K8 = 8192.0


def _sb(cols, dtype):
    return ("sbuf", [128, cols], dtype)


DIAG = {"idm": -1.0, "idq": K8, "idk": -K8 / 2, "idc": -33.0 / 64, "idd": -33.0 / 128,
        "idh": 0.5, "idg": -0.5, "id8": 8.0, "id9": -8.0625, "idz": 2.0 ** 29, "idp": 1.25, "id5": -1.25, "ids": -32.0}
EARLY = ("idm", "id8", "id9", "idz")
SCRATCH = {"xb0": _sb(V + 2 * H, "bfloat16"), "xb1": _sb(V + 2 * H, "bfloat16"), "nbt": _sb(V, "int32"),
           "tw": _sb(NCH * TW, "bfloat16"), "mb": _sb(H, "bfloat16"), "inc": _sb(H, "bfloat16"), "ycs": _sb(1024, "float32"),
           "pi": _sb(8, "int32"), "col": _sb(32, "float32"), "colb": _sb(16, "bfloat16"), "one": _sb(512, "bfloat16"),
           "bt": _sb(8, "bfloat16"), "cu": _sb(516, "bfloat16"), "wi": _sb(16, "int32"), "wa": _sb(48, "float32"),
           "wtab": _sb(16, "bfloat16"), "ee": _sb(2 * LC, "float32"), "li": _sb(4 * LC, "int32"), "mg": _sb(8 * 128, "bfloat16"),
           "run": _sb(G, "bfloat16"),
           "qlo": _sb(5 * LC, "int32"), "qhi": _sb(5 * LC, "int32"), "qq": _sb(15 * LC, "float32"),
           "gg": _sb(5 * LC, "bfloat16"), "sndi": _sb(SC, "int32"), "sndu": _sb(SC, "uint16"), "soff": _sb(SC, "uint16"),
           "less": _sb(W, "bfloat16"), "lv": _sb(2 * LC, "bfloat16"), "idn": _sb(128, "bfloat16"), "nil": _sb(128, "bfloat16"), "idf": _sb(128, "float32"),
           "ps": ("psum", [128, 4096], "float32")}
SCRATCH.update({n: _sb(V, "bfloat16") for n in ("zc", "zl", "wsb", "lr", "pb", "ph", "pl", "dd", "aa", "tt", "sg", "x2")})
SCRATCH.update({n: _sb(144, "bfloat16") for n in ("b0", "bv", "be", "bo", "bz", "bi", "bm")})
SCRATCH.update({n: _sb(128, "bfloat16") for n in DIAG})
SCRATCH.update({n: _sb(LC, "float32") for n in ("t3", "pf")})
SCRATCH.update({n: _sb(LC, "uint16") for n in ("cu16", "off", "sel")})
SCRATCH.update({n: _sb(LC, "bfloat16") for n in ("bias", "curb", "nr", "pn", "posh", "c0b", "l63", "arm", "cb4", "par")})
SCRATCH.update({n: _sb(SC, "float32") for n in ("sndp", "s2")})
SCRATCH.update({n: _sb(SC, "bfloat16") for n in ("ka", "kb", "mph", "mpl")})
SEMAPHORES = (["qv", "qs", "qp", "qg"] + ["d%d" % k for k in range(72)]
              + ["arr%d" % k for k in range(2 * RO)] + ["loc%d" % k for k in range(2 * RO)])

PLAN = {"D": "svsv", "C": "ssss", "T": ["svvh"] * 4 + ["vvvh"], "W": ["vvsv"] * 5, "X": ["svss"] * 4 + ["hsss"], "X2": ["ssss"] * 4,
        "PK": ["-2-2"] * 5, "WH": [["", "WD", "", ""]] * 4 + [["", "WDT", "T", ""]], "SAFE": 1, "DQ": "gggyyyy", "BANK": "012021", "ARM": "v", "VK": ["1111"] * 5, "QV": [],
        "DEC": 2, "SW": "2222", "YC": "svs", "R1": "dddd", "X20": "svsv", "FB": "svh", "SPLIT": 1, "GS": [24, 12], "TRY": 1000, "SHAKE": 8, "NEAR": 20, "FAST": 1, "HEAT": [0.08, 0.04, 0.03, 0.02, 0.02, 0.015],
        "ROUNDS": 6, "STEPS": [7000] * 6, "SEED": 12345}
BETWEEN = [[(-1, 1), (0, 0)], [(-1, 2), (0, 1), (1, 0), (-1, 3)], [(0, 2), (1, 1), (2, 0), (-1, 4), (0, 3)], [(1, 2), (2, 1), (3, 0)]]
CY, PCY, FIX, LAT, GA, FAR_US, NEAR_US = 0.92e-3, 0.46e-3, 0.042, 0.12, 1.58, 3.0, 2.2
SFX, MFX, GT, GFX, ADD_US = 0.015, 0.0, 1.0, 0.1, 2.3
SPEEDS = [(0.92, 1.2), (1.28, 1.95)]
ORDER = []


def build(g, core, T, topo, ops):
    rank = T.rank_of(core)
    first = [0]

    def reg(name, lo, hi):
        if name == "ps":
            return [("ps%d" % b, 0, 1) for b in range(lo // 512, (hi - 1) // 512 + 1)]
        return [(name, lo, hi)]

    def A(name, lo=0, hi=None, step=1, p0=0, p1=128):
        hi = SCRATCH[name][1][1] if hi is None else hi
        ap = T[name][p0:p1, lo:hi:step] if step > 1 else T[name][p0:p1, lo:hi]
        return (ap, reg(name, lo, hi), (hi - lo + step - 1) // step, SCRATCH[name][2], name)

    def PS(bank, lo, hi):
        return A("ps", 512 * bank + lo, 512 * bank + hi)

    def IND(win, offs):
        return (win[0].indirect(offs[0]), win[1] + offs[1], 16 * offs[2], win[3], "ind")

    def add(q, fn, reads, writes, dur, kind="c", extra=None, ind=False):
        ops.append({"q": q, "fn": fn, "r": reads, "w": writes, "dur": dur, "kind": kind, "x": extra, "ind": ind,
                    "tag": len(ops) - first[0] if first[0] else -len(ops)})
        return len(ops) - 1

    def two(*aps):
        return all(a[3] in ("bfloat16", "uint16") for a in aps)

    def sc(s):
        return (s[0], s[1]) if isinstance(s, tuple) else (s, [])

    def vcost(n, f):
        return FIX + CY * max(64, n * f)

    def ts(out, in0, s1, op0, s2=None, op1=None):
        a1, r1 = sc(s1); a2, r2 = sc(s2)
        f = GA if in0[4] == "ind" else (0.5 if two(out, in0) else 1.0)
        if op1 is None:
            fn = lambda: g.vector.tensor_scalar(out[0], in0[0], a1, None, op0)
        else:
            fn = lambda: g.vector.tensor_scalar(out[0], in0[0], a1, a2, op0, op1)
        return add("v", fn, in0[1] + r1 + r2, out[1], vcost(out[2], f), ind=in0[4] == "ind")

    def tt(out, in0, in1, op):
        f = max(GA, GT) if in0[4] == "ind" else (1.0 if "ps" in (in0[4], in1[4]) else 2.0)
        return add("v", lambda: g.vector.tensor_tensor(out[0], in0[0], in1[0], op), in0[1] + in1[1], out[1], vcost(out[2], f),
                   ind=in0[4] == "ind")

    def cp(out, in0):
        f = GA if in0[4] == "ind" else (0.5 if two(out, in0) else 1.0)
        return add("v", lambda: g.vector.tensor_copy(out[0], in0[0]), in0[1], out[1], vcost(out[2], f), ind=in0[4] == "ind")

    def ms(out, val):
        return add("v", lambda: g.vector.memset(out[0], val), [], out[1], vcost(out[2], 0.5 if two(out) else 1.0))

    def scan(out, in0):
        ones = A("run")
        return add("v", lambda: g.vector.tensor_tensor_scan(out[0], ones[0], in0[0], 0.0, ALU.mult, ALU.add),
                   in0[1] + ones[1], out[1], vcost(out[2], 0.5))

    def act(out, in0, func, bias=0.0, scale=1.0):
        ab, rb = sc(bias); as_, rs = sc(scale)
        f = GA if in0[4] == "ind" else 1.0
        return add("s", lambda: g.scalar.activation(out[0], in0[0], func, bias=ab, scale=as_), in0[1] + rb + rs, out[1],
                   vcost(out[2], f) + SFX, ind=in0[4] == "ind")

    def move(e, out, in0, plus=0.0):
        return ts(out, in0, plus, ALU.add) if e == "v" else act(out, in0, ACT.Identity, bias=plus)

    def mm(items):
        def fn():
            ins = None
            for o, l, r, st, sp in items:
                ins = g.tensor.matmul(o[0], l[0], r[0], st, sp)
            return ins
        rd, wr, dur = [], [], FIX
        for o, l, r, st, sp in items:
            rd += l[1] + r[1]; wr += o[1]; dur += MFX + PCY * max(min(64, l[2]), r[2]) * (4 if r[3] == "float32" else 1)
        return add("p", fn, sorted(set(rd)), sorted(set(wr)), dur)

    made = set()

    def acc(out, terms, start=True, stop=True):
        items = []
        for n, t in enumerate(terms):
            if not isinstance(t, int) and t[0] in DIAG and t[0] not in made:
                made.add(t[0])
                keep, first[0] = first[0], 0
                if t[0] in EARLY:
                    act(A(t[0]), A("idn"), ACT.Identity, scale=DIAG[t[0]])
                else:
                    asel(A(t[0]), A("nil"), [[-1, 128]], ALU.not_equal, 0, 1, DIAG[t[0]])
                first[0] = keep + 1 if keep else 0
            l, r = (A("mg", 128 * t, 128 * t + 128, p1=1), A("one", 0, out[2], p1=1)) if isinstance(t, int) else (A(t[0]), t[1])
            items.append((out, l, r, start and n == 0, stop and n == len(terms) - 1))
        return items

    def iota(out, pattern, base, cm):
        if out[3] == "int32":
            fn = lambda: g.iota(out[0], pattern, base, cm)
        else:
            fn = lambda: g.iota(out[0], pattern, base, cm, allow_small_or_imprecise_dtypes=True)
        return add("g", fn, [], out[1], GFX + 0.13 + 2 * CY * out[2])

    def fill(out, val):
        return iota(out, [[0, out[2]]], int(val), 0)

    def asel(out, in0, pattern, cmp_, base, cm, other=0.0):
        return add("g", lambda: g.affine_select(out[0], in0[0], pattern, cmp_, other, base, cm), in0[1], out[1], GFX + 0.17 + 2 * CY * out[2])

    def dma(q, out, in_, reads, writes, nbytes):
        if q == "g":
            return add(q, lambda: g.dma_start(out, in_), reads, writes, 2.5 + nbytes / 200e3, "gdma")
        eng = g.sync if q == "y" else g.scalar
        return add(q, lambda: eng.dma_start(out, in_), reads, writes, 2.0 + nbytes / 200e3, "dma")

    def listmm(out, band, src, lo, hi, k=128, start=True, stop=True):
        return [(out, A(band, 15 - i, 143 - i, p1=k), A(src, lo + i, hi, 16, p1=k), start and i == 0, stop and i == 15)
                for i in range(16)]

    cols = {}

    def C(name):
        return A("col", cols[name], cols[name] + 1)

    def CB(k):
        return A("colb", k, k + 1)

    def Q(name, t, n=1):
        return A(name, t * LC, (t + n) * LC)

    xb = ["xb0", "xb1"]
    shift = [2.0 if PLAN["D"][k] == "v" and PLAN["C"][k] == "v" else 0.0 for k in range(NCH)]

    def leaves(r, d):
        return topo.chip(T.cores[r]) != topo.chip(T.cores[(r + d) % N])

    def blocks(r):
        return sorted(range(N - 1), key=lambda b: not leaves(r, b + 1))
    nfar = sum(leaves(rank, d) for d in range(1, N))
    sends = [(0, nfar), (nfar, N - 1)] if PLAN["SPLIT"] else [(0, N - 1)]

    dma("s", T.zc[0:8, :], T.c0[:, :], [], reg("zc", 0, V), 20e3)
    dma("s", T.zl[0:8, :], T.x[15::16, :], [], reg("zl", 0, V), 20e3)
    cuts = {"1": (0, W), "2": (0, W // 2, W), "3": (0, W // 4, W // 2, W)}
    pieces = [[(k * W + a, k * W + b) for a, b in zip(cuts[c], cuts[c][1:])] for k, c in enumerate(PLAN["SW"])]
    loads = [dma("y", T.nbt[:, a:b], T.nb[:, a:b], [], reg("nbt", a, b), 512 * (b - a))
             for a, b in pieces[0] + pieces[1] + [(2 * W, 3 * W), (3 * W, V)]]
    loads.append(dma("y", T.xb0[:, OWN:GH], T.x[:, :], [], reg("xb0", OWN, GH), 256 * V))
    loads.append(dma("y", T.xb0[:, GH:GH + H], T.gx[:, :], [], reg("xb0", GH, GH + H), 256 * H))
    for j, b in enumerate(blocks(rank)):
        loads.append(dma("y", T.sndi[:, j * GC:(j + 1) * GC], T.snd[:, b * GC:(b + 1) * GC], [], reg("sndi", j * GC, (j + 1) * GC), 20e3))
    for a, b in zip(loads, loads[1:]):
        ops[b]["behind"] = a

    iota(A("pi", 0, 1), [[0, 1]], 0, 1)
    ts(A("pi", 1, 2), A("pi", 0, 1), 15, ALU.bitwise_and)
    ts(A("pi", 2, 3), A("pi", 0, 1), 1, ALU.bitwise_and)
    cols.update({"pm": 0, "lev": 1, "we": 2, "wo": 3, "pw": 4, "pn": 5, "kb": 6})
    cp(C("pm"), A("pi", 1, 2))
    ts(C("lev"), A("pi", 1, 2), 15.0, ALU.is_equal)
    ts(C("we"), A("pi", 2, 3), -0.25, ALU.mult, 0.25, ALU.add)
    ts(C("wo"), A("pi", 2, 3), 0.25, ALU.mult)
    act(C("pw"), C("pm"), ACT.Identity, bias=float(W))
    act(C("pn"), C("pm"), ACT.Identity, bias=-2048.0)
    act(C("kb"), C("pm"), ACT.Identity, bias=-18.0, scale=-1.0)
    BIG, LO = DIAG["id8"], 704.0
    percol = {"f1": (1.0, 0.0), "wv": (-256.0, -7 * 256.0), "wi": (14 * BIG, -BIG)}
    percol.update({"r%d%d" % (shift[k], PLAN["R1"][k] == "d"): (LO + 64 + shift[k], 64.0 + shift[k] + (PLAN["R1"][k] == "d")) for k in range(NCH)})
    assert ("e", "v") not in zip(PLAN["D"], PLAN["C"])
    looks = set(zip(PLAN["D"].replace("e", "v"), PLAN["C"]))
    if ("v", "s") in looks:
        percol["f2"] = (-2.0, 0.0)
    if ("s", "v") in looks:
        percol["c1"] = (-1.0, 0.0)
    for k, nm in enumerate(percol):
        cols[nm] = 10 + k
        act(C(nm), C("lev"), ACT.Identity, bias=percol[nm][0], scale=percol[nm][1] - percol[nm][0])
    if set(PLAN["R1"]) != {"d"}:
        act(CB(4), C("lev"), ACT.Identity)
    if set(PLAN["D"]) != {"s"}:
        act(CB(0), C("f1"), ACT.Identity, scale=2.0 ** 27)
        act(CB(1), C("f1"), ACT.Identity, bias=1.0, scale=2.0 ** 27)
    if ("v", "v") in looks:
        act(CB(2), C("lev"), ACT.Identity, bias=1.0)
        act(CB(3), C("f1"), ACT.Identity, bias=2.0)
    if "s" in PLAN["D"]:
        cols.update({"a1": 7, "a2": 8})
        act(C("a1"), C("f1"), ACT.Identity, scale=1.5 * 2 ** 27)
        act(C("a2"), C("f1"), ACT.Identity, bias=-1.25, scale=1.5 * 2 ** 27)

    ms(A("one"), 1.0)
    ms(A("nil"), 0.0)
    fill(A("bz"), 0)
    asel(A("bz", 15, 143, 16), A("one", 0, 8), [[-1, 8]], ALU.is_equal, 0, 1)
    fill(A("b0"), 0)
    asel(A("bt"), A("one", 0, 8), [[-16, 8]], ALU.is_ge, 0, 1)
    asel(A("b0", 15, 143, 16), A("bt"), [[16, 8]], ALU.is_ge, 15, -1)
    asel(A("idn"), A("one", 0, 128), [[-1, 128]], ALU.is_equal, 0, 1)
    if True:
        asel(A("idf"), A("one", 0, 128), [[-1, 128]], ALU.is_equal, 0, 1)
    for nm, c in (("be", "we"), ("bo", "wo"), ("bv", "wv"), ("bi", "wi")):
        act(A(nm), A("b0"), ACT.Identity, scale=C(c))
    act(A("run"), A("one", 0, G), ACT.Identity, scale=C("lev"))
    M64, M8K, M16, MID, MSG = 0, 2, 4, 6, 7
    for k, val in enumerate((1.5 * 2 ** 29, -1.5 * 2 ** 29, 1.5 * 2 ** 36, -1.5 * 2 ** 36, 1.5 * 2 ** 27, -1.5 * 2 ** 27, 31.5, 12288.0)):
        if k == MID and not any(t != "v" and x != "s" or t != "s" and w == "r" for p in zip(PLAN["T"], PLAN["W"], PLAN["X"]) for t, w, x in zip(*p)):
            continue
        if k // 2 * 2 == M16:
            ms(A("mg", 128 * k, 128 * k + 128, p1=32), val)
        else:
            asel(A("mg", 128 * k, 128 * k + 128, p1=32), A("nil", p1=32), [[0, 128]], ALU.is_gt, 0, 0, val)
    iota(A("wi"), [[-1, 16]], 128, 1)
    ts(A("wi"), A("wi"), 15, ALU.bitwise_and)
    ts(A("wa", 0, 16), A("wi"), 1.5, ALU.is_le, -255.0, ALU.mult)
    ts(A("wa", 16, 32), A("wi"), 3.5, ALU.is_le, 256.0, ALU.mult)
    ts(A("wa", 32, 48), A("wi"), 4.0, ALU.is_equal, 65536.0, ALU.mult)
    tt(A("wa", 0, 16), A("wa", 0, 16), A("wa", 16, 32), ALU.add)
    tt(A("wtab"), A("wa", 0, 16), A("wa", 32, 48), ALU.add)
    iota(A("posh"), [[0, NCH], [16, CW]], 16, 0)
    for k in range(NCH):
        fill(A("tw", k * TW, k * TW + 16), shift[k])
    for s in sorted(set(shift[k] for k in range(NCH) if PLAN["R1"][k] == "d")):
        fill(A("lv", int(s) // 2 * LC, int(s) // 2 * LC + LC), 64 + s)
    iota(A("mph"), [[16, SC]], 0, 0)
    act(A("mpl"), A("one", 0, SC), ACT.Identity, scale=C("pm"))
    fill(A("cu", 0, 4), 0)
    asel(A("cu", 4, 516), A("one"), [[-1, 16], [-16, 8], [-128, 4]], ALU.is_equal, 0, 1)
    marks = []
    for d in range(N - 1):
        cut = {"v": GC, "s": 0, "h": GC // 2}[PLAN["FB"][d]]
        marks.append([m for m in (("v", d * GC, d * GC + cut), ("s", d * GC + cut, (d + 1) * GC)) if m[2] > m[1]])
        for e, la, lb in marks[d]:
            if e == "v":
                fill(A("ka", la, lb), 284); fill(A("kb", la, lb), 1)
            else:
                iota(A("ka", la, lb), [[-16, lb - la]], 512, 0)
                act(A("kb", la, lb), A("one", 0, lb - la), ACT.Identity, scale=C("kb"))

    ZC, ZL = PS(7, 0, LC), PS(7, LC, 2 * LC)
    for la, lb in ((0, CW), (CW, LC)):
        mm(listmm(PS(7, la, lb), "bz", "zc", 16 * la, 16 * lb, k=8))
        cp(A("cu16", la, lb), PS(7, la, lb))
    act(A("c0b"), ZC, ACT.Identity)
    mm(acc(PS(6, 0, LC), [("id9", A("c0b")), M16, M16 + 1, ("id8", A("c0b"))]))
    act(A("par"), PS(6, 0, LC), ACT.Identity, bias=-1.0, scale=-0.25)
    mm(listmm(ZL, "bz", "zl", 0, V, k=8))
    act(A("nr"), ZL, ACT.Sign)
    act(A("l63"), ZL, ACT.Relu, bias=-992.0, scale=16.0)
    act(A("bias"), A("nr"), ACT.Identity, bias=11 * 256.0, scale=20.5 * 256)
    act(A("pn"), A("nr"), ACT.Identity, bias=C("pn"), scale=2048.0)

    def failpos(n, Z, P):
        mm(acc(Z, [("idn", A("l63")), ("idm", A("c0b"))] + [("idg", Q("gg", j)) for j in range(n)]))
        if PLAN["ARM"] == "v":
            ts(A("arm"), Z, n / 2 - 15.0, ALU.is_equal, float(W), ALU.mult)
        else:
            act(A("arm"), Z, ACT.Abs, bias=15.0 - n / 2)
            act(A("arm"), A("arm"), ACT.Relu, bias=float(W), scale=-float(W))
        mm(acc(P, [("idn", A("posh")), ("idn", A("arm"))]))
        act(A("pf"), P, ACT.Identity, bias=C("pw"))
    failpos(0, ZC, ZL)
    cp(A("sndu"), A("sndi"))
    ts(A("sndp"), A("sndi"), float(OWN), ALU.add)

    peers = [c for c in T.cores if c != core]
    far = sorted(set(e for c in peers if topo.chip(c) != topo.chip(core) for e in topo.engines(core, c)))

    def send(n, trips, src, dst):
        off = [p for p, _, _ in trips if topo.chip(T.cores[p]) != topo.chip(core)]
        tr, kf, kn, tot, rd, wr = [], 0, 0, 0, [], []
        for p, so, do in trips:
            dc = T.cores[p]
            assert topo.may_write(core, dc)
            if p in off:
                w = len(far) // len(off)
                es = far[kf * w:(kf + 1) * w]; kf += 1
            else:
                free = [e for e in topo.engines(core, dc) if e not in far]
                w = len(free) // (len(trips) - len(off))
                es = free[kn * w:(kn + 1) * w]; kn += 1
            rid, pid, _ = topo.addr(dc)
            tr.append(RemoteDMATransfer(dst_ids=[DstId(rid=rid, pnc=pid)], dma_engine_mask=sum(1 << e for e in es),
                                        remote_sem=T.sem["arr%d" % n], src=T[src][:, so:so + G], dst=T[dst][:, do:do + G]))
            tot += len(es); rd += reg(src, so, so + G); wr += reg(dst, do, do + G)
        us = FAR_US if off else NEAR_US
        s = add("g", lambda: g.remote_dma_fused(tr, local_sem=T.sem["loc%d" % n]), rd + [("added", 0, NCH)], [], us - 1.0, "send", ("loc%d" % n, tot))
        add("x", None, [], wr, us, "arrive", ("arr%d" % n, tot, s))

    send(2 * RO - 1, [((rank - b - 1) % N, GH + b * G, blocks((rank - b - 1) % N).index(b) * G) for b in range(N - 1)], "xb0", "xb1")

    def shifted(e, k, src):
        a, b = k * W, (k + 1) * W
        if PLAN["D"][k] == "v" and e != "d":
            move(e, A("x2", a, b), A(src, OWN + a, OWN + b), -2.0)
        elif PLAN["D"][k] == "v":
            dma("y", T.x2[:, a:b], T.less[:, :], reg("less", 0, W), reg("x2", a, b), 256 * W)
            add("g", lambda: g.dma_start(T.x2[:, a:b], T[src][:, OWN + a:OWN + b], accum_op=ALU.add), reg(src, OWN + a, OWN + b),
                reg("x2", a, b) + ([("added", k, k + 1)] if PLAN["SAFE"] else []), 2.0 + ADD_US, "gdma")
    if "d" in PLAN["X20"] + "".join(PLAN["X2"]):
        fill(A("less"), -2)
    for k in range(NCH):
        shifted(PLAN["X20"][k], k, "xb0")

    n = W // 2
    for k in range(NCH):
        byd = PLAN["R1"][k] == "d"
        r0 = k * TW + 16 + W
        halves = [(k * W, k * W + n), (k * W + n, (k + 1) * W)]
        for a, b in pieces[k]:
            HP, WP = A("ps", 512 - n + a - k * W, 512 - n + b - k * W), A("ps", 1536 - n + a - k * W, 1536 - n + b - k * W)
            act(A("wsb", a, b), IND(A("wtab"), A("cu16", a // 16, b // 16)), ACT.Identity)
            ts(HP, A("nbt", a, b), 1.5 * 2 ** 31, ALU.add, 1.5 * 2 ** 31, ALU.subtract)
            tt(A("lr", a, b), A("nbt", a, b), HP, ALU.subtract)
            tt(A("ph", a, b), HP, A("wsb", a, b), ALU.mult)
            act(A("pb", a, b), A("lr", a, b), ACT.Identity, bias=LO - 1.5)
            for lo in range(a, b, n):
                hi = min(b, lo + n)
                mm(acc(A("ps", 1536 - n + lo - k * W, 1536 - n + hi - k * W), [("idn", A("wsb", lo, hi))]))
            tt(A("pl", a, b), WP, A("pb", a, b), ALU.mult)
        for a, b in halves:
            RP, r1 = PS(7, 0, n), r0 + byd * W + a - k * W
            mm(acc(RP, [("idn", A("lr", a, b)), ("idm", A("pb", a, b))]))
            act(A("tw", r1, r1 + n), RP, ACT.Identity, bias=C("r%d%d" % (shift[k], byd)), scale=C("f1"))
        if byd:
            lv = int(shift[k]) // 2 * LC
            dma("y", T.tw[:, r0:r0 + W], T.tw[:, r0 + W:r0 + 2 * W], reg("tw", r0 + W, r0 + 2 * W), reg("tw", r0, r0 + W), 256 * W)
            ops[-1]["behind"] = loads[-1]
            dma(PLAN["DQ"][0], T.tw[15::16, r0:r0 + W], T.lv[0:32, lv:lv + LC], reg("lv", lv, lv + LC), reg("tw", r0, r0 + W), 16 * W)
        else:
            move(PLAN["R1"][k], A("tw", r0 + W, r0 + 2 * W), A("tw", r0, r0 + W), CB(4))
        per = NCH // PLAN["DEC"]
        m, la = per * CW, k // per * per * CW

        def sums(j, lo, hi):
            return PS(4 + k // per % 2, j * m + lo, j * m + hi) if 4 * m <= 512 else PS(4 + j % 2, j // 2 * m + lo, j // 2 * m + hi)
        for j, (band, src) in enumerate((("be", "ph"), ("bo", "ph"), ("be", "pl"), ("bo", "pl"))):
            out = sums(j, k % per * CW, (k % per + 1) * CW)
            mm(listmm(out, band, src, k * W, (k + 1) * W, stop=j != 1)
               + (acc(out, [("idz", A("par", k * CW, (k + 1) * CW))], start=False) if j == 1 else []))
        if k % per < per - 1:
            continue
        for j in range(2):
            ee = A("ee", j * LC + la, j * LC + la + m)
            act(ee, sums(2 * j, 0, m), ACT.Identity)
            for t in range(2):
                tt(A("li", (2 * j + t) * LC + la, (2 * j + t) * LC + la + m), sums(2 * j + 1, 0, m), ee, ALU.min if t else ALU.max)
        for dst, j, mask in (("qhi", 0, 127 * 64), ("qlo", 1, 255)):
            ts(A(dst, la, la + m), A("li", 2 * j * LC + la, 2 * j * LC + la + m), mask, ALU.bitwise_and)
        tt(A("qq", la, la + m), A("qlo", la, la + m), A("qhi", la, la + m), ALU.add)
        ts(A("off", la, la + m), A("qq", la, la + m), LO / 4, ALU.subtract)

    def kept(r, t):
        return Q("qq", r * RO - r * (r - 1) // 2 + t)

    def place(t):
        for dst, j, mask in (("qhi", 0, 127 * 64), ("qlo", 1, 255)):
            if t > 1:
                ts(Q(dst, t), Q("li", 2 * j + t % 2), 8 * (t // 2), ALU.arith_shift_right, mask, ALU.bitwise_and)
            else:
                ts(Q(dst, t), Q("li", 2 * j + t), mask, ALU.bitwise_and)
        tt(kept(0, t), Q("qlo", t), Q("qhi", t), ALU.add)

    UB = 7 * 512 - 2 * CW
    slot = [0]

    def pair():
        slot[0] += 1
        return 1024 * int(PLAN["BANK"][slot[0] - 1]) + 512 - n

    def look(s, k, cur):
        ca, cb = k * CW, (k + 1) * CW
        a, b = 16 * ca, 16 * cb
        CC = A("tw", k * TW + 16, k * TW + 16 + W)
        pd = pair() if PLAN["D"][k] != "v" else 0
        for lo, hi in ([(a, b)] if "D" in PLAN["WH"][s][k] else [(a, a + n), (a + n, b)]):
            src = IND(A(cur, OWN, GH + H), A("off", lo // 16, hi // 16))
            if PLAN["D"][k] != "v":
                act(A("dd", lo, hi), src, ACT.Identity)
            else:
                tt(A("dd", lo, hi), src, A("x2", lo, hi), ALU.subtract)
        if PLAN["D"][k] != "v":
            less, plus = ("id5", "idp") if PLAN["D"][k] == "s" else ("idm", "idn")
            for lo, hi in ((a, a + n), (a + n, b)):
                mm(acc(A("ps", pd + lo - a, pd + hi - a), [(less, A(cur, OWN + lo, OWN + hi))], stop=False))
                mm(acc(A("ps", pd + lo - a, pd + hi - a), [(plus, A("dd", lo, hi))], start=False))
        if PLAN["D"][k] == "e":
            for lo, hi in ([(a, b)] if "E" in PLAN["WH"][s][k] else [(a, a + n), (a + n, b)]):
                act(A("dd", lo, hi), A("ps", pd + lo - a, pd + hi - a), ACT.Identity, bias=2.0)
        if PLAN["D"][k] == "s":
            D = A("ps", pd, pd + W)
            ts(A("aa", a, b), D, C("a1"), ALU.add, C("a2"), ALU.is_equal)
            ts(CC, D, C("c1"), ALU.max, C("f1"), ALU.min) if PLAN["C"][k] == "v" else act(CC, D, ACT.Sign, scale=C("f1"))
        else:
            D = A("dd", a, b)
            ts(A("aa", a, b), D, CB(0), ALU.add, CB(1), ALU.is_equal)
            ts(CC, D, CB(2), ALU.max, CB(3), ALU.min) if PLAN["C"][k] == "v" else act(CC, D, ACT.Sign, bias=C("f2"), scale=C("f1"))

    def votes(ca, cb):
        U = A("ps", UB + ca, UB + cb)
        mm(acc(U, [("idn", A("bias", ca, cb))], stop=False) + listmm(U, "bv", "aa", 16 * ca, 16 * cb, start=False, stop=False)
           + acc(U, [M8K, M8K + 1, ("idn", A("posh", ca, cb)), ("idn", A("pn", ca, cb))], start=False))

    def change(s, k, cur, new):
        a = k * W
        eT, eW, eX = PLAN["T"][s][k], PLAN["W"][s][k], PLAN["X"][s][k]
        pb_ = pair()
        halves = [(a, a + n), (a + n, a + W)]

        def parts(stage, e):
            if stage in PLAN["WH"][s][k] and "h" not in (e, eT):
                return [(a, a + W, e == "v")]
            return [(lo, hi, e == "v" or (e == "h" and lo == a)) for lo, hi in halves]
        fused = [eT == "v" or (eT == "h" and lo == a) for lo, _ in halves]
        for lo, hi, byv in parts("T", eT):
            src = IND(A("tw", k * TW, (k + 1) * TW), A("sel", lo // 16, hi // 16))
            if byv:
                tt(A("tt", lo, hi), src, A("x2", lo, hi) if shift[k] else A(cur, OWN + lo, OWN + hi), ALU.add)
            else:
                act(A("tt", lo, hi), src, ACT.Identity, bias=32.5 - shift[k])
        for lo, hi, byv in parts("W", eW):
            if eW != "r" and fused[lo > a]:
                move(eW, A("sg", lo, hi), A("tt", lo, hi), 12288 - 31.5)
        for hf, (lo, hi) in enumerate(halves):
            P = A("ps", pb_ + lo - a, pb_ + hi - a)
            own, t_, xv = A(cur, OWN + lo, OWN + hi), A("tt", lo, hi), eX == "v" or (eX == "h" and hf == 0)
            if not fused[hf]:
                mm(acc(P, [("idm", own)], stop=False))
                mm(acc(P, [("idm", t_), M64, M64 + 1, ("idn", t_), MID if xv else ("idn", own)], start=False))
            elif eW == "r":
                mm(acc(P, [MID], stop=False))
                mm(acc(P, [("idm", t_), M64, M64 + 1] + ([] if xv else [("idn", t_)]), start=False))
            else:
                if xv:
                    mm(acc(P, [MSG], stop=False))
                mm(acc(P, [("idm", A("sg", lo, hi))] + ([] if xv else [("idn", t_)]), start=not xv))
        for lo, hi, byv in parts("X", eX):
            P, out = A("ps", pb_ + lo - a, pb_ + hi - a), A(new, OWN + lo, OWN + hi)
            if byv:
                tt(out, P, A("tt", lo, hi) if fused[lo > a] else A(cur, OWN + lo, OWN + hi), ALU.add)
            else:
                act(out, P, ACT.Identity, bias=31.5 if not fused[lo > a] else 0.0 if eW == "r" else 12288.0)
            if s == RO - 1:
                dma(PLAN["DQ"][3 + k], T.yx[:, lo:hi], T[new][:, OWN + lo:OWN + hi], out[1], [], 256 * (hi - lo))

    def cursors(s, h):
        la, lb = h * LC // 2, (h + 1) * LC // 2
        gl, cl, Z = A("gg", s * LC + la, s * LC + lb), A("cb4", la, lb), PS(6 + h, 128, 128 + LC // 2)
        act(gl, A("ps", UB + la, UB + lb), ACT.Sign, bias=-K8 / 2)
        mm(acc(Z, [("idc", cl), ("idd", gl), M16, M16 + 1, ("idn", cl), ("idh", gl)]))
        move(PLAN["YC"][2], A("curb", la, lb), Z)
        for i0 in range(0, 16, 4):
            mm([(A("ps", (6 + h) * 512 + i, (6 + h) * 512 + n, 16, 0, 32), A("cu", 4 + 32 * i - j, 36 + 32 * i - j),
                 A("curb", la + j * CW // 2, la + (j + 1) * CW // 2), j == 0, j == 3) for i in range(i0, i0 + 4) for j in range(4)])
        move(PLAN["YC"][h], A("ycs", h * n, (h + 1) * n, p1=32), A("ps", (6 + h) * 512, (6 + h) * 512 + n, p1=32))
        dma(PLAN["DQ"][1 + h], T.yc[:, 16 * la:16 * lb], T.ycs[0:32, h * n:(h + 1) * n], reg("ycs", h * n, (h + 1) * n), [], 60e3)

    for s in range(RO):
        cur, new = xb[s % 2], xb[(s + 1) % 2]
        last = s == RO - 1
        first[0] = 0 if last else len(ops)
        todo, slot[0] = [], 0
        for k in range(NCH):
            look(s, k, cur)
            if PLAN["VK"][s][k] != "-":
                votes((k + 1 - int(PLAN["VK"][s][k])) * CW, (k + 1) * CW)
            while todo:
                change(s, todo.pop(0), cur, new)
            if PLAN["PK"][s][k] != "-":
                k0 = k + 1 - int(PLAN["PK"][s][k])
                ca, cb = k0 * CW, (k + 1) * CW
                tt(A("t3", ca, cb), A("ps", UB + ca, UB + cb), A("pf", ca, cb), ALU.min)
                cp(A("sel", ca, cb), A("t3", ca, cb))
                todo = list(range(k0, k + 1))
            if last and k % 2:
                cursors(s, k // 2)
        if not last:
            act(Q("gg", s), A("ps", UB, UB + LC), ACT.Sign, bias=-K8 / 2)
        for k in todo:
            change(s, k, cur, new)
        if last:
            break
        for k in range(NCH):
            shifted(PLAN["X2"][s][k], k, new)
        for j, (d0, d1) in enumerate(sends):
            la, lb = d0 * GC, d1 * GC
            for d in range(d0, d1):
                for e, ma, mb in marks[d]:
                    src = IND(A("tt"), A("sndu", ma, mb))
                    if e == "v":
                        ts(A("mb", 16 * ma, 16 * mb), src, 63.5, ALU.is_ge, 2.0, ALU.mult)
                    else:
                        act(A("mb", 16 * ma, 16 * mb), src, ACT.Sign, bias=-63.5)
            U2 = PS(6 + j, 128 * j + la, 128 * j + lb)
            mm(acc(U2, [("id8", A("ka", la, lb)), ("id8", A("kb", la, lb))], stop=False))
            for d in range(d0, d1):
                scan(A("inc", d * G, (d + 1) * G), A("mb", d * G, (d + 1) * G))
            mm(listmm(U2, "bi", "inc", 16 * la, 16 * lb, start=False, stop=False)
               + acc(U2, [M8K, M8K + 1, ("idn", A("mph", la, lb)), ("idn", A("mpl", la, lb))], start=False))
            tt(A("s2", la, lb), U2, A("sndp", la, lb), ALU.min)
            cp(A("soff", la, lb), A("s2", la, lb))
            hs = la + PLAN["GS"][j]
            if hs > la:
                cp(A(cur, 16 * la, 16 * hs), IND(A(new, 0, GH), A("soff", la, hs)))
            if lb > hs:
                act(A(cur, 16 * hs, 16 * lb), IND(A(new, 0, GH), A("soff", hs, lb)), ACT.Identity)
            send(2 * s + j, [((rank + b + 1) % N, d * G, GH + b * G) for d, b in enumerate(blocks(rank)) if d0 <= d < d1], cur, new)
        first[0] = 0
        free = 2 * int(PLAN["BANK"][2])
        spare = [PS(free, 0, LC), PS(free + 1, 0, LC), PS(7, LC, 2 * LC), PS(6, 128, 128 + LC)]
        failpos(s + 1, spare[3], spare[3])
        for j, (r, t) in enumerate(BETWEEN[s]):
            P = spare[j % 3]
            if r < 0:
                place(t)
                continue
            if (r, t) in PLAN["QV"]:
                mm(acc(P, [("idq", Q("gg", r))]))
                tt(P, P, kept(r, t), ALU.add)
            else:
                mm(acc(P, [("idf", kept(r, t)), ("idq", Q("gg", r))]))
            tt(kept(r + 1, t), P, kept(r, t + 1), ALU.min)
            if t == 0:
                P = spare[(j + 1) % 3]
                mm(acc(P, [("idf", kept(r + 1, 0))] + [("idk", Q("gg", j)) for j in range(s + 1)]))
                ts(A("off"), P, K8 * (s + 1) / 2 - LO / 4, ALU.add)
        if s == RO - 2:
            mm(acc(spare[3], [("idn", A("c0b"))] + [("idh", Q("gg", j)) for j in range(s + 1)]))
            act(A("cb4"), spare[3], ACT.Identity, bias=RO / 2)


def depend(ops):
    acc = {}
    for i, o in enumerate(ops):
        deps = set()
        for regs, wr in ((o["r"], False), (o["w"], True)):
            for name, lo, hi in regs:
                for j, l2, h2, w2 in acc.get(name, []):
                    if l2 < hi and lo < h2 and (w2 or wr or (name.startswith("ps") and ops[j]["q"] != o["q"])):
                        deps.add(j)
        if o["kind"] == "arrive":
            deps = set()
        for regs, wr in ((o["r"], False), (o["w"], True)):
            for name, lo, hi in regs:
                lst = acc.setdefault(name, [])
                if wr:
                    lst[:] = [e for e in lst if not (lo <= e[1] and e[2] <= hi)]
                lst.append((i, lo, hi, wr))
        o["d"] = deps


def lay(ops, before, after, first, key, held={}):
    n = len(ops)
    left = [len(before[i]) for i in range(n)]
    can, at, busy = list(first), [0.0] * n, {q: list(held[q]) for q in held}
    ready = sorted(((key[i], i) for i in range(n) if not left[i]), reverse=True)
    while ready:
        i = ready.pop()[1]
        o = ops[i]
        t, h = can[i], o["hold"]
        line = busy.get(o["q"])
        if line is None:
            line = busy[o["q"]] = []
        k = m = len(line)
        while k and line[k - 1][1] > t:
            k -= 1
        while k < m and line[k][0] < t + h - 1e-9:
            if line[k][1] > t:
                t = line[k][1]
            k += 1
        line.insert(k, (t, t + h))
        at[i] = t
        more = False
        for j, lat in after[i]:
            if can[j] < t + lat:
                can[j] = t + lat
            left[j] -= 1
            if not left[j]:
                ready.append((key[j], j)); more = True
        if more:
            ready.sort(reverse=True)
    return at


def replay(ops, succ, at, c):
    can, free = [0.0] * len(ops), {}
    for i in sorted(range(len(ops)), key=lambda i: (at[i], i)):
        o = ops[i]
        can[i] = max(can[i], free.get(o["q"], 0.0))
        free[o["q"]] = can[i] + o["hold"] + o["more"][c]
        for j, lat in succ[i]:
            can[j] = max(can[j], can[i] + lat + o["more"][c])
    return can


def anneal(ops, succ, at, t0, t1, end, x, steps, heat):
    mine = [i for i in range(len(ops)) if t0 <= at[i] < t1]
    place = {i: k for k, i in enumerate(mine)}
    part, n = [ops[i] for i in mine], len(mine)
    first, due, after, before, held, nxt = [t0] * n, [end - o["dur"] for o in part], [[] for _ in mine], [[] for _ in mine], {}, {}
    for i, o in enumerate(ops):
        if at[i] < t0 < at[i] + o["hold"]:
            held[o["q"]] = [(at[i], at[i] + o["hold"])]
        if at[i] >= t1:
            nxt[o["q"]] = min(nxt.get(o["q"], end), at[i])
        for j, lat in succ[i]:
            if i in place and j in place:
                after[place[i]].append((place[j], lat)); before[place[j]].append(place[i])
            elif i in place:
                due[place[i]] = min(due[place[i]], at[j] - lat)
            elif j in place:
                first[place[j]] = max(first[place[j]], at[i] + lat)
    for k, o in enumerate(part):
        due[k] = min(due[k], nxt.get(o["q"], end) - o["hold"])

    other = []
    for c in range(len(SPEEDS)):
        so = replay(ops, succ, at, c)
        stop = max(so[i] + o["dur"] + o["more"][c] for i, o in enumerate(ops))
        f2, d2, free, nx2 = [0.0] * n, [stop - o["dur"] - o["more"][c] for o in part], {}, {}
        for i, o in enumerate(ops):
            if at[i] < t0:
                free[o["q"]] = max(free.get(o["q"], 0.0), so[i] + o["hold"] + o["more"][c])
            elif at[i] >= t1:
                nx2[o["q"]] = min(nx2.get(o["q"], stop), so[i])
            for j, lat in succ[i]:
                if i in place and j not in place:
                    d2[place[i]] = min(d2[place[i]], so[j] - lat - o["more"][c])
                elif j in place and i not in place:
                    f2[place[j]] = max(f2[place[j]], so[i] + lat + o["more"][c])
        for k, o in enumerate(part):
            d2[k] = min(d2[k], nx2.get(o["q"], stop) - o["hold"] - o["more"][c])
        other.append((f2, d2, free, [(o["q"], o["hold"] + o["more"][c], [(j, lat + o["more"][c]) for j, lat in after[k]]) for k, o in enumerate(part)]))

    def late(key):
        z = lay(part, before, after, first, key, held)
        e = max(z[k] - due[k] for k in range(n)) + 1e-3 * sum(z) / n
        seq = sorted(range(n), key=lambda k: (z[k], k))
        for c, (f2, d2, free, step) in enumerate(other):
            can, free, worst = list(f2), dict(free), -1e9
            for k in seq:
                q, h, nb = step[k]
                t = can[k]
                if free.get(q, 0.0) > t:
                    t = free[q]
                free[q] = t + h
                if t - d2[k] > worst:
                    worst = t - d2[k]
                for j, lat in nb:
                    if can[j] < t + lat:
                        can[j] = t + lat
            e += worst / SPEEDS[c][0]
        return e / (1 + len(other)), z
    now, z = late([at[i] for i in mine])
    best, kept = now, z
    for r in range(steps):
        key = list(z)
        for _ in range(1 + r % 3):
            x = (x * 1103515245 + 12345) % 2 ** 31
            key[(x >> 8) % n] += (-3, -2, -1, -0.6, -0.3, 0.3, 0.6, 1, 2, 3)[(x >> 20) % 10]
        e, y = late(key)
        x = (x * 1103515245 + 12345) % 2 ** 31
        if e <= now - (heat * (1 - r / steps) + 0.003) * math.log(((x >> 8) % 4096 + 1) / 4096):
            now, z = e, y
        if now < best:
            best, kept = now, z
    out = list(at)
    for k, i in enumerate(mine):
        out[i] = kept[k]
    return out, x


def best_order(ops):
    n = len(ops)
    succ, pred, like = [[] for _ in ops], [[] for _ in ops], {}
    for i, o in enumerate(ops):
        o["hold"] = {"dma": max(0.5, o["dur"] - 2.0), "gdma": 1.0, "send": 1.0, "arrive": 0.0}.get(o["kind"], o["dur"])
        o["more"] = [(f * (FIX + (o["dur"] - FIX) * (ga / GA if o["ind"] else 1.0)) - o["dur"]) * (o["kind"] == "c") for f, ga in SPEEDS]
        like.setdefault(o["tag"], []).append(i)
    for j, o in enumerate(ops):
        edges = [(i, ops[i]["dur"] + (0.0 if o["q"] == "p" and ops[i]["q"] == "p" else LAT)) for i in o["d"]]
        if o["kind"] == "arrive":
            edges.append((o["x"][2], 0.0))
        if "behind" in o:
            edges.append((o["behind"], ops[o["behind"]]["hold"]))
        if o["kind"] == "gdma":
            edges.append((min(i for i, p in enumerate(ops) if p["kind"] == "send"), 3.0))
        if o["kind"] == "send":
            edges += [(i, p["hold"]) for i, p in enumerate(ops) if p["q"] == "g" and p["kind"] == "c"]
        for i, lat in edges:
            succ[i].append((j, lat)); pred[j].append((i, lat + o["hold"] - ops[i]["hold"]))
    zero, rest = [0.0] * n, [o["dur"] - o["hold"] for o in ops]

    def turn(at):
        back = lay(ops, succ, pred, rest, [-at[i] - ops[i]["hold"] for i in range(n)])
        at = lay(ops, pred, succ, zero, [-back[i] - ops[i]["hold"] for i in range(n)])
        return max(at[i] + ops[i]["dur"] for i in range(n)) + 1e-5 * sum(at), at

    lead = [i for i, o in enumerate(ops) if o["kind"] == "send"][1::len(PLAN["GS"])]

    def whole(at):
        return max(at[i] + ops[i]["dur"] for i in range(n)) + sum(
            max(t + o["dur"] + o["more"][c] for t, o in zip(replay(ops, succ, at, c), ops)) / SPEEDS[c][0] for c in range(len(SPEEDS)))
    if not ORDER:
        best, at = turn(lay(ops, pred, succ, zero, list(range(n))))
        x = PLAN["SEED"]
        for r in range(PLAN["TRY"]):
            z, seq = list(at), sorted(range(n), key=lambda i: at[i])
            mid = (x >> 6) % n if r % 4 else n - 1 - (x >> 6) % (n // 7)
            for _ in range(PLAN["SHAKE"]):
                x = (x * 1103515245 + 12345) % 2 ** 31
                for j in like[ops[seq[min(n - 1, max(0, mid + (x >> 8) % (2 * PLAN["NEAR"]) - PLAN["NEAR"]))]]["tag"]]:
                    z[j] += (-2, -1, -0.5, -0.25, 0.25, 0.5, 1, 2)[(x >> 4) % 8]
            e, z = turn(z if PLAN["FAST"] else lay(ops, pred, succ, zero, z))
            if e <= best:
                best, at = e, z
        for r in range(PLAN["ROUNDS"]):
            ends = sorted(at[i] + o["dur"] for i, o in enumerate(ops) if o["kind"] == "arrive")[len(PLAN["GS"])::len(PLAN["GS"])]
            cuts = [(0.0, ends[0] / 2), (ends[0] / 4, 3 * ends[0] / 4), (ends[0] / 2, ends[0])] + list(zip(ends, ends[1:] + [best + 1]))
            for w in range(len(cuts) - 1, -1, -1):
                z, x = anneal(ops, succ, at, cuts[w][0], cuts[w][1], best, x, PLAN["STEPS"][r], PLAN["HEAT"][r])
                z = lay(ops, pred, succ, zero, z)
                if whole(z) <= whole(at):
                    best, at = max(z[i] + ops[i]["dur"] for i in range(n)), z
                for v in range(2, len(cuts) - 1):
                    if 2 < w < len(cuts) - 1 and v != w:
                        z = list(at)
                        for same in like.values():
                            if len(same) == RO - 1:
                                z[same[v - 2]] = at[same[w - 2]] - at[lead[w - 2]] + at[lead[v - 2]]
                        z = lay(ops, pred, succ, zero, z)
                        if whole(z) <= whole(at):
                            best, at = max(z[i] + ops[i]["dur"] for i in range(n)), z
        ORDER.append(at)
    at = ORDER[0]
    return sorted(range(n), key=lambda i: (at[i], i)), [at[i] + ops[i]["dur"] for i in range(n)]


def emit(g, T, ops, seq):
    queue = {"v": g.vector, "s": g.scalar, "p": g.tensor, "g": g, "y": g.sync}
    place, known, snap, waits, needed = {}, {}, {}, {}, set()
    for n, i in enumerate(seq):
        place[i] = n
    for i in seq:
        o = ops[i]
        q = o["q"]
        if q == "x":
            snap[i] = {("e", i): 1}
            continue
        kn = known.setdefault(q, {})
        ws = []
        for j in sorted(o["d"], key=lambda j: -place[j]):
            if q == "p" and ops[j]["q"] == "p":
                continue
            key, val = (ops[j]["q"], place[j]) if ops[j]["kind"] == "c" else (("e", j), 1)
            if kn.get(key, -1) >= val:
                continue
            ws.append(j); needed.add(j)
            for k2, v2 in snap[j].items():
                if kn.get(k2, -1) < v2:
                    kn[k2] = v2
        waits[i] = ws
        snap[i] = dict(kn)
        if o["kind"] == "c":
            snap[i][q] = place[i]
        else:
            snap[i][("e", i)] = 1
    token, count, nd = {}, {}, 0
    for i in seq:
        o = ops[i]
        if o["kind"] == "c":
            if i in needed:
                count[o["q"]] = count.get(o["q"], 0) + 1
                token[i] = ("q" + o["q"], count[o["q"]])
        elif o["kind"] in ("dma", "gdma"):
            token[i] = ("d%d" % nd, 16); nd += 1
        else:
            token[i] = o["x"][:2]
    for i in seq:
        o = ops[i]
        if o["q"] == "x":
            continue
        for j in waits[i]:
            queue[o["q"]].wait_ge(T.sem[token[j][0]], token[j][1])
        ins = o["fn"]()
        if o["kind"] in ("dma", "gdma"):
            ins.then_inc(T.sem[token[i][0]], 16)
        elif o["kind"] == "c" and i in needed:
            ins.then_inc(T.sem[token[i][0]], 1)
    for i in seq:
        if ops[i]["kind"] != "c" and i not in needed:
            (g.sync if ops[i]["kind"] == "dma" else g).wait_ge(T.sem[token[i][0]], token[i][1])


def rank_program(g, core, T, topo):
    if T.rank_of(core) is None:
        return
    ops = []
    build(g, core, T, topo, ops)
    depend(ops)
    emit(g, T, ops, best_order(ops)[0])
